import numpy as np, ml_dtypes
CORES = [23,119,17,113]
N = 4
import mx_ref
BF = ml_dtypes.bfloat16
def entries(a):
    return np.ascontiguousarray(a.T).reshape(-1)
def table(e):
    return np.ascontiguousarray(np.reshape(e, (-1, 16)).T).astype(np.int32)
def cols(t, e):
    v = np.concatenate([t.reshape(128, -1, 4), np.zeros((128, 1, 4), BF)], axis=1)
    return np.ascontiguousarray(v[:, e]).reshape(128, -1)
def cut(t, i, w=512):
    return t[:, w * i:w * i + w]
def f(rng, *shape):
    return mx_ref.flush((rng.standard_normal(shape, dtype=np.float32) * np.exp2(rng.integers(-2, 3, shape[:-1] + (1,)))).astype(BF))
def wide(rng, *shape, cols=0):
    v = rng.standard_normal(shape, dtype=np.float32) * np.exp2(rng.integers(-12, 13, shape)).astype(np.float32)
    if cols: v *= np.repeat(np.exp2(rng.integers(-cols, cols + 1, shape[:-2] + (1, shape[-1] // 4))) * (rng.random(shape[:-2] + (1, shape[-1] // 4)) > 0.0625), 4, axis=-1).astype(np.float32)
    return mx_ref.flush(v.astype(BF))
T, V, M, CAPP, R, O = 512, 192, 288, 64, 3, 2
START = np.repeat(np.arange(N), V)
def loose(rng, at, to, who, but=-1):
    to = to.copy(); n = np.zeros((N, N), int); np.add.at(n, (at, to), 1)
    for i in rng.permutation(who):
        q = rng.integers(0, N)
        if q != but and n[:, q].sum() < M and (q == at[i] or n[at[i], q] < CAPP): n[at[i], to[i]] -= 1; n[at[i], q] += 1; to[i] = q
    return to
def turn(rng, at):
    to = at.copy(); far = 1 + rng.permutation(N - 1)
    for s in range(N):
        k = rng.permutation(np.flatnonzero(at == s))
        for i in range(min(N - 1, len(k) // CAPP)): to[k[CAPP * i:CAPP * i + CAPP]] = (s + far[i]) % N
    return to
def collect(rng, at, e):
    to = at.copy(); k = rng.permutation(np.flatnonzero(at == e))[M - (N - 1) * CAPP:]
    to[k] = (e + 1 + np.arange(len(k)) % (N - 1)) % N
    for s in range(N):
        if s != e: to[rng.permutation(np.flatnonzero(at == s))[:CAPP]] = e
    return to
def spill(rng, at, to, who, ranks):
    to = to.copy(); n = np.zeros((N, N), int); others = np.setdiff1d(np.arange(N * V), who); np.add.at(n, (at[others], to[others]), 1)
    for i in rng.permutation(who):
        q = ranks[np.argmin(np.where(n[at[i], ranks] < CAPP, n[:, ranks].sum(axis=0), N * V))]
        n[at[i], q] += 1; to[i] = q
    return to
def lists(rng, a, share=0.25):
    nx = rng.integers(0, N * T, (N, 2 * T)); free = [list(rng.permutation(2 * T)) for r in range(N)]
    way = np.zeros((R - 1, N * V), int)
    for k in range(R - 2, -1, -1):
        goal = a[k + 1] if k == R - 2 else a[k + 1] * T + way[k + 1] // 2
        known = {}
        for i in rng.permutation(N * V):
            s = int(a[k][i]); L = known.setdefault((s, int(goal[i])), [])
            if not L or rng.random() >= share:
                L.append(free[s].pop()); way[k, i] = L[-1]
            else: way[k, i] = L[rng.integers(0, len(L))]
        if k < R - 2: nx[a[k], way[k]] = goal
    nx[a[R - 2], way[R - 2]] = a[R - 1] * T + rng.integers(0, T, N * V)
    st = (way[0] // 2).reshape(N, V); bt = sum((way[k] % 2) << k for k in range(R - 1)).reshape(N, V)
    return {"nx": np.stack([table(e) for e in nx]), "st": np.stack([table(e) for e in st]), "bt": np.stack([table(e) for e in bt])}
def setup_inputs(rng):
    a = [START]
    for k in range(R - 1): a.append(loose(rng, a[k], a[k], np.arange(N * V)))
    return {"x": f(rng, N, 128, 4 * T), "w": f(rng, N, 128, R * O * 512), **lists(rng, a)}
def setup_inputs_through(rng):
    h = rng.integers(1, N); a = [START, START.copy(), (START + h) % N]
    for s in range(N):
        for g, k in enumerate(np.array_split(V * s + rng.permutation(V), -(-V // CAPP))): a[1][k] = (s + g) % N
    return {**setup_inputs(rng), **lists(rng, a)}
def setup_inputs_far(rng):
    a = [START]
    for k in range(R - 1): a.append(turn(rng, a[k]))
    a[R - 1] = loose(rng, a[R - 2], a[R - 1], np.flatnonzero(a[R - 1] == a[R - 2]))
    return {**setup_inputs(rng), **lists(rng, a)}
def setup_inputs_gather(rng):
    p = rng.permutation(N); home, end, bare = p[:3]; a = [START, START.copy()]
    for j, s in enumerate(p[2:]): a[1][rng.permutation(np.flatnonzero(START == s))[:min(CAPP, max(0, M - V - j * CAPP))]] = home
    to = collect(rng, a[1], end)
    to = spill(rng, a[1], to, np.flatnonzero(((a[1] == end) & (to != end)) | (to == bare)), np.append(p[3:], home))
    a.append(loose(rng, a[1], to, np.flatnonzero((to == a[1]) & (a[1] != end)), but=bare))
    return {**setup_inputs(rng), **lists(rng, a, share=0.75)}
def setup_inputs_stay(rng):
    p = rng.integers(0, N); a = [START, collect(rng, START, p)]
    a.append(loose(rng, a[1], a[1], np.flatnonzero(a[1] != p)))
    return {**setup_inputs(rng), **lists(rng, a)}
def setup_inputs_spread(rng):
    d = setup_inputs(rng); d["x"] = wide(rng, N, 128, 4 * T, cols=8); return d
def follow(nx, st, bt):
    n = np.concatenate([entries(t) for t in nx]); bits = np.concatenate([entries(t) for t in bt])
    at = [np.concatenate([entries(st[r]) + r * T for r in range(N)])]
    for k in range(R - 1): at.append(n[2 * at[k] + (bits >> k & 1)])
    return at
def check_inputs(d):
    b = []
    for name, top in (("nx", N * T), ("st", T), ("bt", 2 ** (R - 1))):
        if d[name].min() < 0 or d[name].max() >= top: b.append(name)
    if b: return b
    at = [t // T for t in follow(d["nx"], d["st"], d["bt"])]
    for k in range(R):
        if np.bincount(at[k], minlength=N).max() > M: b.append("walkers on a rank at step " + str(k))
    for k in range(R - 1):
        n = np.zeros((N, N), int); np.add.at(n, (at[k], at[k + 1]), 1); np.fill_diagonal(n, 0)
        if n.max() > CAPP: b.append("walkers from a rank to another from step " + str(k))
    return b
def reference(x, w, nx, st, bt):
    nodes = np.concatenate([x[r] for r in range(N)], axis=1)
    at = follow(nx, st, bt)
    y = np.zeros((N, 128, O * M), np.float32); ids = np.full((N, 2, M), -1, np.float32)
    for e in range(N):
        m = np.flatnonzero(at[R - 1] // T == e)
        ids[e, 0, :len(m)] = m // V; ids[e, 1, :len(m)] = m % V
        for k in range(R):
            c = np.full(M, -1); c[:len(m)] = at[k][m]
            q = mx_ref.quantize(cols(nodes, c))
            for o in range(O): y[e][:, M * o:M * o + M] += mx_ref.matmul(mx_ref.quantize(np.ascontiguousarray(cut(w[e], k * O + o))), q)
    return {"y": y, "id": ids}

@@ -1,0 +1,464 @@
+from concourse.bass import DstId, RemoteDMATransfer
+from concourse.mybir import dt, AluOpType as A, AxisListType, ActivationFunctionType as AF
+
+N, V, M, O = 4, 192, 288, 2
+C = 64
+F, I, U, B = "float32", "int32", "uint16", "bfloat16"
+Q8, S8 = "float8_e4m3fn_x4", "uint8"
+
+
+def _sb(w, d, p=128):
+    return ("sbuf", [p, w], d)
+
+
+SCRATCH = {
+    "nxr": _sb(1024, I, 1), "tb": _sb(1024, I), "sti": _sb(12, I), "bti": _sb(12, I),
+    "xs": _sb(2048, B), "ws": _sb(3072, B),
+    "QX": _sb(512, Q8), "SX": _sb(512, S8), "QW": _sb(704, Q8), "SW": _sb(704, S8), "WQ": _sb(768, Q8), "WS": _sb(768, S8),
+    "Q1": _sb(192, Q8), "S1": _sb(192, S8), "Q3": _sb(192, Q8), "S3": _sb(192, S8), "Q4": _sb(192, Q8), "S4": _sb(192, S8),
+    "TE1": _sb(192, Q8), "TS1": _sb(192, S8), "TE0": _sb(192, Q8), "TS0": _sb(192, S8),
+    "QO": _sb(192, Q8), "SO": _sb(192, S8), "QN1": _sb(384, Q8), "SN1": _sb(384, S8), "QN2": _sb(384, Q8), "SN2": _sb(384, S8),
+    "QE2": _sb(192, Q8), "SE2": _sb(192, S8),
+    "iD": _sb(384, I), "j15": _sb(384, F), "pI": _sb(1, I), "c16": _sb(24, F),
+    "ones": _sb(1024, F), "ident": _sb(1024, F), "mask": _sb(384, F), "seg": _sb(384, F), "maskb": _sb(32, F),
+    "ci": _sb(8, I), "cf": _sb(24, F), "i16": _sb(24, F), "tri": _sb(24, F), "trx": _sb(36, F),
+    "l0": _sb(96, I), "off0": _sb(12, U), "stu": _sb(12, U), "b1x": _sb(12, F), "lbf": _sb(12, F), "lbi": _sb(12, U),
+    "val1": _sb(192, F), "bif": _sb(192, F), "n1m": _sb(192, F), "n1s": _sb(192, F), "n1f": _sb(192, F), "t1": _sb(12, I),
+    "eqa": _sb(72, F), "sa": _sb(36, F), "ba": _sb(96, F), "bta": _sb(96, F), "rr": _sb(6, F), "pa": _sb(36, F),
+    "eqb": _sb(144, F), "sbb": _sb(72, F), "bb": _sb(96, F), "btb": _sb(96, F), "pb": _sb(72, F),
+    "xa": _sb(72, F), "xb": _sb(144, F), "slot1": _sb(12, U), "slot2": _sb(24, U),
+    "w1": _sb(384, F), "w2": _sb(576, F), "f1": _sb(384, F), "f2": _sb(384, F),
+    "R1": _sb(12, I), "RA": _sb(12, I), "R2": _sb(12, I), "TV": _sb(12, I), "stl": _sb(12, U),
+    "vo": _sb(12, F), "VO": _sb(12, I), "lo": _sb(36, I), "la": _sb(48, I), "ofo": _sb(12, U), "ofa": _sb(12, U),
+    "n2m": _sb(384, F), "n2s": _sb(384, F), "tb2": _sb(1024, F), "lad": _sb(24, U), "lu": _sb(24, U),
+    "lub": _sb(24, F), "sk": _sb(12, F), "uf": _sb(384, F), "ad": _sb(384, F), "val2": _sb(384, F), "inv": _sb(24, F), "n2e": _sb(24, F), "t2": _sb(24, I),
+    "fa": _sb(36, I), "l34": _sb(24, U), "l56": _sb(48, U), "l56i": _sb(72, I),
+    "e0": _sb(96, F), "o1": _sb(12, U), "kw": _sb(576, F), "vk": _sb(576, F),
+    "ei": _sb(36, I), "l7": _sb(12, U), "ef": _sb(48, F), "oe2": _sb(12, U), "g1": _sb(1152, F), "bt3": _sb(4, F),
+    "hf": _sb(60, F), "o3": _sb(12, U), "pw": _sb(480, F), "f3": _sb(576, F), "mg": _sb(54, F), "pki": _sb(36, I), "yl": _sb(18, U),
+    "idi": _sb(54, I), "idt": _sb(64, F), "idx": _sb(64, F), "res": _sb(1184, F), "ysb": _sb(576, F),
+    "ps": ("psum", [128, 512 * 6], F),
+}
+DMAS = ["dnx", "dst", "dbt", "dx", "dw0", "dw1", "dq", "dp", "dy0", "dy1", "di0", "di1"]
+HOPS = ("ra", "qa", "sa", "rb", "qb", "sb", "qc", "sc")
+SEMAPHORES = ["v", "s", "t", "g", "loc"] + DMAS + [n + str(k) for n in HOPS for k in range(N - 1)]
+
+
+def plan(topo, src, cores):
+    dsts = [c for c in cores if c != src]
+    off = [c for c in dsts if topo.chip(c) != topo.chip(src)]
+    on = [c for c in dsts if topo.chip(c) == topo.chip(src)]
+    out, used = {}, []
+    for grp in (off, on):
+        if not grp:
+            continue
+        free = [e for e in topo.engines(src, grp[0]) if e not in used]
+        w = 1
+        while 2 * w * len(grp) <= len(free):
+            w *= 2
+        for i, c in enumerate(grp):
+            out[c] = free[w * i:w * i + w]
+        used = used + [e for c in grp for e in out[c]]
+    return out
+
+
+def rank_program(g, core, T, topo):
+    rank = T.rank_of(core)
+    if rank is None:
+        return
+    cores = list(T.cores)
+    oth = [d for d in range(N) if d != rank]
+    eng = {"v": g.vector, "s": g.scalar, "t": g.tensor, "g": g, "y": g.sync}
+    cnt = {q: 0 for q in eng}
+    seen, last, readers, dsum, loc = {}, {}, {}, {}, [0]
+
+    def wait(q, toks):
+        need = {}
+        for sem, val in toks:
+            if val > seen.get((q, sem), 0):
+                need[sem] = max(need.get(sem, 0), val)
+        for sem in need:
+            eng[q].wait_ge(T.sem[sem], need[sem])
+            seen[(q, sem)] = need[sem]
+
+    def deps(q, r, w):
+        toks = []
+        for k in list(r) + list(w):
+            toks += last.get(k, [])
+        for k in w:
+            toks += [t for t in readers.get(k, []) if t[0] != q]
+        wait(q, toks)
+
+    def done(tok, r, w):
+        for k in r:
+            readers.setdefault(k, []).append(tok)
+        for k in w:
+            last[k] = [tok]
+            readers[k] = []
+
+    def E(q, r, w, fn):
+        r, w = r.split(), w.split()
+        deps(q, r, w)
+        fn(eng[q]).then_inc(T.sem[q], 1)
+        cnt[q] += 1
+        done((q, cnt[q]), r, w)
+
+    def D(q, out, in_, sem, r="", w="", fin=True):
+        deps(q, r.split(), w.split())
+        eng[q].dma_start(out, in_).then_inc(T.sem[sem], 16)
+        dsum[sem] = dsum.get(sem, 0) + 16
+        if fin:
+            done((sem, dsum[sem]), r.split(), w.split())
+
+    mine = plan(topo, core, cores)
+
+    def send(sem, r, src, dst):
+        deps("g", r.split(), [])
+        tr = []
+        for i, d in enumerate(oth):
+            k = [x for x in range(N) if x != d].index(rank)
+            rid, pid, _ = topo.addr(cores[d])
+            es = mine[cores[d]]
+            loc[0] += len(es)
+            tr.append(RemoteDMATransfer(dst_ids=[DstId(rid=rid, pnc=pid)], dma_engine_mask=sum(1 << e for e in es),
+                                        remote_sem=T.sem[sem + str(k)], srcs=[src(i)], dsts=[dst(k)]))
+        g.remote_dma_fused(tr, local_sem=T.sem.loc)
+
+    arrivals = {h: [(h + str(k), len(plan(topo, cores[d], cores)[core])) for k, d in enumerate(oth)] for h in HOPS}
+    for h, key in zip(HOPS, ("RA", "QWa", "SWa", "TV", "TE1", "TS1", "TE0", "TS0")):
+        last[key] = arrivals[h]
+
+    def u8(v):
+        return v.bitcast(dt.uint8)
+
+    def u32(v):
+        return v.bitcast(dt.uint32)
+
+    def ts(r, w, out, in0, s1, s2, o1, o2=None):
+        if o2 is None:
+            E("v", r, w, lambda e: e.tensor_scalar(out, in0, s1, None, o1))
+        else:
+            E("v", r, w, lambda e: e.tensor_scalar(out, in0, s1, s2, o1, o2))
+
+    def tt(r, w, out, a, b, op):
+        E("v", r, w, lambda e: e.tensor_tensor(out, a, b, op))
+
+    def cp(r, w, out, in_):
+        E("v", r, w, lambda e: e.tensor_copy(out, in_))
+
+    def ac(r, w, out, in_, scale=None, bias=None):
+        fn = AF.Copy if bias is None else AF.Identity
+        kw = {}
+        if scale is not None:
+            kw["scale"] = scale
+        if bias is not None:
+            kw["bias"] = bias
+        E("s", r, w, lambda e: e.activation(out, in_, fn, **kw))
+
+    def ms(w, ap, c):
+        E("v", "", w, lambda e: e.memset(ap, c))
+
+    def scan(r, w, out, d0, d1, init, o0, o1):
+        E("v", r, w, lambda e: e.tensor_tensor_scan(out, d0, d1, init, o0, o1))
+
+    def zeros(w, ap, n):
+        E("g", "", w, lambda e: e.iota(ap, [[0, n]], 0, 0, allow_small_or_imprecise_dtypes=True))
+
+    def pick(off, offk, qw, sw, qk, sk, qo, so, qok, sok):
+        E("v", offk + " " + qk, qok, lambda e: e.tensor_copy(u32(qo), u32(qw).indirect(off)))
+        E("s", offk + " " + sk, sok, lambda e: e.activation(so, sw.indirect(off), AF.Copy))
+
+    D("s", T.nxr[:], T.nx[:], "dnx", w="nxr")
+    for i in range(8):
+        D("y", T.sti[16 * i:16 * i + 16], T.st[:], "dst", w="sti", fin=(i == 7))
+        D("s", T.bti[16 * i:16 * i + 16], T.bt[:], "dbt", w="bti", fin=(i == 7))
+    D("s", T.xs[:], T.x[:], "dx", w="xs")
+    D("y", T.ws[:, 0:2048], T.w[:, 0:2048], "dw0", w="ws0")
+    D("y", T.ws[:, 2048:3072], T.w[:, 2048:3072], "dw1", w="ws1")
+
+    E("g", "", "pI", lambda e: e.iota(T.pI[:], [[1, 1]], 0, 1))
+    E("g", "", "c16", lambda e: e.iota(T.c16[:], [[16, 24]], 0, 0, allow_small_or_imprecise_dtypes=True))
+    E("g", "", "iD", lambda e: e.iota(T.iD[:], [[-1, 384]], 384, 1))
+    E("g", "", "j15", lambda e: e.iota(T.j15[:], [[0, 24], [1, 16]], 0, 0, allow_small_or_imprecise_dtypes=True))
+    E("g", "nxr", "tb", lambda e: e.partition_broadcast(T.tb[:], T.nxr[:], 128))
+
+    ms("ones", T.ones[:], 1.0)
+    ts("pI", "ci0", T.ci[:, 0:1], T.pI[:], 15, None, A.bitwise_and)
+    ts("pI", "ci1", T.ci[:, 1:2], T.pI[:], 31, None, A.bitwise_and)
+    ts("pI", "ci2", T.ci[:, 2:3], T.pI[:], 5, None, A.arith_shift_right)
+    cp("ci0 ci1 ci2", "cf", T.cf[:, 0:3], T.ci[:, 0:3])
+    r15, p31, qf = T.cf[:, 0:1], T.cf[:, 1:2], T.cf[:, 2:3]
+    ts("c16 cf", "i16", T.i16[:], T.c16[:], r15, 0.0, A.add, A.add)
+    scan("ones", "ident", T.ident[:], T.ones[:], T.ones[:], -1.0, A.add, A.mult)
+    ts("iD", "iD2", T.iD[:], T.iD[:], 15, None, A.bitwise_and)
+    ts("iD2", "mask", T.mask[:], T.iD[:], 0.0, None, A.is_equal)
+    ts("j15", "seg", T.seg[:], T.j15[:], 1.0, None, A.min)
+    ts("j15 cf", "maskb", T.maskb[:], T.j15[:, 0:32], p31, None, A.is_gt)
+
+    L = T.l0
+    ts("sti", "u1", L[:, 0:12], T.sti[:], 7, None, A.bitwise_and)
+    ts("sti", "u2", L[:, 12:24], T.sti[:], 3, None, A.arith_shift_right)
+    cp("sti", "stu", T.stu[:], T.sti[:])
+    ts("bti", "u3", L[:, 24:36], T.bti[:], 1, None, A.bitwise_and)
+    ts("bti", "u4", L[:, 36:48], T.bti[:], 1, None, A.arith_shift_right)
+    ts("u1", "u5", L[:, 48:60], L[:, 0:12], 128.0, None, A.mult)
+    ts("u3", "u6", L[:, 60:72], L[:, 24:36], 64.0, None, A.mult)
+    ts("u4", "b1x", T.b1x[:], L[:, 36:48], 256.0, None, A.mult)
+    tt("u5 u2", "u7", L[:, 72:84], L[:, 48:60], L[:, 12:24], A.add)
+    tt("b1x i16", "lbf", T.lbf[:], T.b1x[:], T.i16[:, 0:12], A.add)
+    tt("u7 u6", "u8", L[:, 84:96], L[:, 72:84], L[:, 60:72], A.add)
+    cp("lbf", "lbi", T.lbi[:], T.lbf[:])
+    cp("u8", "off0", T.off0[:], L[:, 84:96])
+    ac("ident stu", "val1A", T.val1[:], T.ident[:].indirect(T.stu[:]))
+    ac("ident lbi", "bif", T.bif[:], T.ident[:].indirect(T.lbi[:]), scale=1.0 / 512, bias=2048.0)
+    ac("ones", "w2", T.w2[:], T.ones[:, 0:576], scale=0.0)
+    for d in range(3):
+        ts("cf", "ka%d" % d, T.cf[:, 6 + d:7 + d], r15, 191.0, 15.0 - 192 + C * d, A.mult, A.add)
+    ts("c16 cf", "tri", T.tri[:], T.c16[:], r15, 192.0, A.add, A.add)
+    E("v", "xs", "QX SX", lambda e: e.quantize_mx(T.QX[:], T.SX[:], T.xs[:]))
+    D("y", u8(T.QW[:, 0:512]), u8(T.QX[:]), "dq", r="QX", w="QWo")
+    D("y", T.SW[:, 0:512], T.SX[:], "dp", r="SX", w="SWo")
+    ms("w1", T.w1[:], 0.0)
+    for d in range(3):
+        ts("cf", "kb%d" % d, T.cf[:, 9 + d:10 + d], r15, 383.0, 15.0 - 192 + C * d, A.mult, A.add)
+    ts("cf", "cf3", T.cf[:, 3:4], qf, 4.0, None, A.add)
+    ts("cf", "cf4", T.cf[:, 4:5], qf, 256.0, None, A.mult)
+    ms("scA", T.cf[0:64, 12:13], 1.0)
+    ms("scB", T.cf[64:128, 12:13], 2048.0)
+    ms("bcA", T.cf[0:64, 13:14], 0.0)
+    ms("bcB", T.cf[64:128, 13:14], 2097152.0)
+    for i, add in enumerate((288.0, 289.0, 384.0)):
+        ts("c16 cf", "trx%d" % i, T.trx[:, 12 * i:12 * i + 12], T.c16[:, 0:12], r15, add, A.add, A.add)
+    trp, trp1, trk = [T.trx[:, 12 * i:12 * i + 12] for i in range(3)]
+    for k, d in enumerate(oth):
+        ms("sk%d" % k, T.sk[:, 4 * k:4 * k + 4], 256.0 * d)
+    for q in range(N):
+        ms("vb%d" % q, T.cf[32 * q:32 * q + 32, 14:15], 1024.0 * (1 if q == rank else 1 + V + C * oth.index(q)))
+    ms("eq1", T.e0[:, 0:12], 0.0)
+    ms("i1", T.e0[:, 12:24], 0.0)
+    ms("bt3", T.bt3[:], 0.0)
+    ms("idt", T.idt[:], 0.0)
+    ms("resz0", T.res[:, 0:1], 0.0)
+    ms("resz1", T.res[:, 592:593], 0.0)
+
+    def classes(nc, t, tk, eqb, sbuf, bbuf, btbuf, r0, pbuf, xbuf, kc, p, slot):
+        kk = ["ka%d", "kb%d"][nc == 24]
+        for j, d in enumerate(oth):
+            ts(tk, p + "m%d" % j, eqb[:, nc * j:nc * j + nc], t, float(d), -16.0, A.is_equal, A.add)
+        for j in range(3):
+            scan(p + "m%d ones" % j, p + "s%d" % j, sbuf[:, nc * j:nc * j + nc], eqb[:, nc * j:nc * j + nc], T.ones[:, 0:nc], 0.0, A.add, A.mult)
+        for j in range(3):
+            ts(p + "s%d maskb" % j, p + "b%d" % j, bbuf[:, 32 * j:32 * j + 32], T.maskb[:], sbuf[:, nc * j + nc - 1:nc * j + nc], None, A.mult)
+        E("v", " ".join(p + "b%d" % j for j in range(3)), p + "t", lambda e: e.transpose(btbuf[:], bbuf[:]))
+        for j, d in enumerate(oth):
+            ts(tk, p + "e%d" % j, eqb[:, nc * (3 + j):nc * (4 + j)], t, float(d), None, A.is_equal)
+        for j in range(3):
+            E("v", p + "t", p + "r%d" % j, lambda e, j=j: e.tensor_reduce(T.rr[:, r0 + j:r0 + j + 1], btbuf[:, 32 * j:32 * j + 32], AxisListType.X, A.add))
+        for j in range(3):
+            ts(p + "s%d " % j + p + "r%d " % j + kk % j, p + "p%d" % j, pbuf[:, nc * j:nc * j + nc], sbuf[:, nc * j:nc * j + nc], T.rr[:, r0 + j:r0 + j + 1], T.cf[:, kc + j:kc + j + 1], A.add, A.add)
+        tt(" ".join(p + "p%d " % j + p + "e%d" % j for j in range(3)), p + "x", xbuf[:, 0:3 * nc], pbuf[:], eqb[:, 3 * nc:6 * nc], A.mult)
+        tt(p + "x", p + "y0", xbuf[:, 3 * nc:4 * nc], xbuf[:, 0:nc], xbuf[:, nc:2 * nc], A.add)
+        tt(p + "x tri", p + "y1", xbuf[:, 4 * nc:5 * nc], xbuf[:, 2 * nc:3 * nc], T.tri[:, 0:nc], A.add)
+        tt(p + "y0 " + p + "y1", p + "z", xbuf[:, 5 * nc:6 * nc], xbuf[:, 3 * nc:4 * nc], xbuf[:, 4 * nc:5 * nc], A.add)
+        cp(p + "z", p + "slot", slot[:], xbuf[:, 5 * nc:6 * nc])
+
+    tt("tb off0 mask", "n1m", T.n1m[:], T.tb[:].indirect(T.off0[:]), T.mask[:, 0:192], A.mult)
+    scan("n1m seg", "n1s", T.n1s[:], T.seg[:, 0:192], T.n1m[:], 0.0, A.mult, A.add)
+    cp("tb off0", "n1f", T.n1f[:], T.tb[:].indirect(T.off0[:]))
+    n1v = T.n1s[:, 15:192:16]
+    ts("n1s", "t1", T.t1[:], n1v, 1.0 / 512, -255.5 / 512, A.mult, A.add)
+    tt("n1f bif val1A", "val1B", T.val1[64:128], T.n1f[64:128], T.bif[64:128], A.add)
+    classes(12, T.t1[:], "t1", T.eqa, T.sa, T.ba, T.bta, 0, T.pa, T.xa, 6, "a", T.slot1)
+    E("v", "w1 aslot val1A val1B", "w1", lambda e: e.tensor_copy(T.w1[:].indirect(T.slot1[:]), T.val1[:]))
+    tt("w1 mask", "f1a", T.f1[:, 0:192], T.w1[:, 0:192], T.mask[:, 0:192], A.mult)
+    scan("f1a seg", "f1", T.f1[:, 192:384], T.seg[:, 0:192], T.f1[:, 0:192], 0.0, A.mult, A.add)
+    lo_, hi_ = T.f1[0:64, 207:384:16], T.f1[64:128, 207:384:16]
+    ts("f1", "R1b", T.R1[64:128], hi_, 512.0, None, A.mult)
+    ts("f1", "R1a", T.R1[0:64], hi_, 512.0, None, A.mult)
+    cp("f1", "stla", T.stl[0:64], lo_)
+    cp("f1", "stlb", T.stl[64:128], lo_)
+    send("ra", "R1a R1b", lambda i: T.R1[:, 4 * i:4 * i + 4], lambda k: T.RA[:, 4 * k:4 * k + 4])
+    pick(T.stl[:], "stla stlb", T.QX[:], T.SX[:], "QX", "SX", T.Q1[:], T.S1[:], "Q1", "S1")
+    send("qa", "Q1", lambda i: u8(T.Q1[:, C * i:C * i + C]), lambda k: u8(T.QW[:, 512 + C * k:512 + C * k + C]))
+    send("sa", "S1", lambda i: T.S1[:, C * i:C * i + C], lambda k: T.SW[:, 512 + C * k:512 + C * k + C])
+    zeros("kw", T.kw[:], 576)
+    zeros("pw", T.pw[:], 480)
+
+    lo = T.lo
+    ts("n1s", "vo", T.vo[:], n1v, 512.0, None, A.mult)
+    ts("i16", "lub", T.lub[:, 0:12], T.i16[:, 0:12], 256.0 * rank, None, A.add)
+    tt("vo b1x", "VO", T.VO[:], T.vo[:], T.b1x[:], A.add)
+    cp("lub", "luoB", T.lu[64:128, 0:12], T.lub[64:128, 0:12])
+    ts("VO", "lo0", lo[:, 0:12], T.VO[:], 2, 0x3C0, A.arith_shift_right, A.bitwise_and)
+    ts("VO", "lo1", lo[:, 12:24], T.VO[:], 12, 63, A.arith_shift_right, A.bitwise_and)
+    ts("VO", "l5o", T.l56i[:, 0:12], T.VO[:], 9, 511, A.arith_shift_right, A.bitwise_and)
+    tt("lo0 lo1", "lo2", lo[:, 24:36], lo[:, 0:12], lo[:, 12:24], A.add)
+    cp("l5o", "luoA", T.lu[0:64, 0:12], T.l56i[0:64, 0:12])
+    cp("lo2", "ofo", T.ofo[:], lo[:, 24:36])
+    cp("sti", "ladoA", T.lad[0:64, 0:12], T.sti[0:64])
+    tt("tb ofo mask", "n2mo", T.n2m[:, 0:192], T.tb[:].indirect(T.ofo[:]), T.mask[:, 0:192], A.mult)
+    cp("lo2", "ladoB", T.lad[64:128, 0:12], lo[64:128, 24:36])
+    scan("n2mo seg", "n2so", T.n2s[:, 0:192], T.seg[:, 0:192], T.n2m[:, 0:192], 0.0, A.mult, A.add)
+    ts("i16", "ladaA", T.lad[0:64, 12:24], T.i16[0:64, 0:12], 512.0, None, A.add)
+    cp("tb", "tb2B", T.tb2[64:128], T.tb[64:128])
+    ts("t1", "invo", T.inv[:, 0:12], T.t1[:], float(rank), 4096.0, A.not_equal, A.mult)
+    ac("ident", "tb2A", T.tb2[0:64], T.ident[0:64], scale=512.0)
+    ac("ident luoA luoB scA scB bcA bcB", "ufo", T.uf[:, 0:192], T.ident[:].indirect(T.lu[:, 0:12]), scale=T.cf[:, 12:13], bias=T.cf[:, 13:14])
+    ac("tb2A tb2B ladoA ladoB", "ado", T.ad[:, 0:192], T.tb2[:].indirect(T.lad[:, 0:12]))
+    ac("ident cf4", "keyc", T.vk[:, 384:576], T.ident[:, 0:192], bias=T.cf[:, 4:5])
+    ac("ident vb0 vb1 vb2 vb3", "v1", T.vk[:, 0:192], T.ident[:, 0:192], scale=1024.0, bias=T.cf[:, 14:15])
+    ac("ones", "v2a", T.vk[:, 192:384], T.ident[:, 0:192], scale=1024.0, bias=1024.0 * 385)
+
+    la = T.la
+    ts("RA", "la0", la[:, 0:12], T.RA[:], 2, 0x3C0, A.arith_shift_right, A.bitwise_and)
+    ts("RA", "la1", la[:, 12:24], T.RA[:], 12, 63, A.arith_shift_right, A.bitwise_and)
+    ts("RA", "la3", la[:, 36:48], T.RA[:], 255, None, A.bitwise_and)
+    tt("la0 la1", "la2", la[:, 24:36], la[:, 0:12], la[:, 12:24], A.add)
+    ts("RA", "l5a", T.l56i[:, 12:24], T.RA[:], 9, 511, A.arith_shift_right, A.bitwise_and)
+    cp("la2", "ofa", T.ofa[:], la[:, 24:36])
+    tt("la3 sk0 sk1 sk2", "lub1", T.lub[:, 12:24], la[:, 36:48], T.sk[:], A.add)
+    tt("tb ofa mask", "n2ma", T.n2m[:, 192:384], T.tb[:].indirect(T.ofa[:]), T.mask[:, 0:192], A.mult)
+    ts("RA", "inva", T.inv[:, 12:24], T.RA[:], 1048576.0, 4096.0, A.is_lt, A.mult)
+    scan("n2ma seg", "n2sa", T.n2s[:, 192:384], T.seg[:, 0:192], T.n2m[:, 192:384], 0.0, A.mult, A.add)
+    cp("la2", "ladaB", T.lad[64:128, 12:24], la[64:128, 24:36])
+    cp("l5a", "luaA", T.lu[0:64, 12:24], T.l56i[0:64, 12:24])
+    cp("lub1", "luaB", T.lu[64:128, 12:24], T.lub[64:128, 12:24])
+    ac("tb2A tb2B ladaA ladaB", "ada", T.ad[:, 192:384], T.tb2[:].indirect(T.lad[:, 12:24]))
+    ac("ident luaA luaB scA scB bcA bcB", "ufa", T.uf[:, 192:384], T.ident[:].indirect(T.lu[:, 12:24]), scale=T.cf[:, 12:13], bias=T.cf[:, 13:14])
+    n2v = T.n2s[:, 15:384:16]
+    tt("n2so n2sa invo inva", "n2e", T.n2e[:], n2v, T.inv[:], A.add)
+    ts("n2e", "t2", T.t2[:], T.n2e[:], 1.0 / 512, -255.5 / 512, A.mult, A.add)
+    classes(24, T.t2[:], "t2", T.eqb, T.sbb, T.bb, T.btb, 3, T.pb, T.xb, 9, "b", T.slot2)
+    tt("ufo ado ufa ada", "val2", T.val2[:], T.uf[:], T.ad[:], A.add)
+    E("v", "w2 bslot val2", "w2", lambda e: e.tensor_copy(T.w2[:].indirect(T.slot2[:]), T.val2[:]))
+    tt("w2 mask", "f2a", T.f2[:, 0:192], T.w2[:, 0:192], T.mask[:, 0:192], A.mult)
+    scan("f2a seg", "f2", T.f2[:, 192:384], T.seg[:, 0:192], T.f2[:, 0:192], 0.0, A.mult, A.add)
+    lo_, hi_ = T.f2[0:64, 207:384:16], T.f2[64:128, 207:384:16]
+    cp("f2", "R2a", T.R2[0:64], hi_)
+    cp("f2", "R2b", T.R2[64:128], hi_)
+    cp("f2", "faa", T.fa[0:64, 0:12], lo_)
+    cp("f2", "fab", T.fa[64:128, 0:12], lo_)
+    send("rb", "R2a R2b", lambda i: T.R2[:, 4 * i:4 * i + 4], lambda k: T.TV[:, 4 * k:4 * k + 4])
+    ts("faa fab", "fa1", T.fa[:, 12:24], T.fa[:, 0:12], 511, None, A.bitwise_and)
+    ts("faa fab", "fa2", T.fa[:, 24:36], T.fa[:, 0:12], 9, None, A.arith_shift_right)
+    cp("fa1", "l3", T.l34[:, 0:12], T.fa[:, 12:24])
+    cp("fa2", "l4", T.l34[:, 12:24], T.fa[:, 24:36])
+    pick(T.l34[:, 0:12], "l3", T.QX[:], T.SX[:], "QX", "SX", T.Q3[:], T.S3[:], "Q3", "S3")
+    send("qb", "Q3", lambda i: u8(T.Q3[:, C * i:C * i + C]), lambda k: u8(T.TE1[:, C * k:C * k + C]))
+    pick(T.l34[:, 12:24], "l4", T.QW[:], T.SW[:], "QWo QWa", "SWo SWa", T.Q4[:], T.S4[:], "Q4", "S4")
+    send("sb", "S3", lambda i: T.S3[:, C * i:C * i + C], lambda k: T.TS1[:, C * k:C * k + C])
+    send("qc", "Q4", lambda i: u8(T.Q4[:, C * i:C * i + C]), lambda k: u8(T.TE0[:, C * k:C * k + C]))
+    send("sc", "S4", lambda i: T.S4[:, C * i:C * i + C], lambda k: T.TS0[:, C * k:C * k + C])
+
+    ef = T.e0
+    for q in range(N):
+        k = oth.index(q) if q != rank else None
+        a, n = (0, 12) if q == rank else (12 + 4 * k, 4)
+        P = slice(32 * q, 32 * q + 32)
+        ts("t2 eq1", "eq1%d" % q, ef[P, 0:n], T.t2[P, a:a + n], float(rank), None, A.is_equal)
+        if q == rank:
+            ac("i16 i1", "i1%d" % q, ef[P, 12:24], T.i16[P, 0:12])
+        else:
+            ac("lub1 i1", "i1%d" % q, ef[P, 12:16], T.lub[P, 12 + 4 * k:16 + 4 * k], bias=-256.0 * q)
+    eks = " ".join("eq1%d i1%d" % (q, q) for q in range(N))
+    E("v", "ws0", "WQ0", lambda e: e.quantize_mx(T.WQ[:, 0:512], T.WS[:, 0:512], T.ws[:, 0:2048]))
+    tt(eks + " eq1 i1 trx2", "e2", ef[:, 24:36], ef[:, 12:24], trk, A.subtract)
+    E("v", "ws1", "WQ1", lambda e: e.quantize_mx(T.WQ[:, 512:768], T.WS[:, 512:768], T.ws[:, 2048:3072]))
+    tt(eks + " eq1 e2", "e3", ef[:, 36:48], ef[:, 24:36], ef[:, 0:12], A.mult)
+    cp("n2so n2sa", "l6i", T.l56i[:, 24:48], n2v)
+    tt("e3 trx2", "e4", ef[:, 48:60], ef[:, 36:48], trk, A.add)
+    ts("l6i", "l6j", T.l56i[:, 48:72], T.l56i[:, 24:48], 511, None, A.bitwise_and)
+    cp("e4", "o1", T.o1[:], ef[:, 48:60])
+    cp("l6j", "l6", T.l56[:, 24:48], T.l56i[:, 48:72])
+    cp("l5o l5a", "l5", T.l56[:, 0:24], T.l56i[:, 0:24])
+    E("v", "kw o1 v1", "kw", lambda e: e.tensor_copy(T.kw[:].indirect(T.o1[:]), T.vk[:, 0:192]))
+    pick(T.stu[:], "stu", T.QX[:], T.SX[:], "QX", "SX", T.QO[:], T.SO[:], "QO", "SO")
+    pick(T.l56[:, 0:24], "l5", T.QX[:], T.SX[:], "QX", "SX", T.QN1[:], T.SN1[:], "QN1", "SN1")
+
+    def mm(bank, o, k, q, s, keys, start, stop):
+        a = 128 * (k * O + o)
+        E("t", keys + " WQ0 WQ1", "ps%d" % bank if stop else "", lambda e: e.matmul_mx(
+            T.ps[:, 512 * bank:512 * bank + 192], T.WQ[:, a:a + 128], T.WS[:, a:a + 128], q, s, start, stop))
+
+    ei, hf = T.ei, T.ef
+    ts("TV", "ei0", ei[:, 0:12], T.TV[:], 11, 255, A.arith_shift_right, A.bitwise_and)
+    ts("TV", "ei1", ei[:, 12:24], T.TV[:], 19, None, A.arith_shift_right)
+    ts("TV", "ei2", ei[:, 24:36], T.TV[:], 511, None, A.bitwise_and)
+    tt("ei0 tri", "h0", hf[:, 0:12], ei[:, 0:12], T.tri[:, 0:12], A.subtract)
+    ts("ei1 cf3", "h1", hf[:, 12:24], ei[:, 12:24], T.cf[:, 3:4], None, A.is_equal)
+    tt("h0 h1", "h2", hf[:, 24:36], hf[:, 0:12], hf[:, 12:24], A.mult)
+    cp("ei2", "l7", T.l7[:], ei[:, 24:36])
+    tt("h2 tri", "h3", hf[:, 36:48], hf[:, 24:36], T.tri[:, 0:12], A.add)
+    cp("h3", "oe2", T.oe2[:], hf[:, 36:48])
+    E("v", "kw oe2 v2a", "kw", lambda e: e.tensor_copy(T.kw[:].indirect(T.oe2[:]), T.vk[:, 192:384]))
+    pick(T.l56[:, 24:48], "l6", T.QX[:], T.SX[:], "QX", "SX", T.QN2[:], T.SN2[:], "QN2", "SN2")
+    pick(T.l7[:], "l7", T.QX[:], T.SX[:], "QX", "SX", T.QE2[:], T.SE2[:], "QE2", "SE2")
+
+    for o in range(O):
+        mm(o, o, 0, T.QO[:], T.SO[:], "QO SO", True, False)
+        mm(o, o, 1, T.QN1[:, 0:192], T.SN1[:, 0:192], "QN1 SN1", False, False)
+        mm(2 + o, o, 0, T.QW[:, 512:704], T.SW[:, 512:704], "QWa SWa", True, False)
+        mm(2 + o, o, 1, T.QN1[:, 192:384], T.SN1[:, 192:384], "QN1 SN1", False, False)
+    for o in range(O):
+        mm(o, o, 2, T.QN2[:, 0:192], T.SN2[:, 0:192], "QN2 SN2", False, True)
+        mm(2 + o, o, 2, T.QN2[:, 192:384], T.SN2[:, 192:384], "QN2 SN2", False, True)
+    for o in range(O):
+        mm(4 + o, o, 2, T.QE2[:], T.SE2[:], "QE2 SE2", True, False)
+    for o in range(O):
+        mm(4 + o, o, 1, T.TE1[:], T.TS1[:], "TE1 TS1", False, False)
+    for o in range(O):
+        mm(4 + o, o, 0, T.TE0[:], T.TS0[:], "TE0 TS0", False, True)
+    for o in range(O):
+        for b in range(2):
+            ac("ps%d" % (2 * b + o), "res%d%d" % (o, b), T.res[:, 592 * o + 1 + 192 * b:592 * o + 193 + 192 * b], T.ps[:, 512 * (2 * b + o):512 * (2 * b + o) + 192])
+
+    g1, h = T.g1, T.hf
+    pres, cum, pm, mk, mf, pk = [g1[:, 192 * i:192 * i + 192] for i in range(6)]
+    ts("kw", "pres", pres, T.kw[:, 0:192], 0.0, None, A.is_gt)
+    scan("pres ones", "cum", cum, pres, T.ones[:, 0:192], 0.0, A.add, A.mult)
+    tt("pres mask", "pm", pm, pres, T.mask[:, 0:192], A.mult)
+    for a, b, n, c in ((64, 0, 64, 0), (32, 0, 32, 1), (96, 64, 32, 1), (64, 32, 32, 2), (96, 0, 32, 2)):
+        ac("cum bt3", "bx%d%d" % (a, c), T.bt3[a:a + n, c:c + 1], g1[b:b + n, 383:384])
+    tt("pm cum", "mmm", mk, pm, cum, A.mult)
+    scan("mmm seg", "mf", mf, T.seg[:, 0:192], mk, 0.0, A.mult, A.add)
+    E("v", "bt3 bx640 bx321 bx961 bx642 bx962", "base", lambda e: e.tensor_reduce(h[:, 48:49], T.bt3[:, 0:3], AxisListType.X, A.add))
+    cI = g1[:, 192 * 4 + 15:192 * 5:16]
+    ts("mf", "k0", h[:, 0:12], cI, 0.0, None, A.is_gt)
+    tt("mf trx1", "k1", h[:, 12:24], cI, trp1, A.subtract)
+    ts("k1 base", "k2", h[:, 24:36], h[:, 12:24], h[:, 48:49], None, A.add)
+    tt("kw keyc", "pk", pk, T.kw[:, 0:192], T.vk[:, 384:576], A.add)
+    tt("k0 k2", "k3", h[:, 36:48], h[:, 0:12], h[:, 24:36], A.mult)
+    tt("k3 trx0 k1 k2", "k4", h[:, 12:24], h[:, 36:48], trp, A.add)
+    cp("k4", "o3", T.o3[:], h[:, 12:24])
+    E("v", "pw o3 pk", "pw", lambda e: e.tensor_copy(T.pw[:].indirect(T.o3[:]), pk))
+    tt("pw mask", "f3a", T.f3[:, 0:288], T.pw[:, 0:288], T.mask[:, 0:288], A.mult)
+    scan("f3a seg", "f3", T.f3[:, 288:576], T.seg[:, 0:288], T.f3[:, 0:288], 0.0, A.mult, A.add)
+    f3v = T.f3[:, 303:576:16]
+    mg = T.mg
+    ac("f3", "ga", mg[0:64, 0:18], T.f3[64:128, 303:576:16])
+    cp("f3", "gb", mg[64:128, 0:18], T.f3[0:64, 303:576:16])
+    tt("f3 ga gb", "gc", mg[:, 18:36], f3v, mg[:, 0:18], A.add)
+    for q in range(N):
+        a, b = 32 * q, 32 * (q ^ 1)
+        (ac if q % 2 else cp)("gc", "gd%d" % q, mg[a:a + 32, 36:54], mg[b:b + 32, 18:36])
+    tt("gc gd0 gd1 gd2 gd3", "pki", T.pki[:, 0:18], mg[:, 18:36], mg[:, 36:54], A.add)
+    pki = T.pki[:, 0:18]
+    ts("pki", "yli", T.pki[:, 18:36], pki, 10, None, A.arith_shift_right)
+    cp("yli", "yl", T.yl[:], T.pki[:, 18:36])
+    cp("ps4", "res02", T.res[:, 385:577], T.ps[:, 512 * 4:512 * 4 + 192])
+    ac("ps5", "res12", T.res[:, 592 + 385:592 + 577], T.ps[:, 512 * 5:512 * 5 + 192])
+    E("v", "resz0 res00 res01 res02 yl", "ys0", lambda e: e.tensor_copy(T.ysb[:, 0:M], T.res[:, 0:577].indirect(T.yl[:])))
+    ac("resz1 res10 res11 res12 yl", "ys1", T.ysb[:, M:2 * M], T.res[:, 592:592 + 577].indirect(T.yl[:]))
+    D("y", T.y[:, 0:M], T.ysb[:, 0:M], "dy0", r="ys0")
+    D("s", T.y[:, M:2 * M], T.ysb[:, M:2 * M], "dy1", r="ys1")
+    ii = T.idi
+    ts("pki", "ii0", ii[:, 0:18], pki, 8, 3, A.arith_shift_right, A.bitwise_and)
+    ts("pki", "ii1", ii[:, 18:36], pki, 255, None, A.bitwise_and)
+    ts("pki", "ii2", ii[:, 36:54], pki, 1024.0, -1.0, A.is_ge, A.add)
+    tt("ii0 ii2 idt", "it0", T.idt[:, 0:18], ii[:, 0:18], ii[:, 36:54], A.add)
+    tt("ii1 ii2 idt", "it1", T.idt[:, 32:50], ii[:, 18:36], ii[:, 36:54], A.add)
+    E("v", "it0 it1 idt", "idx", lambda e: e.transpose(T.idx[:], T.idt[:]))
+    D("y", T.id[0:1, :], T.idx[0:18, 0:16], "di0", r="idx")
+    D("s", T.id[1:2, :], T.idx[0:18, 32:48], "di1", r="idx")
+
+    wait("g", [(q, cnt[q]) for q in ("v", "s", "t", "g")] + [("loc", loc[0])] + [(s, dsum[s]) for s in DMAS] + [a for h_ in HOPS for a in arrivals[h_]])

@@ -12,26 +12,26 @@ def _sb(w, d, p=128):
 
 
 SCRATCH = {
-    "nxr": _sb(1024, I, 1), "tb": _sb(1024, I), "sti": _sb(12, I), "bti": _sb(12, I),
+    "tba": _sb(1024, I), "tb": _sb(1024, I), "sb": _sb(24, I), "nv": _sb(24, F), "n1x": _sb(192, F), "nxi": _sb(64, I, 16), "nxf": _sb(64, F, 16),
     "xs": _sb(2048, B), "ws": _sb(3072, B),
     "QX": _sb(512, Q8), "SX": _sb(512, S8), "QW": _sb(704, Q8), "SW": _sb(704, S8), "WQ": _sb(768, Q8), "WS": _sb(768, S8),
     "Q1": _sb(192, Q8), "S1": _sb(192, S8), "Q3": _sb(192, Q8), "S3": _sb(192, S8), "Q4": _sb(192, Q8), "S4": _sb(192, S8),
     "TE1": _sb(192, Q8), "TS1": _sb(192, S8), "TE0": _sb(192, Q8), "TS0": _sb(192, S8),
     "QO": _sb(192, Q8), "SO": _sb(192, S8), "QN1": _sb(384, Q8), "SN1": _sb(384, S8), "QN2": _sb(384, Q8), "SN2": _sb(384, S8),
     "QE2": _sb(192, Q8), "SE2": _sb(192, S8),
-    "iD": _sb(384, I), "j15": _sb(384, F), "pI": _sb(1, I), "c16": _sb(24, F),
-    "ones": _sb(1024, F), "ident": _sb(1024, F), "mask": _sb(384, F), "seg": _sb(384, F), "maskb": _sb(32, F),
+    "j15": _sb(384, F), "pI": _sb(1, I), "c16": _sb(24, F),
+    "ones": _sb(192, F), "ident": _sb(1024, F), "mask": _sb(384, F), "seg": _sb(384, F), "maskb": _sb(32, F), "sg": _sb(204, F),
     "ci": _sb(8, I), "cf": _sb(24, F), "i16": _sb(24, F), "tri": _sb(24, F), "trx": _sb(36, F),
-    "l0": _sb(96, I), "off0": _sb(12, U), "stu": _sb(12, U), "b1x": _sb(12, F), "lbf": _sb(12, F), "lbi": _sb(12, U),
+    "l0": _sb(96, I), "lx": _sb(36, U), "b1x": _sb(24, F),
     "val1": _sb(192, F), "bif": _sb(192, F), "n1m": _sb(192, F), "n1s": _sb(192, F), "n1f": _sb(192, F), "t1": _sb(12, I),
-    "eqa": _sb(72, F), "sa": _sb(36, F), "ba": _sb(96, F), "bta": _sb(96, F), "rr": _sb(6, F), "pa": _sb(36, F),
-    "eqb": _sb(144, F), "sbb": _sb(72, F), "bb": _sb(96, F), "btb": _sb(96, F), "pb": _sb(72, F),
-    "xa": _sb(72, F), "xb": _sb(144, F), "slot1": _sb(12, U), "slot2": _sb(24, U),
-    "w1": _sb(384, F), "w2": _sb(576, F), "f1": _sb(384, F), "f2": _sb(384, F),
+    "eqa": _sb(72, F), "sa": _sb(36, F), "ba": _sb(96, F), "bta": _sb(96, F), "ra": _sb(96, F), "pa": _sb(36, F),
+    "eqb": _sb(144, F), "sbb": _sb(72, F), "bb": _sb(96, F), "btb": _sb(96, F), "rb": _sb(96, F), "pb": _sb(72, F),
+    "xa": _sb(72, F), "xb": _sb(144, F), "sl": _sb(24, U),
+    "w1": _sb(384, F), "w2": _sb(576, F), "f1": _sb(384, F), "f2": _sb(384, F), "hg": _sb(24, F),
     "R1": _sb(12, I), "RA": _sb(12, I), "R2": _sb(12, I), "TV": _sb(12, I), "stl": _sb(12, U),
-    "vo": _sb(12, F), "VO": _sb(12, I), "lo": _sb(36, I), "la": _sb(48, I), "ofo": _sb(12, U), "ofa": _sb(12, U),
-    "n2m": _sb(384, F), "n2s": _sb(384, F), "tb2": _sb(1024, F), "lad": _sb(24, U), "lu": _sb(24, U),
-    "lub": _sb(24, F), "sk": _sb(12, F), "uf": _sb(384, F), "ad": _sb(384, F), "val2": _sb(384, F), "inv": _sb(24, F), "n2e": _sb(24, F), "t2": _sb(24, I),
+    "VO": _sb(12, I), "lo": _sb(36, I), "la": _sb(48, I), "of": _sb(24, U),
+    "n2m": _sb(384, F), "n2s": _sb(384, F), "tb2": _sb(1024, F), "lad": _sb(12, U), "lu": _sb(12, U),
+    "lub": _sb(24, F), "sk": _sb(12, F), "uf": _sb(192, F), "ad": _sb(192, F), "val2": _sb(192, F), "inv": _sb(24, F), "n2e": _sb(24, F), "t2": _sb(24, I),
     "fa": _sb(36, I), "l34": _sb(24, U), "l56": _sb(48, U), "l56i": _sb(72, I),
     "e0": _sb(96, F), "o1": _sb(12, U), "kw": _sb(576, F), "vk": _sb(576, F),
     "ei": _sb(36, I), "l7": _sb(12, U), "ef": _sb(48, F), "oe2": _sb(12, U), "g1": _sb(1152, F), "bt3": _sb(4, F),
@@ -39,7 +39,7 @@ SCRATCH = {
     "idi": _sb(54, I), "idt": _sb(64, F), "idx": _sb(64, F), "res": _sb(1184, F), "ysb": _sb(576, F),
     "ps": ("psum", [128, 512 * 6], F),
 }
-DMAS = ["dnx", "dst", "dbt", "dx", "dw0", "dw1", "dq", "dp", "dy0", "dy1", "di0", "di1"]
+DMAS = ["dnx", "dst", "dx", "dw0", "dw1", "dq", "dp", "dni", "dz", "df", "dy0", "dy1", "di0", "di1"]
 HOPS = ("ra", "qa", "sa", "rb", "qb", "sb", "qc", "sc")
 SEMAPHORES = ["v", "s", "t", "g", "loc"] + DMAS + [n + str(k) for n in HOPS for k in range(N - 1)]
 
@@ -71,6 +71,8 @@ def rank_program(g, core, T, topo):
     eng = {"v": g.vector, "s": g.scalar, "t": g.tensor, "g": g, "y": g.sync}
     cnt = {q: 0 for q in eng}
     seen, last, readers, dsum, loc = {}, {}, {}, {}, [0]
+    Qd = [slice(32 * q, 32 * q + 32) for q in range(4)]
+    lower, upper, every = slice(0, 64), slice(64, 128), slice(0, 128)
 
     def wait(q, toks):
         need = {}
@@ -146,8 +148,8 @@ def rank_program(g, core, T, topo):
     def cp(r, w, out, in_):
         E("v", r, w, lambda e: e.tensor_copy(out, in_))
 
-    def ac(r, w, out, in_, scale=None, bias=None):
-        fn = AF.Copy if bias is None else AF.Identity
+    def ac(r, w, out, in_, scale=None, bias=None, fn=None):
+        fn = fn or (AF.Copy if bias is None else AF.Identity)
         kw = {}
         if scale is not None:
             kw["scale"] = scale
@@ -155,159 +157,187 @@ def rank_program(g, core, T, topo):
             kw["bias"] = bias
         E("s", r, w, lambda e: e.activation(out, in_, fn, **kw))
 
-    def ms(w, ap, c):
-        E("v", "", w, lambda e: e.memset(ap, c))
+    def co(w, ap, P, n, c):
+        ac("ident0", w, ap, T.ident[P, 0:n], scale=0.0, bias=c)
 
     def scan(r, w, out, d0, d1, init, o0, o1):
         E("v", r, w, lambda e: e.tensor_tensor_scan(out, d0, d1, init, o0, o1))
 
-    def zeros(w, ap, n):
-        E("g", "", w, lambda e: e.iota(ap, [[0, n]], 0, 0, allow_small_or_imprecise_dtypes=True))
+    def iota(w, ap, pattern, cm=0, flag=True):
+        if flag:
+            E("g", "", w, lambda e: e.iota(ap, pattern, 0, cm, allow_small_or_imprecise_dtypes=True))
+        else:
+            E("g", "", w, lambda e: e.iota(ap, pattern, 0, cm))
 
     def pick(off, offk, qw, sw, qk, sk, qo, so, qok, sok):
         E("v", offk + " " + qk, qok, lambda e: e.tensor_copy(u32(qo), u32(qw).indirect(off)))
         E("s", offk + " " + sk, sok, lambda e: e.activation(so, sw.indirect(off), AF.Copy))
 
-    D("s", T.nxr[:], T.nx[:], "dnx", w="nxr")
-    for i in range(8):
-        D("y", T.sti[16 * i:16 * i + 16], T.st[:], "dst", w="sti", fin=(i == 7))
-        D("s", T.bti[16 * i:16 * i + 16], T.bt[:], "dbt", w="bti", fin=(i == 7))
-    D("s", T.xs[:], T.x[:], "dx", w="xs")
-    D("y", T.ws[:, 0:2048], T.w[:, 0:2048], "dw0", w="ws0")
-    D("y", T.ws[:, 2048:3072], T.w[:, 2048:3072], "dw1", w="ws1")
+    D("y", T.nxi[:], T.nx[:], "dni", w="nxi")
+    for i in range(2):
+        D("y", T.sb[16 * i:16 * i + 16, 0:12], T.st[:], "dst", w="sb", fin=False)
+        D("s", T.sb[16 * i:16 * i + 16, 12:24], T.bt[:], "dst", w="sb", fin=(i == 1))
+    for i in range(16):
+        D("y", T.tba[i:i + 1, :], T.nx[:], "dnx", w="tba", fin=False)
+        D("s", T.tba[16 + i:17 + i, :], T.nx[:], "dnx", w="tba", fin=(i == 15))
+    E("v", "", "tbz", lambda e: e.memset(T.tba[Qd[1]], 0))
+    D("y", T.tba[Qd[2]], T.tba[Qd[1]], "dz", r="tbz", w="tbz1", fin=False)
+    D("y", T.tba[Qd[3]], T.tba[Qd[1]], "dz", r="tbz", w="tbz1 tbz2")
+    D("y", T.xs[:], T.x[:], "dx", w="xs")
 
-    E("g", "", "pI", lambda e: e.iota(T.pI[:], [[1, 1]], 0, 1))
-    E("g", "", "c16", lambda e: e.iota(T.c16[:], [[16, 24]], 0, 0, allow_small_or_imprecise_dtypes=True))
-    E("g", "", "iD", lambda e: e.iota(T.iD[:], [[-1, 384]], 384, 1))
-    E("g", "", "j15", lambda e: e.iota(T.j15[:], [[0, 24], [1, 16]], 0, 0, allow_small_or_imprecise_dtypes=True))
-    E("g", "nxr", "tb", lambda e: e.partition_broadcast(T.tb[:], T.nxr[:], 128))
+    iota("pI", T.pI[:], [[1, 1]], 1, False)
+    iota("c16", T.c16[:], [[16, 24]])
+    iota("j15", T.j15[:], [[0, 24], [1, 16]])
+    iota("ident0", T.ident[:, 0:256], [[1, 256]])
+    iota("sg0", T.sg[:, 0:36], [[0, 3], [1, 12]])
+    iota("sg1", T.sg[:, 36:108], [[0, 3], [1, 24]])
+    iota("sg2", T.sg[:, 108:204], [[0, 3], [1, 32]])
+    E("g", "tba", "tb", lambda e: e.partition_broadcast(T.tb[:], T.tba[0:1, :], 128))
+    ac("j15", "seg", T.seg[:], T.j15[:], fn=AF.Sign)
+    ac("sg0 sg1 sg2", "sg", T.sg[:], T.sg[:], fn=AF.Sign)
+    ac("ident0", "ident1", T.ident[:, 256:512], T.ident[:, 0:256], bias=256.0)
+    ac("ident0 ident1", "ident", T.ident[:, 512:1024], T.ident[:, 0:512], bias=512.0)
+    ac("ident0", "w1", T.w1[:, 0:256], T.ident[:, 0:256], scale=0.0)
+    ac("ident0 w1", "w1", T.w1[:, 256:384], T.ident[:, 0:128], scale=0.0)
+    ac("ident0 ident", "w2", T.w2[:], T.ident[:, 0:576], scale=0.0)
+    ac("ident0", "tb2A", T.tb2[lower], T.ident[lower], scale=512.0)
 
-    ms("ones", T.ones[:], 1.0)
+    E("v", "", "ones", lambda e: e.memset(T.ones[:], 1.0))
     ts("pI", "ci0", T.ci[:, 0:1], T.pI[:], 15, None, A.bitwise_and)
     ts("pI", "ci1", T.ci[:, 1:2], T.pI[:], 31, None, A.bitwise_and)
     ts("pI", "ci2", T.ci[:, 2:3], T.pI[:], 5, None, A.arith_shift_right)
     cp("ci0 ci1 ci2", "cf", T.cf[:, 0:3], T.ci[:, 0:3])
     r15, p31, qf = T.cf[:, 0:1], T.cf[:, 1:2], T.cf[:, 2:3]
     ts("c16 cf", "i16", T.i16[:], T.c16[:], r15, 0.0, A.add, A.add)
-    scan("ones", "ident", T.ident[:], T.ones[:], T.ones[:], -1.0, A.add, A.mult)
-    ts("iD", "iD2", T.iD[:], T.iD[:], 15, None, A.bitwise_and)
-    ts("iD2", "mask", T.mask[:], T.iD[:], 0.0, None, A.is_equal)
-    ts("j15", "seg", T.seg[:], T.j15[:], 1.0, None, A.min)
+    cp("nxi", "nxf", T.nxf[:], T.nxi[:])
+    for i in range(32):
+        D("y", T.tb2[64 + i:65 + i, :], T.nxf[:], "df", r="nxf", w="tb2B", fin=(i == 31))
+    D("y", T.ws[:, 0:2048], T.w[:, 0:2048], "dw0", w="ws0")
+    D("y", T.ws[:, 2048:3072], T.w[:, 2048:3072], "dw1", w="ws1")
+    ts("j15 cf", "mask", T.mask[:], T.j15[:], r15, None, A.is_equal)
     ts("j15 cf", "maskb", T.maskb[:], T.j15[:, 0:32], p31, None, A.is_gt)
 
     L = T.l0
-    ts("sti", "u1", L[:, 0:12], T.sti[:], 7, None, A.bitwise_and)
-    ts("sti", "u2", L[:, 12:24], T.sti[:], 3, None, A.arith_shift_right)
-    cp("sti", "stu", T.stu[:], T.sti[:])
-    ts("bti", "u3", L[:, 24:36], T.bti[:], 1, None, A.bitwise_and)
-    ts("bti", "u4", L[:, 36:48], T.bti[:], 1, None, A.arith_shift_right)
+    sti, bti = T.sb[:, 0:12], T.sb[:, 12:24]
+    off0, stu, lbi = [T.lx[:, 12 * i:12 * i + 12] for i in range(3)]
+    b1x = T.b1x[:, 0:12]
+    cp("sb", "sb1", T.sb[Qd[1]], T.sb[Qd[0]])
+    cp("sb sb1", "sb2", T.sb[upper], T.sb[lower])
+    ts("sb sb1 sb2", "u1", L[:, 0:12], sti, 7, None, A.bitwise_and)
+    ts("sb", "u2", L[:, 12:24], sti, 3, None, A.arith_shift_right)
+    cp("sb", "stu", stu, sti)
+    ts("sb", "u3", L[:, 24:36], bti, 1, None, A.bitwise_and)
+    ts("sb", "u4", L[:, 36:48], bti, 1, None, A.arith_shift_right)
     ts("u1", "u5", L[:, 48:60], L[:, 0:12], 128.0, None, A.mult)
     ts("u3", "u6", L[:, 60:72], L[:, 24:36], 64.0, None, A.mult)
-    ts("u4", "b1x", T.b1x[:], L[:, 36:48], 256.0, None, A.mult)
+    ts("u4", "b1x", b1x, L[:, 36:48], 256.0, None, A.mult)
     tt("u5 u2", "u7", L[:, 72:84], L[:, 48:60], L[:, 12:24], A.add)
-    tt("b1x i16", "lbf", T.lbf[:], T.b1x[:], T.i16[:, 0:12], A.add)
+    tt("b1x i16", "lbf", T.b1x[:, 12:24], b1x, T.i16[:, 0:12], A.add)
     tt("u7 u6", "u8", L[:, 84:96], L[:, 72:84], L[:, 60:72], A.add)
-    cp("lbf", "lbi", T.lbi[:], T.lbf[:])
-    cp("u8", "off0", T.off0[:], L[:, 84:96])
-    ac("ident stu", "val1A", T.val1[:], T.ident[:].indirect(T.stu[:]))
-    ac("ident lbi", "bif", T.bif[:], T.ident[:].indirect(T.lbi[:]), scale=1.0 / 512, bias=2048.0)
-    ac("ones", "w2", T.w2[:], T.ones[:, 0:576], scale=0.0)
+    cp("lbf", "lbi", lbi, T.b1x[:, 12:24])
+    cp("u8", "off0", off0, L[:, 84:96])
+    ac("ident stu", "val1A", T.val1[:], T.ident[:].indirect(stu))
+    ac("ident lbi", "bif", T.bif[:], T.ident[:].indirect(lbi), scale=1.0 / 512, bias=2048.0)
     for d in range(3):
         ts("cf", "ka%d" % d, T.cf[:, 6 + d:7 + d], r15, 191.0, 15.0 - 192 + C * d, A.mult, A.add)
     ts("c16 cf", "tri", T.tri[:], T.c16[:], r15, 192.0, A.add, A.add)
-    E("v", "xs", "QX SX", lambda e: e.quantize_mx(T.QX[:], T.SX[:], T.xs[:]))
-    D("y", u8(T.QW[:, 0:512]), u8(T.QX[:]), "dq", r="QX", w="QWo")
-    D("y", T.SW[:, 0:512], T.SX[:], "dp", r="SX", w="SWo")
-    ms("w1", T.w1[:], 0.0)
-    for d in range(3):
-        ts("cf", "kb%d" % d, T.cf[:, 9 + d:10 + d], r15, 383.0, 15.0 - 192 + C * d, A.mult, A.add)
-    ts("cf", "cf3", T.cf[:, 3:4], qf, 4.0, None, A.add)
-    ts("cf", "cf4", T.cf[:, 4:5], qf, 256.0, None, A.mult)
-    ms("scA", T.cf[0:64, 12:13], 1.0)
-    ms("scB", T.cf[64:128, 12:13], 2048.0)
-    ms("bcA", T.cf[0:64, 13:14], 0.0)
-    ms("bcB", T.cf[64:128, 13:14], 2097152.0)
-    for i, add in enumerate((288.0, 289.0, 384.0)):
-        ts("c16 cf", "trx%d" % i, T.trx[:, 12 * i:12 * i + 12], T.c16[:, 0:12], r15, add, A.add, A.add)
-    trp, trp1, trk = [T.trx[:, 12 * i:12 * i + 12] for i in range(3)]
-    for k, d in enumerate(oth):
-        ms("sk%d" % k, T.sk[:, 4 * k:4 * k + 4], 256.0 * d)
-    for q in range(N):
-        ms("vb%d" % q, T.cf[32 * q:32 * q + 32, 14:15], 1024.0 * (1 if q == rank else 1 + V + C * oth.index(q)))
-    ms("eq1", T.e0[:, 0:12], 0.0)
-    ms("i1", T.e0[:, 12:24], 0.0)
-    ms("bt3", T.bt3[:], 0.0)
-    ms("idt", T.idt[:], 0.0)
-    ms("resz0", T.res[:, 0:1], 0.0)
-    ms("resz1", T.res[:, 592:593], 0.0)
 
-    def classes(nc, t, tk, eqb, sbuf, bbuf, btbuf, r0, pbuf, xbuf, kc, p, slot):
+    def classes(nc, t, tk, eqb, sbuf, bbuf, btbuf, rbuf, pbuf, xbuf, kc, p, s0):
         kk = ["ka%d", "kb%d"][nc == 24]
+        w = 3 * nc
         for j, d in enumerate(oth):
             ts(tk, p + "m%d" % j, eqb[:, nc * j:nc * j + nc], t, float(d), -16.0, A.is_equal, A.add)
+        scan(p + "m0 " + p + "m1 " + p + "m2 sg", p + "s", sbuf[:], T.sg[:, s0:s0 + w], eqb[:, 0:w], 0.0, A.mult, A.add)
         for j in range(3):
-            scan(p + "m%d ones" % j, p + "s%d" % j, sbuf[:, nc * j:nc * j + nc], eqb[:, nc * j:nc * j + nc], T.ones[:, 0:nc], 0.0, A.add, A.mult)
-        for j in range(3):
-            ts(p + "s%d maskb" % j, p + "b%d" % j, bbuf[:, 32 * j:32 * j + 32], T.maskb[:], sbuf[:, nc * j + nc - 1:nc * j + nc], None, A.mult)
+            ts(p + "s maskb", p + "b%d" % j, bbuf[:, 32 * j:32 * j + 32], T.maskb[:], sbuf[:, nc * j + nc - 1:nc * j + nc], None, A.mult)
         E("v", " ".join(p + "b%d" % j for j in range(3)), p + "t", lambda e: e.transpose(btbuf[:], bbuf[:]))
-        for j, d in enumerate(oth):
-            ts(tk, p + "e%d" % j, eqb[:, nc * (3 + j):nc * (4 + j)], t, float(d), None, A.is_equal)
+        ts(p + "m0", p + "e", eqb[:, w:2 * w], eqb[:, 0:w], 16.0, None, A.add)
+        scan(p + "t sg", p + "r", rbuf[:], T.sg[:, 108:204], btbuf[:], 0.0, A.mult, A.add)
         for j in range(3):
-            E("v", p + "t", p + "r%d" % j, lambda e, j=j: e.tensor_reduce(T.rr[:, r0 + j:r0 + j + 1], btbuf[:, 32 * j:32 * j + 32], AxisListType.X, A.add))
-        for j in range(3):
-            ts(p + "s%d " % j + p + "r%d " % j + kk % j, p + "p%d" % j, pbuf[:, nc * j:nc * j + nc], sbuf[:, nc * j:nc * j + nc], T.rr[:, r0 + j:r0 + j + 1], T.cf[:, kc + j:kc + j + 1], A.add, A.add)
-        tt(" ".join(p + "p%d " % j + p + "e%d" % j for j in range(3)), p + "x", xbuf[:, 0:3 * nc], pbuf[:], eqb[:, 3 * nc:6 * nc], A.mult)
-        tt(p + "x", p + "y0", xbuf[:, 3 * nc:4 * nc], xbuf[:, 0:nc], xbuf[:, nc:2 * nc], A.add)
+            ts(p + "s " + p + "r " + kk % j, p + "p%d" % j, pbuf[:, nc * j:nc * j + nc], sbuf[:, nc * j:nc * j + nc], rbuf[:, 32 * j + 31:32 * j + 32], T.cf[:, kc + j:kc + j + 1], A.add, A.add)
+        tt(" ".join(p + "p%d" % j for j in range(3)) + " " + p + "e", p + "x", xbuf[:, 0:w], pbuf[:], eqb[:, w:2 * w], A.mult)
         tt(p + "x tri", p + "y1", xbuf[:, 4 * nc:5 * nc], xbuf[:, 2 * nc:3 * nc], T.tri[:, 0:nc], A.add)
+        tt(p + "x", p + "y0", xbuf[:, 3 * nc:4 * nc], xbuf[:, 0:nc], xbuf[:, nc:2 * nc], A.add)
         tt(p + "y0 " + p + "y1", p + "z", xbuf[:, 5 * nc:6 * nc], xbuf[:, 3 * nc:4 * nc], xbuf[:, 4 * nc:5 * nc], A.add)
-        cp(p + "z", p + "slot", slot[:], xbuf[:, 5 * nc:6 * nc])
 
-    tt("tb off0 mask", "n1m", T.n1m[:], T.tb[:].indirect(T.off0[:]), T.mask[:, 0:192], A.mult)
+    tt("tba tbz tbz1 tbz2 off0 mask", "n1m", T.n1m[:], T.tba[:].indirect(off0), T.mask[:, 0:192], A.mult)
     scan("n1m seg", "n1s", T.n1s[:], T.seg[:, 0:192], T.n1m[:], 0.0, A.mult, A.add)
-    cp("tb off0", "n1f", T.n1f[:], T.tb[:].indirect(T.off0[:]))
-    n1v = T.n1s[:, 15:192:16]
-    ts("n1s", "t1", T.t1[:], n1v, 1.0 / 512, -255.5 / 512, A.mult, A.add)
-    tt("n1f bif val1A", "val1B", T.val1[64:128], T.n1f[64:128], T.bif[64:128], A.add)
-    classes(12, T.t1[:], "t1", T.eqa, T.sa, T.ba, T.bta, 0, T.pa, T.xa, 6, "a", T.slot1)
-    E("v", "w1 aslot val1A val1B", "w1", lambda e: e.tensor_copy(T.w1[:].indirect(T.slot1[:]), T.val1[:]))
+    cp("tba off0", "n1f", T.n1f[:], T.tba[:].indirect(off0))
+    n1v = T.n1s[0:32, 15:192:16]
+    for q in range(4):
+        ts("n1s", "t1%d" % q, T.t1[Qd[q]], n1v, 1.0 / 512, -255.5 / 512, A.mult, A.add)
+    ac("n1f", "n1x2", T.n1x[Qd[2]], T.n1f[Qd[0]])
+    ac("n1f", "n1x3", T.n1x[Qd[3]], T.n1f[Qd[0]])
+    for q in range(4):
+        ac("n1s", "nv%d" % q, T.nv[Qd[q], 0:12], n1v)
+    co("scA", T.cf[lower, 12:13], lower, 1, 1.0)
+    co("scB", T.cf[upper, 12:13], upper, 1, 2048.0)
+    co("bcA", T.cf[lower, 13:14], lower, 1, 0.0)
+    co("bcB", T.cf[upper, 13:14], upper, 1, 2097152.0)
+    ac("i16", "lub", T.lub[:, 0:12], T.i16[:, 0:12], bias=256.0 * rank)
+    for k, d in enumerate(oth):
+        co("sk%d" % k, T.sk[:, 4 * k:4 * k + 4], every, 4, 256.0 * d)
+    for d in range(3):
+        ac("cf", "kb%d" % d, T.cf[:, 9 + d:10 + d], r15, scale=383.0, bias=15.0 - 192 + C * d)
+    ac("cf", "cf3", T.cf[:, 3:4], qf, bias=4.0)
+    ac("cf", "cf4", T.cf[:, 4:5], qf, scale=256.0)
+    for i, add in enumerate((288.0, 289.0, 384.0)):
+        ac("i16", "trx%d" % i, T.trx[:, 12 * i:12 * i + 12], T.i16[:, 0:12], bias=add)
+    trp, trp1, trk = [T.trx[:, 12 * i:12 * i + 12] for i in range(3)]
+    for q in range(N):
+        co("vb%d" % q, T.cf[Qd[q], 14:15], Qd[q], 1, 1024.0 * (1 if q == rank else 1 + V + C * oth.index(q)))
+    co("eq1", T.e0[:, 0:12], every, 12, 0.0)
+    co("i1", T.e0[:, 12:24], every, 12, 0.0)
+    co("bt3", T.bt3[:], every, 4, 0.0)
+    co("idt", T.idt[:], every, 64, 0.0)
+    co("resz0", T.res[:, 0:1], every, 1, 0.0)
+    co("resz1", T.res[:, 592:593], every, 1, 0.0)
+
+    classes(12, T.t1[:], "t10 t11 t12 t13", T.eqa, T.sa, T.ba, T.bta, T.ra, T.pa, T.xa, 6, "a", 0)
+    slot1 = T.sl[:, 0:12]
+    cp("az", "aslot", slot1, T.xa[:, 60:72])
+    tt("n1x2 n1x3 bif val1A", "val1B", T.val1[upper], T.n1x[upper], T.bif[upper], A.add)
+    E("v", "w1 aslot val1A val1B", "w1", lambda e: e.tensor_copy(T.w1[:].indirect(slot1), T.val1[:]))
     tt("w1 mask", "f1a", T.f1[:, 0:192], T.w1[:, 0:192], T.mask[:, 0:192], A.mult)
     scan("f1a seg", "f1", T.f1[:, 192:384], T.seg[:, 0:192], T.f1[:, 0:192], 0.0, A.mult, A.add)
-    lo_, hi_ = T.f1[0:64, 207:384:16], T.f1[64:128, 207:384:16]
-    ts("f1", "R1b", T.R1[64:128], hi_, 512.0, None, A.mult)
-    ts("f1", "R1a", T.R1[0:64], hi_, 512.0, None, A.mult)
-    cp("f1", "stla", T.stl[0:64], lo_)
-    cp("f1", "stlb", T.stl[64:128], lo_)
+    lo_, hi_ = T.f1[lower, 207:384:16], T.f1[upper, 207:384:16]
+    ts("f1", "R1b", T.R1[upper], hi_, 512.0, None, A.mult)
+    ts("f1", "R1a", T.R1[lower], hi_, 512.0, None, A.mult)
+    cp("f1", "stla", T.stl[lower], lo_)
+    cp("f1", "stlb", T.stl[upper], lo_)
     send("ra", "R1a R1b", lambda i: T.R1[:, 4 * i:4 * i + 4], lambda k: T.RA[:, 4 * k:4 * k + 4])
+    E("v", "xs", "QX SX", lambda e: e.quantize_mx(T.QX[:], T.SX[:], T.xs[:]))
     pick(T.stl[:], "stla stlb", T.QX[:], T.SX[:], "QX", "SX", T.Q1[:], T.S1[:], "Q1", "S1")
     send("qa", "Q1", lambda i: u8(T.Q1[:, C * i:C * i + C]), lambda k: u8(T.QW[:, 512 + C * k:512 + C * k + C]))
     send("sa", "S1", lambda i: T.S1[:, C * i:C * i + C], lambda k: T.SW[:, 512 + C * k:512 + C * k + C])
-    zeros("kw", T.kw[:], 576)
-    zeros("pw", T.pw[:], 480)
+    D("y", u8(T.QW[:, 0:512]), u8(T.QX[:]), "dq", r="QX", w="QWo")
+    D("y", T.SW[:, 0:512], T.SX[:], "dp", r="SX", w="SWo")
+    iota("kw", T.kw[:], [[0, 576]])
+    iota("pw", T.pw[:], [[0, 480]])
 
-    lo = T.lo
-    ts("n1s", "vo", T.vo[:], n1v, 512.0, None, A.mult)
-    ts("i16", "lub", T.lub[:, 0:12], T.i16[:, 0:12], 256.0 * rank, None, A.add)
-    tt("vo b1x", "VO", T.VO[:], T.vo[:], T.b1x[:], A.add)
-    cp("lub", "luoB", T.lu[64:128, 0:12], T.lub[64:128, 0:12])
+    lo, ofo, ofa = T.lo, T.of[:, 0:12], T.of[:, 12:24]
+    ts("nv0 nv1 nv2 nv3", "vo", T.nv[:, 12:24], T.nv[:, 0:12], 512.0, None, A.mult)
+    tt("vo b1x", "VO", T.VO[:], T.nv[:, 12:24], b1x, A.add)
     ts("VO", "lo0", lo[:, 0:12], T.VO[:], 2, 0x3C0, A.arith_shift_right, A.bitwise_and)
     ts("VO", "lo1", lo[:, 12:24], T.VO[:], 12, 63, A.arith_shift_right, A.bitwise_and)
     ts("VO", "l5o", T.l56i[:, 0:12], T.VO[:], 9, 511, A.arith_shift_right, A.bitwise_and)
     tt("lo0 lo1", "lo2", lo[:, 24:36], lo[:, 0:12], lo[:, 12:24], A.add)
-    cp("l5o", "luoA", T.lu[0:64, 0:12], T.l56i[0:64, 0:12])
-    cp("lo2", "ofo", T.ofo[:], lo[:, 24:36])
-    cp("sti", "ladoA", T.lad[0:64, 0:12], T.sti[0:64])
-    tt("tb ofo mask", "n2mo", T.n2m[:, 0:192], T.tb[:].indirect(T.ofo[:]), T.mask[:, 0:192], A.mult)
-    cp("lo2", "ladoB", T.lad[64:128, 0:12], lo[64:128, 24:36])
+    ts("t10 t11 t12 t13", "invo", T.inv[:, 0:12], T.t1[:], float(rank), 4096.0, A.not_equal, A.mult)
+    cp("lo2", "ofo", ofo, lo[:, 24:36])
+    pick(stu, "stu", T.QX[:], T.SX[:], "QX", "SX", T.QO[:], T.SO[:], "QO", "SO")
+    tt("tb ofo mask", "n2mo", T.n2m[:, 0:192], T.tb[:].indirect(ofo), T.mask[:, 0:192], A.mult)
+    cp("l5o", "lu0", T.lu[Qd[0]], T.l56i[Qd[0], 0:12])
     scan("n2mo seg", "n2so", T.n2s[:, 0:192], T.seg[:, 0:192], T.n2m[:, 0:192], 0.0, A.mult, A.add)
-    ts("i16", "ladaA", T.lad[0:64, 12:24], T.i16[0:64, 0:12], 512.0, None, A.add)
-    cp("tb", "tb2B", T.tb2[64:128], T.tb[64:128])
-    ts("t1", "invo", T.inv[:, 0:12], T.t1[:], float(rank), 4096.0, A.not_equal, A.mult)
-    ac("ident", "tb2A", T.tb2[0:64], T.ident[0:64], scale=512.0)
-    ac("ident luoA luoB scA scB bcA bcB", "ufo", T.uf[:, 0:192], T.ident[:].indirect(T.lu[:, 0:12]), scale=T.cf[:, 12:13], bias=T.cf[:, 13:14])
-    ac("tb2A tb2B ladoA ladoB", "ado", T.ad[:, 0:192], T.tb2[:].indirect(T.lad[:, 0:12]))
+    cp("lub", "lu2", T.lu[Qd[2]], T.lub[Qd[2], 0:12])
+    cp("sb", "lad0", T.lad[Qd[0]], T.sb[Qd[0], 0:12])
+    ts("i16", "lad1", T.lad[Qd[1]], T.i16[Qd[1], 0:12], 512.0, None, A.add)
+    cp("lo2", "lad2", T.lad[Qd[2]], lo[Qd[2], 24:36])
+    ac("tb2B", "tb2C", T.tb2[Qd[3]], T.tb2[Qd[2]])
     ac("ident cf4", "keyc", T.vk[:, 384:576], T.ident[:, 0:192], bias=T.cf[:, 4:5])
     ac("ident vb0 vb1 vb2 vb3", "v1", T.vk[:, 0:192], T.ident[:, 0:192], scale=1024.0, bias=T.cf[:, 14:15])
-    ac("ones", "v2a", T.vk[:, 192:384], T.ident[:, 0:192], scale=1024.0, bias=1024.0 * 385)
+    ac("ident", "v2a", T.vk[:, 192:384], T.ident[:, 0:192], scale=1024.0, bias=1024.0 * 385)
+    E("v", "ws0", "WQ0", lambda e: e.quantize_mx(T.WQ[:, 0:512], T.WS[:, 0:512], T.ws[:, 0:2048]))
+    E("v", "ws1", "WQ1", lambda e: e.quantize_mx(T.WQ[:, 512:768], T.WS[:, 512:768], T.ws[:, 2048:3072]))
 
     la = T.la
     ts("RA", "la0", la[:, 0:12], T.RA[:], 2, 0x3C0, A.arith_shift_right, A.bitwise_and)
@@ -315,29 +345,36 @@ def rank_program(g, core, T, topo):
     ts("RA", "la3", la[:, 36:48], T.RA[:], 255, None, A.bitwise_and)
     tt("la0 la1", "la2", la[:, 24:36], la[:, 0:12], la[:, 12:24], A.add)
     ts("RA", "l5a", T.l56i[:, 12:24], T.RA[:], 9, 511, A.arith_shift_right, A.bitwise_and)
-    cp("la2", "ofa", T.ofa[:], la[:, 24:36])
+    cp("la2", "ofa", ofa, la[:, 24:36])
     tt("la3 sk0 sk1 sk2", "lub1", T.lub[:, 12:24], la[:, 36:48], T.sk[:], A.add)
-    tt("tb ofa mask", "n2ma", T.n2m[:, 192:384], T.tb[:].indirect(T.ofa[:]), T.mask[:, 0:192], A.mult)
+    tt("tb ofa mask", "n2ma", T.n2m[:, 192:384], T.tb[:].indirect(ofa), T.mask[:, 0:192], A.mult)
     ts("RA", "inva", T.inv[:, 12:24], T.RA[:], 1048576.0, 4096.0, A.is_lt, A.mult)
     scan("n2ma seg", "n2sa", T.n2s[:, 192:384], T.seg[:, 0:192], T.n2m[:, 192:384], 0.0, A.mult, A.add)
-    cp("la2", "ladaB", T.lad[64:128, 12:24], la[64:128, 24:36])
-    cp("l5a", "luaA", T.lu[0:64, 12:24], T.l56i[0:64, 12:24])
-    cp("lub1", "luaB", T.lu[64:128, 12:24], T.lub[64:128, 12:24])
-    ac("tb2A tb2B ladaA ladaB", "ada", T.ad[:, 192:384], T.tb2[:].indirect(T.lad[:, 12:24]))
-    ac("ident luaA luaB scA scB bcA bcB", "ufa", T.uf[:, 192:384], T.ident[:].indirect(T.lu[:, 12:24]), scale=T.cf[:, 12:13], bias=T.cf[:, 13:14])
+    cp("la2", "lad3", T.lad[Qd[3]], la[Qd[3], 24:36])
     n2v = T.n2s[:, 15:384:16]
     tt("n2so n2sa invo inva", "n2e", T.n2e[:], n2v, T.inv[:], A.add)
+    cp("l5a", "lu1", T.lu[Qd[1]], T.l56i[Qd[1], 12:24])
     ts("n2e", "t2", T.t2[:], T.n2e[:], 1.0 / 512, -255.5 / 512, A.mult, A.add)
-    classes(24, T.t2[:], "t2", T.eqb, T.sbb, T.bb, T.btb, 3, T.pb, T.xb, 9, "b", T.slot2)
-    tt("ufo ado ufa ada", "val2", T.val2[:], T.uf[:], T.ad[:], A.add)
-    E("v", "w2 bslot val2", "w2", lambda e: e.tensor_copy(T.w2[:].indirect(T.slot2[:]), T.val2[:]))
+    cp("lub1", "lu3", T.lu[Qd[3]], T.lub[Qd[3], 12:24])
+    ac("tb2A tb2B tb2C lad0 lad1 lad2 lad3", "ad", T.ad[:], T.tb2[:].indirect(T.lad[:]))
+    ac("ident lu0 lu1 lu2 lu3 scA scB bcA bcB", "uf", T.uf[:], T.ident[:].indirect(T.lu[:]), scale=T.cf[:, 12:13], bias=T.cf[:, 13:14])
+    classes(24, T.t2[:], "t2", T.eqb, T.sbb, T.bb, T.btb, T.rb, T.pb, T.xb, 9, "b", 36)
+    slot2 = T.sl[:, 12:24]
+    for q in range(4):
+        a = 120 + 12 * (q % 2)
+        cp("bz", "bslot%d" % q, T.sl[Qd[q], 12:24], T.xb[Qd[q], a:a + 12])
+    tt("uf ad", "val2", T.val2[:], T.uf[:], T.ad[:], A.add)
+    E("v", "w2 bslot0 bslot1 bslot2 bslot3 val2", "w2", lambda e: e.tensor_copy(T.w2[:].indirect(slot2), T.val2[:]))
     tt("w2 mask", "f2a", T.f2[:, 0:192], T.w2[:, 0:192], T.mask[:, 0:192], A.mult)
     scan("f2a seg", "f2", T.f2[:, 192:384], T.seg[:, 0:192], T.f2[:, 0:192], 0.0, A.mult, A.add)
-    lo_, hi_ = T.f2[0:64, 207:384:16], T.f2[64:128, 207:384:16]
-    cp("f2", "R2a", T.R2[0:64], hi_)
-    cp("f2", "R2b", T.R2[64:128], hi_)
-    cp("f2", "faa", T.fa[0:64, 0:12], lo_)
-    cp("f2", "fab", T.fa[64:128, 0:12], lo_)
+    for q in range(4):
+        (ac if q % 2 else cp)("f2", "hg%d" % q, T.hg[Qd[q], 0:12], T.f2[Qd[q ^ 1], 207:384:16])
+    tt("f2 hg0 hg1 hg2 hg3", "hh", T.hg[:, 12:24], T.f2[:, 207:384:16], T.hg[:, 0:12], A.add)
+    lo_, hi_ = T.hg[lower, 12:24], T.hg[upper, 12:24]
+    cp("hh", "R2a", T.R2[lower], hi_)
+    cp("hh", "R2b", T.R2[upper], hi_)
+    cp("hh", "faa", T.fa[lower, 0:12], lo_)
+    cp("hh", "fab", T.fa[upper, 0:12], lo_)
     send("rb", "R2a R2b", lambda i: T.R2[:, 4 * i:4 * i + 4], lambda k: T.TV[:, 4 * k:4 * k + 4])
     ts("faa fab", "fa1", T.fa[:, 12:24], T.fa[:, 0:12], 511, None, A.bitwise_and)
     ts("faa fab", "fa2", T.fa[:, 24:36], T.fa[:, 0:12], 9, None, A.arith_shift_right)
@@ -354,25 +391,21 @@ def rank_program(g, core, T, topo):
     for q in range(N):
         k = oth.index(q) if q != rank else None
         a, n = (0, 12) if q == rank else (12 + 4 * k, 4)
-        P = slice(32 * q, 32 * q + 32)
-        ts("t2 eq1", "eq1%d" % q, ef[P, 0:n], T.t2[P, a:a + n], float(rank), None, A.is_equal)
+        ts("t2 eq1", "eq1%d" % q, ef[Qd[q], 0:n], T.t2[Qd[q], a:a + n], float(rank), None, A.is_equal)
         if q == rank:
-            ac("i16 i1", "i1%d" % q, ef[P, 12:24], T.i16[P, 0:12])
+            ac("i16 i1", "i1%d" % q, ef[Qd[q], 12:24], T.i16[Qd[q], 0:12])
         else:
-            ac("lub1 i1", "i1%d" % q, ef[P, 12:16], T.lub[P, 12 + 4 * k:16 + 4 * k], bias=-256.0 * q)
+            ac("lub1 i1", "i1%d" % q, ef[Qd[q], 12:16], T.lub[Qd[q], 12 + 4 * k:16 + 4 * k], bias=-256.0 * q)
     eks = " ".join("eq1%d i1%d" % (q, q) for q in range(N))
-    E("v", "ws0", "WQ0", lambda e: e.quantize_mx(T.WQ[:, 0:512], T.WS[:, 0:512], T.ws[:, 0:2048]))
-    tt(eks + " eq1 i1 trx2", "e2", ef[:, 24:36], ef[:, 12:24], trk, A.subtract)
-    E("v", "ws1", "WQ1", lambda e: e.quantize_mx(T.WQ[:, 512:768], T.WS[:, 512:768], T.ws[:, 2048:3072]))
-    tt(eks + " eq1 e2", "e3", ef[:, 36:48], ef[:, 24:36], ef[:, 0:12], A.mult)
     cp("n2so n2sa", "l6i", T.l56i[:, 24:48], n2v)
-    tt("e3 trx2", "e4", ef[:, 48:60], ef[:, 36:48], trk, A.add)
+    tt(eks + " eq1 i1 trx2", "e2", ef[:, 24:36], ef[:, 12:24], trk, A.subtract)
     ts("l6i", "l6j", T.l56i[:, 48:72], T.l56i[:, 24:48], 511, None, A.bitwise_and)
-    cp("e4", "o1", T.o1[:], ef[:, 48:60])
-    cp("l6j", "l6", T.l56[:, 24:48], T.l56i[:, 48:72])
+    tt(eks + " eq1 e2", "e3", ef[:, 36:48], ef[:, 24:36], ef[:, 0:12], A.mult)
     cp("l5o l5a", "l5", T.l56[:, 0:24], T.l56i[:, 0:24])
+    tt("e3 trx2", "e4", ef[:, 48:60], ef[:, 36:48], trk, A.add)
+    cp("l6j", "l6", T.l56[:, 24:48], T.l56i[:, 48:72])
+    cp("e4", "o1", T.o1[:], ef[:, 48:60])
     E("v", "kw o1 v1", "kw", lambda e: e.tensor_copy(T.kw[:].indirect(T.o1[:]), T.vk[:, 0:192]))
-    pick(T.stu[:], "stu", T.QX[:], T.SX[:], "QX", "SX", T.QO[:], T.SO[:], "QO", "SO")
     pick(T.l56[:, 0:24], "l5", T.QX[:], T.SX[:], "QX", "SX", T.QN1[:], T.SN1[:], "QN1", "SN1")
 
     def mm(bank, o, k, q, s, keys, start, stop):
@@ -396,8 +429,9 @@ def rank_program(g, core, T, topo):
 
     for o in range(O):
         mm(o, o, 0, T.QO[:], T.SO[:], "QO SO", True, False)
-        mm(o, o, 1, T.QN1[:, 0:192], T.SN1[:, 0:192], "QN1 SN1", False, False)
         mm(2 + o, o, 0, T.QW[:, 512:704], T.SW[:, 512:704], "QWa SWa", True, False)
+    for o in range(O):
+        mm(o, o, 1, T.QN1[:, 0:192], T.SN1[:, 0:192], "QN1 SN1", False, False)
         mm(2 + o, o, 1, T.QN1[:, 192:384], T.SN1[:, 192:384], "QN1 SN1", False, False)
     for o in range(O):
         mm(o, o, 2, T.QN2[:, 0:192], T.SN2[:, 0:192], "QN2 SN2", False, True)
@@ -408,17 +442,17 @@ def rank_program(g, core, T, topo):
         mm(4 + o, o, 1, T.TE1[:], T.TS1[:], "TE1 TS1", False, False)
     for o in range(O):
         mm(4 + o, o, 0, T.TE0[:], T.TS0[:], "TE0 TS0", False, True)
-    for o in range(O):
-        for b in range(2):
-            ac("ps%d" % (2 * b + o), "res%d%d" % (o, b), T.res[:, 592 * o + 1 + 192 * b:592 * o + 193 + 192 * b], T.ps[:, 512 * (2 * b + o):512 * (2 * b + o) + 192])
 
     g1, h = T.g1, T.hf
     pres, cum, pm, mk, mf, pk = [g1[:, 192 * i:192 * i + 192] for i in range(6)]
-    ts("kw", "pres", pres, T.kw[:, 0:192], 0.0, None, A.is_gt)
-    scan("pres ones", "cum", cum, pres, T.ones[:, 0:192], 0.0, A.add, A.mult)
-    tt("pres mask", "pm", pm, pres, T.mask[:, 0:192], A.mult)
+    ac("kw", "pres", pres, T.kw[:, 0:192], fn=AF.Sign)
+    tt("kw mask", "pm", pm, T.kw[:, 0:192], T.mask[:, 0:192], A.min)
+    scan("pres ones", "cum", cum, pres, T.ones[:], 0.0, A.add, A.mult)
     for a, b, n, c in ((64, 0, 64, 0), (32, 0, 32, 1), (96, 64, 32, 1), (64, 32, 32, 2), (96, 0, 32, 2)):
         ac("cum bt3", "bx%d%d" % (a, c), T.bt3[a:a + n, c:c + 1], g1[b:b + n, 383:384])
+    for o in range(O):
+        for b in range(2):
+            ac("ps%d" % (2 * b + o), "res%d%d" % (o, b), T.res[:, 592 * o + 1 + 192 * b:592 * o + 193 + 192 * b], T.ps[:, 512 * (2 * b + o):512 * (2 * b + o) + 192])
     tt("pm cum", "mmm", mk, pm, cum, A.mult)
     scan("mmm seg", "mf", mf, T.seg[:, 0:192], mk, 0.0, A.mult, A.add)
     E("v", "bt3 bx640 bx321 bx961 bx642 bx962", "base", lambda e: e.tensor_reduce(h[:, 48:49], T.bt3[:, 0:3], AxisListType.X, A.add))
@@ -433,19 +467,17 @@ def rank_program(g, core, T, topo):
     E("v", "pw o3 pk", "pw", lambda e: e.tensor_copy(T.pw[:].indirect(T.o3[:]), pk))
     tt("pw mask", "f3a", T.f3[:, 0:288], T.pw[:, 0:288], T.mask[:, 0:288], A.mult)
     scan("f3a seg", "f3", T.f3[:, 288:576], T.seg[:, 0:288], T.f3[:, 0:288], 0.0, A.mult, A.add)
-    f3v = T.f3[:, 303:576:16]
     mg = T.mg
-    ac("f3", "ga", mg[0:64, 0:18], T.f3[64:128, 303:576:16])
-    cp("f3", "gb", mg[64:128, 0:18], T.f3[0:64, 303:576:16])
-    tt("f3 ga gb", "gc", mg[:, 18:36], f3v, mg[:, 0:18], A.add)
+    ac("f3", "ga", mg[lower, 0:18], T.f3[upper, 303:576:16])
+    cp("f3", "gb", mg[upper, 0:18], T.f3[lower, 303:576:16])
+    tt("f3 ga gb", "gc", mg[:, 18:36], T.f3[:, 303:576:16], mg[:, 0:18], A.add)
     for q in range(N):
-        a, b = 32 * q, 32 * (q ^ 1)
-        (ac if q % 2 else cp)("gc", "gd%d" % q, mg[a:a + 32, 36:54], mg[b:b + 32, 18:36])
+        (ac if q % 2 else cp)("gc", "gd%d" % q, mg[Qd[q], 36:54], mg[Qd[q ^ 1], 18:36])
     tt("gc gd0 gd1 gd2 gd3", "pki", T.pki[:, 0:18], mg[:, 18:36], mg[:, 36:54], A.add)
     pki = T.pki[:, 0:18]
     ts("pki", "yli", T.pki[:, 18:36], pki, 10, None, A.arith_shift_right)
     cp("yli", "yl", T.yl[:], T.pki[:, 18:36])
-    cp("ps4", "res02", T.res[:, 385:577], T.ps[:, 512 * 4:512 * 4 + 192])
+    ac("ps4", "res02", T.res[:, 385:577], T.ps[:, 512 * 4:512 * 4 + 192])
     ac("ps5", "res12", T.res[:, 592 + 385:592 + 577], T.ps[:, 512 * 5:512 * 5 + 192])
     E("v", "resz0 res00 res01 res02 yl", "ys0", lambda e: e.tensor_copy(T.ysb[:, 0:M], T.res[:, 0:577].indirect(T.yl[:])))
     ac("resz1 res10 res11 res12 yl", "ys1", T.ysb[:, M:2 * M], T.res[:, 592:592 + 577].indirect(T.yl[:]))

@@ -1,46 +1,45 @@
 from concourse.bass import DstId, RemoteDMATransfer
-from concourse.mybir import dt, AluOpType as A, AxisListType, ActivationFunctionType as AF
+from concourse.mybir import dt, AluOpType as A, ActivationFunctionType as AF
 
 N, V, M, O = 4, 192, 288, 2
 C = 64
+Z0 = 8
+X0 = Z0 + 512
+X1 = X0 + 192
+H = 160
 F, I, U, B = "float32", "int32", "uint16", "bfloat16"
 Q8, S8 = "float8_e4m3fn_x4", "uint8"
 
 
-def _sb(w, d, p=128):
-    return ("sbuf", [p, w], d)
+def _sb(w, d):
+    return ("sbuf", [128, w], d)
 
 
 SCRATCH = {
-    "tba": _sb(1024, I), "tb": _sb(1024, I), "sb": _sb(24, I), "nv": _sb(24, F), "n1x": _sb(192, F), "nxi": _sb(64, I, 16), "nxf": _sb(64, F, 16),
-    "xs": _sb(2048, B), "ws": _sb(3072, B),
-    "QX": _sb(512, Q8), "SX": _sb(512, S8), "QW": _sb(704, Q8), "SW": _sb(704, S8), "WQ": _sb(768, Q8), "WS": _sb(768, S8),
+    "tba": _sb(1024, I), "tb": _sb(1032, F), "tbd": ("dram", [1, 1024], F), "sb": _sb(24, I), "nxi": _sb(64, I), "nxf": _sb(64, F), "nxt": _sb(64, F),
+    "xs": _sb(4 * X0, B), "ws": _sb(3072, B),
+    "QX": _sb(X0, Q8), "SX": _sb(X0, S8), "W1": _sb(X1 + 192, Q8), "P1": _sb(X1 + 192, S8), "W2": _sb(X1 + 192, Q8), "P2": _sb(X1 + 192, S8),
+    "WQ": _sb(768, Q8), "WS": _sb(768, S8),
     "Q1": _sb(192, Q8), "S1": _sb(192, S8), "Q3": _sb(192, Q8), "S3": _sb(192, S8), "Q4": _sb(192, Q8), "S4": _sb(192, S8),
-    "TE1": _sb(192, Q8), "TS1": _sb(192, S8), "TE0": _sb(192, Q8), "TS0": _sb(192, S8),
-    "QO": _sb(192, Q8), "SO": _sb(192, S8), "QN1": _sb(384, Q8), "SN1": _sb(384, S8), "QN2": _sb(384, Q8), "SN2": _sb(384, S8),
-    "QE2": _sb(192, Q8), "SE2": _sb(192, S8),
-    "j15": _sb(384, F), "pI": _sb(1, I), "c16": _sb(24, F),
-    "ones": _sb(192, F), "ident": _sb(1024, F), "mask": _sb(384, F), "seg": _sb(384, F), "maskb": _sb(32, F), "sg": _sb(204, F),
-    "ci": _sb(8, I), "cf": _sb(24, F), "i16": _sb(24, F), "tri": _sb(24, F), "trx": _sb(36, F),
-    "l0": _sb(96, I), "lx": _sb(36, U), "b1x": _sb(24, F),
-    "val1": _sb(192, F), "bif": _sb(192, F), "n1m": _sb(192, F), "n1s": _sb(192, F), "n1f": _sb(192, F), "t1": _sb(12, I),
-    "eqa": _sb(72, F), "sa": _sb(36, F), "ba": _sb(96, F), "bta": _sb(96, F), "ra": _sb(96, F), "pa": _sb(36, F),
-    "eqb": _sb(144, F), "sbb": _sb(72, F), "bb": _sb(96, F), "btb": _sb(96, F), "rb": _sb(96, F), "pb": _sb(72, F),
-    "xa": _sb(72, F), "xb": _sb(144, F), "sl": _sb(24, U),
-    "w1": _sb(384, F), "w2": _sb(576, F), "f1": _sb(384, F), "f2": _sb(384, F), "hg": _sb(24, F),
-    "R1": _sb(12, I), "RA": _sb(12, I), "R2": _sb(12, I), "TV": _sb(12, I), "stl": _sb(12, U),
-    "VO": _sb(12, I), "lo": _sb(36, I), "la": _sb(48, I), "of": _sb(24, U),
-    "n2m": _sb(384, F), "n2s": _sb(384, F), "tb2": _sb(1024, F), "lad": _sb(12, U), "lu": _sb(12, U),
-    "lub": _sb(24, F), "sk": _sb(12, F), "uf": _sb(192, F), "ad": _sb(192, F), "val2": _sb(192, F), "inv": _sb(24, F), "n2e": _sb(24, F), "t2": _sb(24, I),
-    "fa": _sb(36, I), "l34": _sb(24, U), "l56": _sb(48, U), "l56i": _sb(72, I),
-    "e0": _sb(96, F), "o1": _sb(12, U), "kw": _sb(576, F), "vk": _sb(576, F),
-    "ei": _sb(36, I), "l7": _sb(12, U), "ef": _sb(48, F), "oe2": _sb(12, U), "g1": _sb(1152, F), "bt3": _sb(4, F),
-    "hf": _sb(60, F), "o3": _sb(12, U), "pw": _sb(480, F), "f3": _sb(576, F), "mg": _sb(54, F), "pki": _sb(36, I), "yl": _sb(18, U),
-    "idi": _sb(54, I), "idt": _sb(64, F), "idx": _sb(64, F), "res": _sb(1184, F), "ysb": _sb(576, F),
-    "ps": ("psum", [128, 512 * 6], F),
+    "G0": _sb(288, Q8), "H0": _sb(288, S8), "G1": _sb(288, Q8), "H1": _sb(288, S8), "G2": _sb(288, Q8), "H2": _sb(288, S8),
+    "j15": _sb(192, F), "pI": _sb(1, I), "c16": _sb(12, F), "ident": _sb(1104, F), "mask": _sb(192, F), "seg": _sb(192, F), "maskb": _sb(32, F),
+    "maskc": _sb(32, F), "sg": _sb(144, F), "ci": _sb(4, I), "cf": _sb(24, F), "i16": _sb(12, F), "tri": _sb(12, F), "park": _sb(12, F), "K2": _sb(12, F),
+    "l0": _sb(84, I), "lx": _sb(24, U), "b2f": _sb(12, F), "stf": _sb(12, F),
+    "val1": _sb(192, F), "n1m": _sb(192, F), "n1s": _sb(192, F), "t1": _sb(12, I), "E1x": _sb(12, F), "E1": _sb(12, F), "M1": _sb(12, U), "A1": _sb(36, U),
+    "MP": _sb(12, B), "AP": _sb(36, B),
+    "eqa": _sb(72, F), "sa": _sb(36, F), "ba": _sb(96, F), "bta": _sb(96, F), "ra": _sb(96, F), "pa": _sb(36, F), "xa": _sb(72, F),
+    "eqb": _sb(72, F), "sc": _sb(36, F), "bb": _sb(96, F), "btb": _sb(96, F), "rb": _sb(96, F), "pb": _sb(36, F), "xb": _sb(72, F), "g9": _sb(18, F),
+    "sl": _sb(36, U), "w1": _sb(384, F), "w2": _sb(384, F), "pw": _sb(480, F), "f1": _sb(384, F), "f2": _sb(384, F), "f3": _sb(288, F),
+    "stl": _sb(12, U), "off": _sb(12, U), "n2m": _sb(192, F), "n2s": _sb(192, F), "t2": _sb(12, I), "c1i": _sb(12, I), "c1u": _sb(12, U), "c1o": _sb(12, F),
+    "L0f": _sb(12, F), "L0e": _sb(12, F), "L0u": _sb(12, U), "SBm": _sb(12, F), "n2k": _sb(12, F), "M2": _sb(12, F), "A2": _sb(36, F), "uf1": _sb(192, F), "val2": _sb(192, F),
+    "hg": _sb(36, F), "fa": _sb(48, I), "l34": _sb(24, U),
+    "Zf": _sb(36, F), "Zi": _sb(48, I), "zl": _sb(24, U), "ze": _sb(24, F), "uf2": _sb(192, F), "val3": _sb(192, F), "pr": _sb(12, F), "PZ": _sb(32, F),
+    "tc": _sb(224, F), "g3": _sb(6, F), "pz": _sb(24, F), "hm": _sb(18, F), "F32": _sb(32, F), "TF": _sb(32, F), "hx": _sb(32, F), "DD": _sb(64, F), "LT": _sb(64, F),
+    "li": _sb(108, I), "LU": _sb(36, U), "HU": _sb(18, U), "idi": _sb(72, I), "idt": _sb(64, F), "idx": _sb(64, F), "ysb": _sb(576, F),
+    "ps": ("psum", [128, 2048], F),
 }
-DMAS = ["dnx", "dst", "dx", "dw0", "dw1", "dq", "dp", "dni", "dz", "df", "dy0", "dy1", "di0", "di1"]
-HOPS = ("ra", "qa", "sa", "rb", "qb", "sb", "qc", "sc")
+DMAS = ["dnx", "dst", "dx", "dw0", "dw1", "dni", "dz", "dtd", "dtr", "dtq", "dq1", "dq2", "dy0", "dy1", "di0", "di1"]
+HOPS = ("ma", "mp", "qa", "sa", "mz", "qb", "sb", "qc", "sc")
 SEMAPHORES = ["v", "s", "t", "g", "loc"] + DMAS + [n + str(k) for n in HOPS for k in range(N - 1)]
 
 
@@ -67,12 +66,41 @@ def rank_program(g, core, T, topo):
     if rank is None:
         return
     cores = list(T.cores)
-    oth = [d for d in range(N) if d != rank]
+    oth = [rank ^ (k + 1) for k in range(N - 1)]
     eng = {"v": g.vector, "s": g.scalar, "t": g.tensor, "g": g, "y": g.sync}
     cnt = {q: 0 for q in eng}
-    seen, last, readers, dsum, loc = {}, {}, {}, {}, [0]
+    seen, writers, readers, dsum, pend, loc = {}, {}, {}, {}, {}, [0]
     Qd = [slice(32 * q, 32 * q + 32) for q in range(4)]
     lower, upper, every = slice(0, 64), slice(64, 128), slice(0, 128)
+    QM = Qd[rank]
+
+    def R(name, a=0, b=None, P=every, st=1):
+        return (name, P.start, P.stop, a, SCRATCH[name][1][1] if b is None else b, st)
+
+    def ind(win, off):
+        return ("ind", win, off)
+
+    def ap(x):
+        if x[0] == "ind":
+            return ap(x[1]).indirect(ap(x[2]))
+        if x[5] == 1:
+            return T[x[0]][x[1]:x[2], x[3]:x[4]]
+        return T[x[0]][x[1]:x[2], x[3]:x[4]:x[5]]
+
+    def flat(xs):
+        out = []
+        for x in xs:
+            if isinstance(x, tuple):
+                out += flat(x[1:]) if x[0] == "ind" else [x]
+        return out
+
+    def meet(x, y):
+        if x[1] >= y[2] or y[1] >= x[2] or x[3] >= y[4] or y[3] >= x[4]:
+            return False
+        return not (x[5] == y[5] and (x[3] - y[3]) % x[5])
+
+    def inside(x, y):
+        return y[1] <= x[1] and x[2] <= y[2] and y[3] <= x[3] and x[4] <= y[4] and (y[5] == 1 or y == x)
 
     def wait(q, toks):
         need = {}
@@ -83,52 +111,39 @@ def rank_program(g, core, T, topo):
             eng[q].wait_ge(T.sem[sem], need[sem])
             seen[(q, sem)] = need[sem]
 
-    def deps(q, r, w):
+    def deps(q, rs, ws):
         toks = []
-        for k in list(r) + list(w):
-            toks += last.get(k, [])
-        for k in w:
-            toks += [t for t in readers.get(k, []) if t[0] != q]
+        for x in rs + ws:
+            toks += [t for y, t in writers.get(x[0], []) if meet(x, y)]
+        for x in ws:
+            toks += [t for y, t in readers.get(x[0], []) if meet(x, y) and t[0] != q]
         wait(q, toks)
 
-    def done(tok, r, w):
-        for k in r:
-            readers.setdefault(k, []).append(tok)
-        for k in w:
-            last[k] = [tok]
-            readers[k] = []
+    def done(tok, rs, ws):
+        for x in rs:
+            readers.setdefault(x[0], []).append((x, tok))
+        for x in ws:
+            writers[x[0]] = [e for e in writers.get(x[0], []) if not inside(e[0], x)] + [(x, tok)]
+            readers[x[0]] = [e for e in readers.get(x[0], []) if not inside(e[0], x)]
 
-    def E(q, r, w, fn):
-        r, w = r.split(), w.split()
-        deps(q, r, w)
+    def E(q, rs, ws, fn):
+        rs, ws = flat(rs), flat(ws)
+        deps(q, rs, ws)
         fn(eng[q]).then_inc(T.sem[q], 1)
         cnt[q] += 1
-        done((q, cnt[q]), r, w)
+        done((q, cnt[q]), rs, ws)
 
-    def D(q, out, in_, sem, r="", w="", fin=True):
-        deps(q, r.split(), w.split())
-        eng[q].dma_start(out, in_).then_inc(T.sem[sem], 16)
+    def D(q, out, in_, sem, fin=True, outap=None, inap=None):
+        rs, ws = flat([in_]), flat([out])
+        deps(q, rs, ws)
+        eng[q].dma_start(ap(out) if outap is None else outap, ap(in_) if inap is None else inap).then_inc(T.sem[sem], 16)
         dsum[sem] = dsum.get(sem, 0) + 16
+        pend.setdefault(sem, []).append((rs, ws))
         if fin:
-            done((sem, dsum[sem]), r.split(), w.split())
+            for rs, ws in pend.pop(sem):
+                done((sem, dsum[sem]), rs, ws)
 
     mine = plan(topo, core, cores)
-
-    def send(sem, r, src, dst):
-        deps("g", r.split(), [])
-        tr = []
-        for i, d in enumerate(oth):
-            k = [x for x in range(N) if x != d].index(rank)
-            rid, pid, _ = topo.addr(cores[d])
-            es = mine[cores[d]]
-            loc[0] += len(es)
-            tr.append(RemoteDMATransfer(dst_ids=[DstId(rid=rid, pnc=pid)], dma_engine_mask=sum(1 << e for e in es),
-                                        remote_sem=T.sem[sem + str(k)], srcs=[src(i)], dsts=[dst(k)]))
-        g.remote_dma_fused(tr, local_sem=T.sem.loc)
-
-    arrivals = {h: [(h + str(k), len(plan(topo, cores[d], cores)[core])) for k, d in enumerate(oth)] for h in HOPS}
-    for h, key in zip(HOPS, ("RA", "QWa", "SWa", "TV", "TE1", "TS1", "TE0", "TS0")):
-        last[key] = arrivals[h]
 
     def u8(v):
         return v.bitcast(dt.uint8)
@@ -136,361 +151,444 @@ def rank_program(g, core, T, topo):
     def u32(v):
         return v.bitcast(dt.uint32)
 
-    def ts(r, w, out, in0, s1, s2, o1, o2=None):
+    land = {"ma": ("A1", 0, 12), "mp": ("AP", 0, 12), "qa": ("W1", X0, C), "sa": ("P1", X0, C), "mz": ("A2", 0, 12),
+            "qb": ("W1", X1, C), "sb": ("P1", X1, C), "qc": ("W2", X1, C), "sc": ("P2", X1, C)}
+
+    def landed(h, k):
+        n, a, w = land[h]
+        return R(n, a + w * k, a + w * k + w)
+
+    def send(h, src, codes=False):
+        deps("g", flat([src(k) for k in range(N - 1)]), [])
+        tr = []
+        for k, d in enumerate(oth):
+            rid, pid, _ = topo.addr(cores[d])
+            es = mine[cores[d]]
+            loc[0] += len(es)
+            s, t = ap(src(k)), ap(landed(h, k))
+            tr.append(RemoteDMATransfer(dst_ids=[DstId(rid=rid, pnc=pid)], dma_engine_mask=sum(1 << e for e in es),
+                                        remote_sem=T.sem[h + str(k)], srcs=[u8(s) if codes else s], dsts=[u8(t) if codes else t]))
+        g.remote_dma_fused(tr, local_sem=T.sem.loc)
+
+    def block(n):
+        return lambda k: R(n, C * k, C * k + C)
+
+    arrivals = []
+    for h in HOPS:
+        for k, d in enumerate(oth):
+            tok = (h + str(k), len(plan(topo, cores[d], cores)[core]))
+            arrivals.append(tok)
+            writers.setdefault(land[h][0], []).append((landed(h, k), tok))
+
+    def sc_(x):
+        return ap(x) if isinstance(x, tuple) else x
+
+    def ts(out, in0, s1, s2, o1, o2=None):
         if o2 is None:
-            E("v", r, w, lambda e: e.tensor_scalar(out, in0, s1, None, o1))
+            E("v", [in0, s1], [out], lambda e: e.tensor_scalar(ap(out), ap(in0), sc_(s1), None, o1))
         else:
-            E("v", r, w, lambda e: e.tensor_scalar(out, in0, s1, s2, o1, o2))
+            E("v", [in0, s1, s2], [out], lambda e: e.tensor_scalar(ap(out), ap(in0), sc_(s1), sc_(s2), o1, o2))
 
-    def tt(r, w, out, a, b, op):
-        E("v", r, w, lambda e: e.tensor_tensor(out, a, b, op))
+    def tt(out, a, b, op):
+        E("v", [a, b], [out], lambda e: e.tensor_tensor(ap(out), ap(a), ap(b), op))
 
-    def cp(r, w, out, in_):
-        E("v", r, w, lambda e: e.tensor_copy(out, in_))
+    def cp(out, in_):
+        E("v", [in_], [out], lambda e: e.tensor_copy(ap(out), ap(in_)))
 
-    def ac(r, w, out, in_, scale=None, bias=None, fn=None):
-        fn = fn or (AF.Copy if bias is None else AF.Identity)
+    def scatter(win, off, val):
+        E("v", [off, val], [win], lambda e: e.tensor_copy(ap(win).indirect(ap(off)), ap(val)))
+
+    def fill(out, c):
+        E("v", [], [out], lambda e: e.memset(ap(out), c))
+
+    def scan(out, d0, d1):
+        E("v", [d0, d1], [out], lambda e: e.tensor_tensor_scan(ap(out), ap(d0), ap(d1), 0.0, A.mult, A.add))
+
+    def turn(out, in_):
+        E("v", [in_], [out], lambda e: e.transpose(ap(out), ap(in_)))
+
+    def ac(out, in_, scale=None, bias=None, fn=None):
+        f = fn or (AF.Copy if bias is None else AF.Identity)
         kw = {}
         if scale is not None:
-            kw["scale"] = scale
+            kw["scale"] = sc_(scale)
         if bias is not None:
-            kw["bias"] = bias
-        E("s", r, w, lambda e: e.activation(out, in_, fn, **kw))
+            kw["bias"] = sc_(bias)
+        E("s", [in_, scale, bias], [out], lambda e: e.activation(ap(out), ap(in_), f, **kw))
 
-    def co(w, ap, P, n, c):
-        ac("ident0", w, ap, T.ident[P, 0:n], scale=0.0, bias=c)
+    def co(out, c):
+        n = out[4] - out[3]
+        ac(out, R("j15" if n <= 192 else "ident", 0, n, slice(out[1], out[2])), scale=0.0, bias=c)
 
-    def scan(r, w, out, d0, d1, init, o0, o1):
-        E("v", r, w, lambda e: e.tensor_tensor_scan(out, d0, d1, init, o0, o1))
-
-    def iota(w, ap, pattern, cm=0, flag=True):
+    def iota(out, pattern, cm=0, flag=True):
         if flag:
-            E("g", "", w, lambda e: e.iota(ap, pattern, 0, cm, allow_small_or_imprecise_dtypes=True))
+            E("g", [], [out], lambda e: e.iota(ap(out), pattern, 0, cm, allow_small_or_imprecise_dtypes=True))
         else:
-            E("g", "", w, lambda e: e.iota(ap, pattern, 0, cm))
+            E("g", [], [out], lambda e: e.iota(ap(out), pattern, 0, cm))
 
-    def pick(off, offk, qw, sw, qk, sk, qo, so, qok, sok):
-        E("v", offk + " " + qk, qok, lambda e: e.tensor_copy(u32(qo), u32(qw).indirect(off)))
-        E("s", offk + " " + sk, sok, lambda e: e.activation(so, sw.indirect(off), AF.Copy))
+    def pickq(out, win, off):
+        E("v", [win, off], [out], lambda e: e.tensor_copy(u32(ap(out)), u32(ap(win)).indirect(ap(off))))
 
-    D("y", T.nxi[:], T.nx[:], "dni", w="nxi")
+    def picks(out, win, off):
+        E("s", [win, off], [out], lambda e: e.activation(ap(out), ap(win).indirect(ap(off)), AF.Copy))
+
+    def quant(q, s, in_):
+        E("v", [in_], [q, s], lambda e: e.quantize_mx(ap(q), ap(s), ap(in_)))
+
+    def col(i, P=every):
+        return R("cf", i, i + 1, P)
+
+    def ends(name, P=every, n=12, a=0):
+        return R(name, a + 15, a + 16 * n, P, 16)
+
     for i in range(2):
-        D("y", T.sb[16 * i:16 * i + 16, 0:12], T.st[:], "dst", w="sb", fin=False)
-        D("s", T.sb[16 * i:16 * i + 16, 12:24], T.bt[:], "dst", w="sb", fin=(i == 1))
+        D("y", R("sb", 0, 12, slice(16 * i, 16 * i + 16)), None, "dst", False, inap=T.st[:])
+        D("s", R("sb", 12, 24, slice(16 * i, 16 * i + 16)), None, "dst", i == 1, inap=T.bt[:])
     for i in range(16):
-        D("y", T.tba[i:i + 1, :], T.nx[:], "dnx", w="tba", fin=False)
-        D("s", T.tba[16 + i:17 + i, :], T.nx[:], "dnx", w="tba", fin=(i == 15))
-    E("v", "", "tbz", lambda e: e.memset(T.tba[Qd[1]], 0))
-    D("y", T.tba[Qd[2]], T.tba[Qd[1]], "dz", r="tbz", w="tbz1", fin=False)
-    D("y", T.tba[Qd[3]], T.tba[Qd[1]], "dz", r="tbz", w="tbz1 tbz2")
-    D("y", T.xs[:], T.x[:], "dx", w="xs")
+        D("y", R("tba", P=slice(i, i + 1)), None, "dnx", False, inap=T.nx[:])
+        D("s", R("tba", P=slice(16 + i, 17 + i)), None, "dnx", i == 15, inap=T.nx[:])
+    iota(R("pI"), [[1, 1]], 1, False)
+    fill(R("tba", P=Qd[1]), 0)
+    D("y", R("tba", P=Qd[2]), R("tba", P=Qd[1]), "dz", False)
+    D("y", R("tba", P=Qd[3]), R("tba", P=Qd[1]), "dz")
+    for i in range(2):
+        D("y", R("nxi", P=slice(16 * i, 16 * i + 16)), None, "dni", i == 1, inap=T.nx[:])
+    D("y", R("xs", 4 * Z0), None, "dx", inap=T.x[:])
+    iota(R("c16"), [[16, 12]])
+    iota(R("j15"), [[0, 12], [1, 16]])
+    iota(R("sg", 0, 36), [[0, 3], [1, 12]])
+    iota(R("sg", 36, 132), [[0, 3], [1, 32]])
+    iota(R("sg", 132, 141), [[0, 3], [1, 3]])
+    iota(R("ident", 0, 256), [[1, 256]])
+    idn = R("ident")
 
-    iota("pI", T.pI[:], [[1, 1]], 1, False)
-    iota("c16", T.c16[:], [[16, 24]])
-    iota("j15", T.j15[:], [[0, 24], [1, 16]])
-    iota("ident0", T.ident[:, 0:256], [[1, 256]])
-    iota("sg0", T.sg[:, 0:36], [[0, 3], [1, 12]])
-    iota("sg1", T.sg[:, 36:108], [[0, 3], [1, 24]])
-    iota("sg2", T.sg[:, 108:204], [[0, 3], [1, 32]])
-    E("g", "tba", "tb", lambda e: e.partition_broadcast(T.tb[:], T.tba[0:1, :], 128))
-    ac("j15", "seg", T.seg[:], T.j15[:], fn=AF.Sign)
-    ac("sg0 sg1 sg2", "sg", T.sg[:], T.sg[:], fn=AF.Sign)
-    ac("ident0", "ident1", T.ident[:, 256:512], T.ident[:, 0:256], bias=256.0)
-    ac("ident0 ident1", "ident", T.ident[:, 512:1024], T.ident[:, 0:512], bias=512.0)
-    ac("ident0", "w1", T.w1[:, 0:256], T.ident[:, 0:256], scale=0.0)
-    ac("ident0 w1", "w1", T.w1[:, 256:384], T.ident[:, 0:128], scale=0.0)
-    ac("ident0 ident", "w2", T.w2[:], T.ident[:, 0:576], scale=0.0)
-    ac("ident0", "tb2A", T.tb2[lower], T.ident[lower], scale=512.0)
+    r15, p31, qf, ev, od = [col(i) for i in range(5)]
+    ts(R("ci", 0, 1), R("pI"), 15, None, A.bitwise_and)
+    ts(R("ci", 1, 2), R("pI"), 31, None, A.bitwise_and)
+    ts(R("ci", 2, 3), R("pI"), 5, None, A.arith_shift_right)
+    cp(R("cf", 0, 3), R("ci", 0, 3))
+    sti, bti = R("sb", 0, 12), R("sb", 12, 24)
+    cp(R("sb", P=Qd[1]), R("sb", P=Qd[0]))
+    cp(R("sb", P=upper), R("sb", P=lower))
 
-    E("v", "", "ones", lambda e: e.memset(T.ones[:], 1.0))
-    ts("pI", "ci0", T.ci[:, 0:1], T.pI[:], 15, None, A.bitwise_and)
-    ts("pI", "ci1", T.ci[:, 1:2], T.pI[:], 31, None, A.bitwise_and)
-    ts("pI", "ci2", T.ci[:, 2:3], T.pI[:], 5, None, A.arith_shift_right)
-    cp("ci0 ci1 ci2", "cf", T.cf[:, 0:3], T.ci[:, 0:3])
-    r15, p31, qf = T.cf[:, 0:1], T.cf[:, 1:2], T.cf[:, 2:3]
-    ts("c16 cf", "i16", T.i16[:], T.c16[:], r15, 0.0, A.add, A.add)
-    cp("nxi", "nxf", T.nxf[:], T.nxi[:])
-    for i in range(32):
-        D("y", T.tb2[64 + i:65 + i, :], T.nxf[:], "df", r="nxf", w="tb2B", fin=(i == 31))
-    D("y", T.ws[:, 0:2048], T.w[:, 0:2048], "dw0", w="ws0")
-    D("y", T.ws[:, 2048:3072], T.w[:, 2048:3072], "dw1", w="ws1")
-    ts("j15 cf", "mask", T.mask[:], T.j15[:], r15, None, A.is_equal)
-    ts("j15 cf", "maskb", T.maskb[:], T.j15[:, 0:32], p31, None, A.is_gt)
+    def l0(i):
+        return R("l0", 12 * i, 12 * i + 12)
+    off0, stu = R("lx", 0, 12), R("lx", 12, 24)
+    ts(l0(0), bti, 1, None, A.bitwise_and)
+    ts(l0(1), sti, 2.0, None, A.mult)
+    ts(l0(6), bti, 1, None, A.arith_shift_right)
+    tt(l0(2), l0(1), l0(0), A.add)
+    ts(R("mask"), R("j15"), r15, None, A.is_equal)
+    ts(l0(3), l0(2), 4, None, A.arith_shift_right)
+    ts(l0(4), l0(2), 64.0, None, A.mult)
+    cp(stu, sti)
+    ts(l0(5), l0(3), -1023.0, None, A.mult)
+    cp(R("b2f"), l0(6))
+    tt(l0(2), l0(4), l0(5), A.add)
+    cp(R("stf"), sti)
+    cp(off0, l0(2))
 
-    L = T.l0
-    sti, bti = T.sb[:, 0:12], T.sb[:, 12:24]
-    off0, stu, lbi = [T.lx[:, 12 * i:12 * i + 12] for i in range(3)]
-    b1x = T.b1x[:, 0:12]
-    cp("sb", "sb1", T.sb[Qd[1]], T.sb[Qd[0]])
-    cp("sb sb1", "sb2", T.sb[upper], T.sb[lower])
-    ts("sb sb1 sb2", "u1", L[:, 0:12], sti, 7, None, A.bitwise_and)
-    ts("sb", "u2", L[:, 12:24], sti, 3, None, A.arith_shift_right)
-    cp("sb", "stu", stu, sti)
-    ts("sb", "u3", L[:, 24:36], bti, 1, None, A.bitwise_and)
-    ts("sb", "u4", L[:, 36:48], bti, 1, None, A.arith_shift_right)
-    ts("u1", "u5", L[:, 48:60], L[:, 0:12], 128.0, None, A.mult)
-    ts("u3", "u6", L[:, 60:72], L[:, 24:36], 64.0, None, A.mult)
-    ts("u4", "b1x", b1x, L[:, 36:48], 256.0, None, A.mult)
-    tt("u5 u2", "u7", L[:, 72:84], L[:, 48:60], L[:, 12:24], A.add)
-    tt("b1x i16", "lbf", T.b1x[:, 12:24], b1x, T.i16[:, 0:12], A.add)
-    tt("u7 u6", "u8", L[:, 84:96], L[:, 72:84], L[:, 60:72], A.add)
-    cp("lbf", "lbi", lbi, T.b1x[:, 12:24])
-    cp("u8", "off0", off0, L[:, 84:96])
-    ac("ident stu", "val1A", T.val1[:], T.ident[:].indirect(stu))
-    ac("ident lbi", "bif", T.bif[:], T.ident[:].indirect(lbi), scale=1.0 / 512, bias=2048.0)
+    ac(R("seg"), R("j15"), fn=AF.Sign)
+    ac(R("sg", 0, 141), R("sg", 0, 141), fn=AF.Sign)
+    ac(R("i16"), R("c16", 0, 12), bias=r15)
+    ac(R("tri"), R("i16"), bias=192.0)
     for d in range(3):
-        ts("cf", "ka%d" % d, T.cf[:, 6 + d:7 + d], r15, 191.0, 15.0 - 192 + C * d, A.mult, A.add)
-    ts("c16 cf", "tri", T.tri[:], T.c16[:], r15, 192.0, A.add, A.add)
+        ac(col(8 + d), r15, scale=191.0, bias=15.0 - 192 + C * d)
+    ac(R("ident", 256, 512), R("ident", 0, 256), bias=256.0)
+    ac(R("ident", 512, 1024), R("ident", 0, 512), bias=512.0)
+    ac(R("ident", 1024, 1104), R("ident", 0, 80), bias=1024.0)
 
-    def classes(nc, t, tk, eqb, sbuf, bbuf, btbuf, rbuf, pbuf, xbuf, kc, p, s0):
-        kk = ["ka%d", "kb%d"][nc == 24]
-        w = 3 * nc
+    tt(R("n1m"), ind(R("tba"), off0), R("mask"), A.mult)
+    cp(R("nxf", P=Qd[0]), R("nxi", P=Qd[0]))
+    fill(R("M1"), 0)
+    scan(R("n1s"), R("seg"), R("n1m"))
+    turn(R("nxt", P=Qd[0]), R("nxf", P=Qd[0]))
+    n1v = ends("n1s", Qd[0])
+    ts(R("E1x", P=QM), n1v, 2.0, None, A.mult)
+    for q in range(2):
+        ts(R("t1", P=Qd[q]), n1v, 1.0 / 512, -255.5 / 512, A.mult, A.add)
+    tt(R("E1", P=QM), R("E1x", P=QM), R("b2f", P=QM), A.add)
+    ts(R("maskb"), R("j15", 0, 32), p31, None, A.is_gt)
+    for q in range(2, 4):
+        ts(R("t1", P=Qd[q]), n1v, 1.0 / 512, -255.5 / 512, A.mult, A.add)
+    cp(R("M1", P=QM), R("E1", P=QM))
+    send("ma", lambda k: R("M1"))
+    co(R("tb", 0, 4), 4096.0)
+    co(R("tb", 1028, 1032), 4096.0)
+    for i in range(2):
+        D("y", ("tbd", 0, 1, 512 * i, 512 * i + 512, 1), R("nxt", 32 * i, 32 * i + 16, Qd[0]), "dtd", i == 1)
+    for i in range(16):
+        D("y", R("tb", 4, 1028, slice(i, i + 1)), ("tbd", 0, 1, 0, 1024, 1), "dtr", i == 15)
+    for i in range(1, 8):
+        D("y", R("tb", 4, 1028, slice(16 * i, 16 * i + 16)), R("tb", 4, 1028, slice(0, 16)), "dtq", i == 7)
+    D("y", R("ws", 0, 2048), None, "dw0", inap=T.w[:, 0:2048])
+    D("y", R("ws", 2048, 3072), None, "dw1", inap=T.w[:, 2048:3072])
+
+    ac(R("val1"), ind(idn, stu), bias=float(Z0))
+    co(R("w1", 0, 192), 0.0)
+
+    def classes(t, eq, s, bb, bt, rr, pp, xx, kc, cross, fillers):
+        def part(name, j, n=12):
+            return R(name, n * j, n * j + n)
+
+        def gap():
+            if fillers:
+                fillers.pop(0)()
+        gap()
         for j, d in enumerate(oth):
-            ts(tk, p + "m%d" % j, eqb[:, nc * j:nc * j + nc], t, float(d), -16.0, A.is_equal, A.add)
-        scan(p + "m0 " + p + "m1 " + p + "m2 sg", p + "s", sbuf[:], T.sg[:, s0:s0 + w], eqb[:, 0:w], 0.0, A.mult, A.add)
+            ts(part(eq, j), t, float(d), -16.0, A.is_equal, A.add)
+        gap()
+        scan(R(s), R("sg", 0, 36), R(eq, 0, 36))
+        ac(R(eq, 36, 72), R(eq, 0, 36), bias=16.0)
+        if cross:
+            for a, b, n, c, v in ((64, 32, 32, 2, 0), (32, 0, 32, 1, 0), (64, 0, 64, 0, 1), (96, 64, 32, 1, 1), (96, 0, 32, 2, 1)):
+                o, i_ = R("g9", c, 9, slice(a, a + n), 3), R(s, 11, 36, slice(b, b + n), 12)
+                if v:
+                    ts(o, i_, 0.5, None, A.mult)
+                else:
+                    ac(o, i_, scale=0.5)
+            gap()
+            scan(R("g9", 9, 18), R("sg", 132, 141), R("g9", 0, 9))
+        gap()
         for j in range(3):
-            ts(p + "s maskb", p + "b%d" % j, bbuf[:, 32 * j:32 * j + 32], T.maskb[:], sbuf[:, nc * j + nc - 1:nc * j + nc], None, A.mult)
-        E("v", " ".join(p + "b%d" % j for j in range(3)), p + "t", lambda e: e.transpose(btbuf[:], bbuf[:]))
-        ts(p + "m0", p + "e", eqb[:, w:2 * w], eqb[:, 0:w], 16.0, None, A.add)
-        scan(p + "t sg", p + "r", rbuf[:], T.sg[:, 108:204], btbuf[:], 0.0, A.mult, A.add)
+            last = R(s, 12 * j + 11, 12 * j + 12)
+            if cross:
+                ts(part(bb, j, 32), R("maskb"), last, R("g9", 11 + 3 * j, 12 + 3 * j), A.mult, A.add)
+            else:
+                ts(part(bb, j, 32), R("maskb"), last, None, A.mult)
+        gap()
+        turn(R(bt), R(bb))
+        gap()
+        scan(R(rr), R("sg", 36, 132), R(bt))
+        gap()
         for j in range(3):
-            ts(p + "s " + p + "r " + kk % j, p + "p%d" % j, pbuf[:, nc * j:nc * j + nc], sbuf[:, nc * j:nc * j + nc], rbuf[:, 32 * j + 31:32 * j + 32], T.cf[:, kc + j:kc + j + 1], A.add, A.add)
-        tt(" ".join(p + "p%d" % j for j in range(3)) + " " + p + "e", p + "x", xbuf[:, 0:w], pbuf[:], eqb[:, w:2 * w], A.mult)
-        tt(p + "x tri", p + "y1", xbuf[:, 4 * nc:5 * nc], xbuf[:, 2 * nc:3 * nc], T.tri[:, 0:nc], A.add)
-        tt(p + "x", p + "y0", xbuf[:, 3 * nc:4 * nc], xbuf[:, 0:nc], xbuf[:, nc:2 * nc], A.add)
-        tt(p + "y0 " + p + "y1", p + "z", xbuf[:, 5 * nc:6 * nc], xbuf[:, 3 * nc:4 * nc], xbuf[:, 4 * nc:5 * nc], A.add)
+            ts(part(pp, j), part(s, j), R(rr, 32 * j + 31, 32 * j + 32), col(kc + j), A.add, A.add)
+        gap()
+        tt(R(xx, 0, 36), R(pp), R(eq, 36, 72), A.mult)
+        gap()
+        tt(part(xx, 4), part(xx, 2), R("tri"), A.add)
+        tt(part(xx, 3), part(xx, 0), part(xx, 1), A.add)
+        gap()
+        tt(part(xx, 5), part(xx, 3), part(xx, 4), A.add)
+        return part(xx, 5)
 
-    tt("tba tbz tbz1 tbz2 off0 mask", "n1m", T.n1m[:], T.tba[:].indirect(off0), T.mask[:, 0:192], A.mult)
-    scan("n1m seg", "n1s", T.n1s[:], T.seg[:, 0:192], T.n1m[:], 0.0, A.mult, A.add)
-    cp("tba off0", "n1f", T.n1f[:], T.tba[:].indirect(off0))
-    n1v = T.n1s[0:32, 15:192:16]
-    for q in range(4):
-        ts("n1s", "t1%d" % q, T.t1[Qd[q]], n1v, 1.0 / 512, -255.5 / 512, A.mult, A.add)
-    ac("n1f", "n1x2", T.n1x[Qd[2]], T.n1f[Qd[0]])
-    ac("n1f", "n1x3", T.n1x[Qd[3]], T.n1f[Qd[0]])
-    for q in range(4):
-        ac("n1s", "nv%d" % q, T.nv[Qd[q], 0:12], n1v)
-    co("scA", T.cf[lower, 12:13], lower, 1, 1.0)
-    co("scB", T.cf[upper, 12:13], upper, 1, 2048.0)
-    co("bcA", T.cf[lower, 13:14], lower, 1, 0.0)
-    co("bcB", T.cf[upper, 13:14], upper, 1, 2097152.0)
-    ac("i16", "lub", T.lub[:, 0:12], T.i16[:, 0:12], bias=256.0 * rank)
-    for k, d in enumerate(oth):
-        co("sk%d" % k, T.sk[:, 4 * k:4 * k + 4], every, 4, 256.0 * d)
+    def zeros():
+        fill(R("xs", 0, 4 * Z0), 0.0)
+        ts(ev, p31, 16.0, None, A.is_lt)
+
+    def own():
+        ts(R("off", P=QM), R("E1", P=QM), 4.0 - 1024 * rank, 1028.0, A.add, A.min)
+
+    def qx(i):
+        return lambda: quant(R("QX", 130 * i, 130 * i + 130), R("SX", 130 * i, 130 * i + 130), R("xs", 520 * i, 520 * i + 520))
+
+    def wq(i):
+        return lambda: quant(R("WQ", 128 * i, 128 * i + 128), R("WS", 128 * i, 128 * i + 128), R("ws", 512 * i, 512 * i + 512))
+
+    z1 = classes(R("t1"), "eqa", "sa", "ba", "bta", "ra", "pa", "xa", 8, False,
+                 [zeros, own, lambda: ts(R("maskc"), R("ident", 0, 32), p31, None, A.is_gt)] + [qx(i) for i in range(4)])
+    slot1 = R("sl", 0, 12)
+    cp(slot1, z1)
+    ac(R("MP"), z1)
+    send("mp", lambda k: R("MP"))
+    ac(od, ev, scale=-1.0, bias=1.0)
+    ac(col(6), ev, scale=float(Z0))
+    ac(col(7), qf, scale=262144.0)
+    ac(col(15), col(7), scale=od)
     for d in range(3):
-        ac("cf", "kb%d" % d, T.cf[:, 9 + d:10 + d], r15, scale=383.0, bias=15.0 - 192 + C * d)
-    ac("cf", "cf3", T.cf[:, 3:4], qf, bias=4.0)
-    ac("cf", "cf4", T.cf[:, 4:5], qf, scale=256.0)
-    for i, add in enumerate((288.0, 289.0, 384.0)):
-        ac("i16", "trx%d" % i, T.trx[:, 12 * i:12 * i + 12], T.i16[:, 0:12], bias=add)
-    trp, trp1, trk = [T.trx[:, 12 * i:12 * i + 12] for i in range(3)]
-    for q in range(N):
-        co("vb%d" % q, T.cf[Qd[q], 14:15], Qd[q], 1, 1024.0 * (1 if q == rank else 1 + V + C * oth.index(q)))
-    co("eq1", T.e0[:, 0:12], every, 12, 0.0)
-    co("i1", T.e0[:, 12:24], every, 12, 0.0)
-    co("bt3", T.bt3[:], every, 4, 0.0)
-    co("idt", T.idt[:], every, 64, 0.0)
-    co("resz0", T.res[:, 0:1], every, 1, 0.0)
-    co("resz1", T.res[:, 592:593], every, 1, 0.0)
+        ac(col(11 + d), qf, scale=3072.0, bias=col(8 + d))
+    ac(col(14), qf, scale=192.0, bias=-288.0)
+    ac(R("park"), R("i16"), bias=288.0)
+    ac(R("K2"), R("i16"), scale=od, bias=col(6))
+    co(R("g9", 0, 9), 0.0)
+    ac(R("L0f", P=QM), R("stf", P=QM), bias=float(Z0))
+    co(R("w2", 0, 192), 0.0)
 
-    classes(12, T.t1[:], "t10 t11 t12 t13", T.eqa, T.sa, T.ba, T.bta, T.ra, T.pa, T.xa, 6, "a", 0)
-    slot1 = T.sl[:, 0:12]
-    cp("az", "aslot", slot1, T.xa[:, 60:72])
-    tt("n1x2 n1x3 bif val1A", "val1B", T.val1[upper], T.n1x[upper], T.bif[upper], A.add)
-    E("v", "w1 aslot val1A val1B", "w1", lambda e: e.tensor_copy(T.w1[:].indirect(slot1), T.val1[:]))
-    tt("w1 mask", "f1a", T.f1[:, 0:192], T.w1[:, 0:192], T.mask[:, 0:192], A.mult)
-    scan("f1a seg", "f1", T.f1[:, 192:384], T.seg[:, 0:192], T.f1[:, 0:192], 0.0, A.mult, A.add)
-    lo_, hi_ = T.f1[lower, 207:384:16], T.f1[upper, 207:384:16]
-    ts("f1", "R1b", T.R1[upper], hi_, 512.0, None, A.mult)
-    ts("f1", "R1a", T.R1[lower], hi_, 512.0, None, A.mult)
-    cp("f1", "stla", T.stl[lower], lo_)
-    cp("f1", "stlb", T.stl[upper], lo_)
-    send("ra", "R1a R1b", lambda i: T.R1[:, 4 * i:4 * i + 4], lambda k: T.RA[:, 4 * k:4 * k + 4])
-    E("v", "xs", "QX SX", lambda e: e.quantize_mx(T.QX[:], T.SX[:], T.xs[:]))
-    pick(T.stl[:], "stla stlb", T.QX[:], T.SX[:], "QX", "SX", T.Q1[:], T.S1[:], "Q1", "S1")
-    send("qa", "Q1", lambda i: u8(T.Q1[:, C * i:C * i + C]), lambda k: u8(T.QW[:, 512 + C * k:512 + C * k + C]))
-    send("sa", "S1", lambda i: T.S1[:, C * i:C * i + C], lambda k: T.SW[:, 512 + C * k:512 + C * k + C])
-    D("y", u8(T.QW[:, 0:512]), u8(T.QX[:]), "dq", r="QX", w="QWo")
-    D("y", T.SW[:, 0:512], T.SX[:], "dp", r="SX", w="SWo")
-    iota("kw", T.kw[:], [[0, 576]])
-    iota("pw", T.pw[:], [[0, 480]])
+    scatter(R("w1"), slot1, R("val1"))
+    tt(R("f1", 0, 192), R("w1", 0, 192), R("mask"), A.mult)
+    scan(R("f1", 192, 384), R("seg"), R("f1", 0, 192))
+    cp(R("stl"), ends("f1", a=192))
+    pickq(R("Q1"), R("QX"), R("stl"))
+    picks(R("S1"), R("SX"), R("stl"))
+    send("qa", block("Q1"), True)
+    send("sa", block("S1"))
+    D("y", R("W1", 0, X0), R("QX"), "dq1", False, outap=u8(ap(R("W1", 0, X0))), inap=u8(ap(R("QX"))))
+    D("y", R("P1", 0, X0), R("SX"), "dq1")
+    D("y", R("W2", 0, X1), R("W1", 0, X1), "dq2", False, outap=u8(ap(R("W2", 0, X1))), inap=u8(ap(R("W1", 0, X1))))
+    D("y", R("P2", 0, X1), R("P1", 0, X1), "dq2")
 
-    lo, ofo, ofa = T.lo, T.of[:, 0:12], T.of[:, 12:24]
-    ts("nv0 nv1 nv2 nv3", "vo", T.nv[:, 12:24], T.nv[:, 0:12], 512.0, None, A.mult)
-    tt("vo b1x", "VO", T.VO[:], T.nv[:, 12:24], b1x, A.add)
-    ts("VO", "lo0", lo[:, 0:12], T.VO[:], 2, 0x3C0, A.arith_shift_right, A.bitwise_and)
-    ts("VO", "lo1", lo[:, 12:24], T.VO[:], 12, 63, A.arith_shift_right, A.bitwise_and)
-    ts("VO", "l5o", T.l56i[:, 0:12], T.VO[:], 9, 511, A.arith_shift_right, A.bitwise_and)
-    tt("lo0 lo1", "lo2", lo[:, 24:36], lo[:, 0:12], lo[:, 12:24], A.add)
-    ts("t10 t11 t12 t13", "invo", T.inv[:, 0:12], T.t1[:], float(rank), 4096.0, A.not_equal, A.mult)
-    cp("lo2", "ofo", ofo, lo[:, 24:36])
-    pick(stu, "stu", T.QX[:], T.SX[:], "QX", "SX", T.QO[:], T.SO[:], "QO", "SO")
-    tt("tb ofo mask", "n2mo", T.n2m[:, 0:192], T.tb[:].indirect(ofo), T.mask[:, 0:192], A.mult)
-    cp("l5o", "lu0", T.lu[Qd[0]], T.l56i[Qd[0], 0:12])
-    scan("n2mo seg", "n2so", T.n2s[:, 0:192], T.seg[:, 0:192], T.n2m[:, 0:192], 0.0, A.mult, A.add)
-    cp("lub", "lu2", T.lu[Qd[2]], T.lub[Qd[2], 0:12])
-    cp("sb", "lad0", T.lad[Qd[0]], T.sb[Qd[0], 0:12])
-    ts("i16", "lad1", T.lad[Qd[1]], T.i16[Qd[1], 0:12], 512.0, None, A.add)
-    cp("lo2", "lad2", T.lad[Qd[2]], lo[Qd[2], 24:36])
-    ac("tb2B", "tb2C", T.tb2[Qd[3]], T.tb2[Qd[2]])
-    ac("ident cf4", "keyc", T.vk[:, 384:576], T.ident[:, 0:192], bias=T.cf[:, 4:5])
-    ac("ident vb0 vb1 vb2 vb3", "v1", T.vk[:, 0:192], T.ident[:, 0:192], scale=1024.0, bias=T.cf[:, 14:15])
-    ac("ident", "v2a", T.vk[:, 192:384], T.ident[:, 0:192], scale=1024.0, bias=1024.0 * 385)
-    E("v", "ws0", "WQ0", lambda e: e.quantize_mx(T.WQ[:, 0:512], T.WS[:, 0:512], T.ws[:, 0:2048]))
-    E("v", "ws1", "WQ1", lambda e: e.quantize_mx(T.WQ[:, 512:768], T.WS[:, 512:768], T.ws[:, 2048:3072]))
+    for k, d in enumerate(oth):
+        ts(R("off", P=Qd[d]), R("A1", 12 * k, 12 * k + 12, Qd[d]), 4.0 - 1024 * rank, 1028.0, A.add, A.min)
+    tt(R("n2m"), ind(R("tb"), R("off")), R("mask"), A.mult)
+    ts(R("c1i"), R("off"), 0.5, Z0 - 2.25, A.mult, A.add)
+    scan(R("n2s"), R("seg"), R("n2m"))
+    cp(R("c1u"), R("c1i"))
+    n2v = ends("n2s")
+    ts(R("t2"), n2v, 1.0 / 512, -255.5 / 512, A.mult, A.add)
+    ac(R("uf1"), ind(idn, R("c1u")), scale=1024.0)
+    ac(R("n2k"), n2v, scale=2048.0, bias=float(X1))
+    z2 = classes(R("t2"), "eqb", "sc", "bb", "btb", "rb", "pb", "xb", 11, True,
+                 [lambda: ts(R("c1o"), R("c1i"), od, float(-X1), A.mult, A.add)] + [wq(i) for i in range(6)])
+    for k, d in enumerate(oth):
+        ac(R("L0f", P=Qd[d]), R("AP", 12 * k, 12 * k + 12, Qd[d]), bias=float(X0))
+    ac(R("L0e"), R("L0f"), scale=ev)
+    tt(R("M2"), R("n2k"), z2, A.add)
+    send("mz", lambda k: R("M2"))
+    cp(R("L0u"), R("L0f"))
+    slot2 = R("sl", 12, 24)
+    cp(slot2, z2)
+    tt(R("val2"), ind(idn, R("L0u")), R("uf1"), A.add)
+    scatter(R("w2"), slot2, R("val2"))
+    tt(R("SBm"), R("L0e"), R("c1o"), A.add)
+    co(R("pw", 0, 288), 0.0)
+    co(R("PZ"), 0.0)
+    co(R("g3", 0, 3), 0.0)
+    co(R("F32"), 0.0)
+    co(R("idt"), 0.0)
+    tc = [R("tc", 32 * i, 32 * i + 32) for i in range(7)]
 
-    la = T.la
-    ts("RA", "la0", la[:, 0:12], T.RA[:], 2, 0x3C0, A.arith_shift_right, A.bitwise_and)
-    ts("RA", "la1", la[:, 12:24], T.RA[:], 12, 63, A.arith_shift_right, A.bitwise_and)
-    ts("RA", "la3", la[:, 36:48], T.RA[:], 255, None, A.bitwise_and)
-    tt("la0 la1", "la2", la[:, 24:36], la[:, 0:12], la[:, 12:24], A.add)
-    ts("RA", "l5a", T.l56i[:, 12:24], T.RA[:], 9, 511, A.arith_shift_right, A.bitwise_and)
-    cp("la2", "ofa", ofa, la[:, 24:36])
-    tt("la3 sk0 sk1 sk2", "lub1", T.lub[:, 12:24], la[:, 36:48], T.sk[:], A.add)
-    tt("tb ofa mask", "n2ma", T.n2m[:, 192:384], T.tb[:].indirect(ofa), T.mask[:, 0:192], A.mult)
-    ts("RA", "inva", T.inv[:, 12:24], T.RA[:], 1048576.0, 4096.0, A.is_lt, A.mult)
-    scan("n2ma seg", "n2sa", T.n2s[:, 192:384], T.seg[:, 0:192], T.n2m[:, 192:384], 0.0, A.mult, A.add)
-    cp("la2", "lad3", T.lad[Qd[3]], la[Qd[3], 24:36])
-    n2v = T.n2s[:, 15:384:16]
-    tt("n2so n2sa invo inva", "n2e", T.n2e[:], n2v, T.inv[:], A.add)
-    cp("l5a", "lu1", T.lu[Qd[1]], T.l56i[Qd[1], 12:24])
-    ts("n2e", "t2", T.t2[:], T.n2e[:], 1.0 / 512, -255.5 / 512, A.mult, A.add)
-    cp("lub1", "lu3", T.lu[Qd[3]], T.lub[Qd[3], 12:24])
-    ac("tb2A tb2B tb2C lad0 lad1 lad2 lad3", "ad", T.ad[:], T.tb2[:].indirect(T.lad[:]))
-    ac("ident lu0 lu1 lu2 lu3 scA scB bcA bcB", "uf", T.uf[:], T.ident[:].indirect(T.lu[:]), scale=T.cf[:, 12:13], bias=T.cf[:, 13:14])
-    classes(24, T.t2[:], "t2", T.eqb, T.sbb, T.bb, T.btb, T.rb, T.pb, T.xb, 9, "b", 36)
-    slot2 = T.sl[:, 12:24]
-    for q in range(4):
-        a = 120 + 12 * (q % 2)
-        cp("bz", "bslot%d" % q, T.sl[Qd[q], 12:24], T.xb[Qd[q], a:a + 12])
-    tt("uf ad", "val2", T.val2[:], T.uf[:], T.ad[:], A.add)
-    E("v", "w2 bslot0 bslot1 bslot2 bslot3 val2", "w2", lambda e: e.tensor_copy(T.w2[:].indirect(slot2), T.val2[:]))
-    tt("w2 mask", "f2a", T.f2[:, 0:192], T.w2[:, 0:192], T.mask[:, 0:192], A.mult)
-    scan("f2a seg", "f2", T.f2[:, 192:384], T.seg[:, 0:192], T.f2[:, 0:192], 0.0, A.mult, A.add)
-    for q in range(4):
-        (ac if q % 2 else cp)("f2", "hg%d" % q, T.hg[Qd[q], 0:12], T.f2[Qd[q ^ 1], 207:384:16])
-    tt("f2 hg0 hg1 hg2 hg3", "hh", T.hg[:, 12:24], T.f2[:, 207:384:16], T.hg[:, 0:12], A.add)
-    lo_, hi_ = T.hg[lower, 12:24], T.hg[upper, 12:24]
-    cp("hh", "R2a", T.R2[lower], hi_)
-    cp("hh", "R2b", T.R2[upper], hi_)
-    cp("hh", "faa", T.fa[lower, 0:12], lo_)
-    cp("hh", "fab", T.fa[upper, 0:12], lo_)
-    send("rb", "R2a R2b", lambda i: T.R2[:, 4 * i:4 * i + 4], lambda k: T.TV[:, 4 * k:4 * k + 4])
-    ts("faa fab", "fa1", T.fa[:, 12:24], T.fa[:, 0:12], 511, None, A.bitwise_and)
-    ts("faa fab", "fa2", T.fa[:, 24:36], T.fa[:, 0:12], 9, None, A.arith_shift_right)
-    cp("fa1", "l3", T.l34[:, 0:12], T.fa[:, 12:24])
-    cp("fa2", "l4", T.l34[:, 12:24], T.fa[:, 24:36])
-    pick(T.l34[:, 0:12], "l3", T.QX[:], T.SX[:], "QX", "SX", T.Q3[:], T.S3[:], "Q3", "S3")
-    send("qb", "Q3", lambda i: u8(T.Q3[:, C * i:C * i + C]), lambda k: u8(T.TE1[:, C * k:C * k + C]))
-    pick(T.l34[:, 12:24], "l4", T.QW[:], T.SW[:], "QWo QWa", "SWo SWa", T.Q4[:], T.S4[:], "Q4", "S4")
-    send("sb", "S3", lambda i: T.S3[:, C * i:C * i + C], lambda k: T.TS1[:, C * k:C * k + C])
-    send("qc", "Q4", lambda i: u8(T.Q4[:, C * i:C * i + C]), lambda k: u8(T.TE0[:, C * k:C * k + C]))
-    send("sc", "S4", lambda i: T.S4[:, C * i:C * i + C], lambda k: T.TS0[:, C * k:C * k + C])
+    def s0():
+        tt(R("f2", 0, 192), R("w2", 0, 192), R("mask"), A.mult)
 
-    ef = T.e0
-    for q in range(N):
-        k = oth.index(q) if q != rank else None
-        a, n = (0, 12) if q == rank else (12 + 4 * k, 4)
-        ts("t2 eq1", "eq1%d" % q, ef[Qd[q], 0:n], T.t2[Qd[q], a:a + n], float(rank), None, A.is_equal)
-        if q == rank:
-            ac("i16 i1", "i1%d" % q, ef[Qd[q], 12:24], T.i16[Qd[q], 0:12])
-        else:
-            ac("lub1 i1", "i1%d" % q, ef[Qd[q], 12:16], T.lub[Qd[q], 12 + 4 * k:16 + 4 * k], bias=-256.0 * q)
-    eks = " ".join("eq1%d i1%d" % (q, q) for q in range(N))
-    cp("n2so n2sa", "l6i", T.l56i[:, 24:48], n2v)
-    tt(eks + " eq1 i1 trx2", "e2", ef[:, 24:36], ef[:, 12:24], trk, A.subtract)
-    ts("l6i", "l6j", T.l56i[:, 48:72], T.l56i[:, 24:48], 511, None, A.bitwise_and)
-    tt(eks + " eq1 e2", "e3", ef[:, 36:48], ef[:, 24:36], ef[:, 0:12], A.mult)
-    cp("l5o l5a", "l5", T.l56[:, 0:24], T.l56i[:, 0:24])
-    tt("e3 trx2", "e4", ef[:, 48:60], ef[:, 36:48], trk, A.add)
-    cp("l6j", "l6", T.l56[:, 24:48], T.l56i[:, 48:72])
-    cp("e4", "o1", T.o1[:], ef[:, 48:60])
-    E("v", "kw o1 v1", "kw", lambda e: e.tensor_copy(T.kw[:].indirect(T.o1[:]), T.vk[:, 0:192]))
-    pick(T.l56[:, 0:24], "l5", T.QX[:], T.SX[:], "QX", "SX", T.QN1[:], T.SN1[:], "QN1", "SN1")
+    def e0():
+        tt(R("Zf", 0, 12), R("n2k"), R("SBm"), A.add)
 
-    def mm(bank, o, k, q, s, keys, start, stop):
-        a = 128 * (k * O + o)
-        E("t", keys + " WQ0 WQ1", "ps%d" % bank if stop else "", lambda e: e.matmul_mx(
-            T.ps[:, 512 * bank:512 * bank + 192], T.WQ[:, a:a + 128], T.WS[:, a:a + 128], q, s, start, stop))
+    def s1():
+        scan(R("f2", 192, 384), R("seg"), R("f2", 0, 192))
 
-    ei, hf = T.ei, T.ef
-    ts("TV", "ei0", ei[:, 0:12], T.TV[:], 11, 255, A.arith_shift_right, A.bitwise_and)
-    ts("TV", "ei1", ei[:, 12:24], T.TV[:], 19, None, A.arith_shift_right)
-    ts("TV", "ei2", ei[:, 24:36], T.TV[:], 511, None, A.bitwise_and)
-    tt("ei0 tri", "h0", hf[:, 0:12], ei[:, 0:12], T.tri[:, 0:12], A.subtract)
-    ts("ei1 cf3", "h1", hf[:, 12:24], ei[:, 12:24], T.cf[:, 3:4], None, A.is_equal)
-    tt("h0 h1", "h2", hf[:, 24:36], hf[:, 0:12], hf[:, 12:24], A.mult)
-    cp("ei2", "l7", T.l7[:], ei[:, 24:36])
-    tt("h2 tri", "h3", hf[:, 36:48], hf[:, 24:36], T.tri[:, 0:12], A.add)
-    cp("h3", "oe2", T.oe2[:], hf[:, 36:48])
-    E("v", "kw oe2 v2a", "kw", lambda e: e.tensor_copy(T.kw[:].indirect(T.oe2[:]), T.vk[:, 192:384]))
-    pick(T.l56[:, 24:48], "l6", T.QX[:], T.SX[:], "QX", "SX", T.QN2[:], T.SN2[:], "QN2", "SN2")
-    pick(T.l7[:], "l7", T.QX[:], T.SX[:], "QX", "SX", T.QE2[:], T.SE2[:], "QE2", "SE2")
+    def e1():
+        tt(R("Zf", 12, 24), R("Zf", 0, 12), landed("mz", 0), A.min)
 
-    for o in range(O):
-        mm(o, o, 0, T.QO[:], T.SO[:], "QO SO", True, False)
-        mm(2 + o, o, 0, T.QW[:, 512:704], T.SW[:, 512:704], "QWa SWa", True, False)
-    for o in range(O):
-        mm(o, o, 1, T.QN1[:, 0:192], T.SN1[:, 0:192], "QN1 SN1", False, False)
-        mm(2 + o, o, 1, T.QN1[:, 192:384], T.SN1[:, 192:384], "QN1 SN1", False, False)
-    for o in range(O):
-        mm(o, o, 2, T.QN2[:, 0:192], T.SN2[:, 0:192], "QN2 SN2", False, True)
-        mm(2 + o, o, 2, T.QN2[:, 192:384], T.SN2[:, 192:384], "QN2 SN2", False, True)
-    for o in range(O):
-        mm(4 + o, o, 2, T.QE2[:], T.SE2[:], "QE2 SE2", True, False)
-    for o in range(O):
-        mm(4 + o, o, 1, T.TE1[:], T.TS1[:], "TE1 TS1", False, False)
-    for o in range(O):
-        mm(4 + o, o, 0, T.TE0[:], T.TS0[:], "TE0 TS0", False, True)
+    def s2():
+        for q in (1, 3, 0, 2):
+            (ac if q % 2 else cp)(R("hg", 0, 12, Qd[q]), ends("f2", Qd[q ^ 1], a=192))
 
-    g1, h = T.g1, T.hf
-    pres, cum, pm, mk, mf, pk = [g1[:, 192 * i:192 * i + 192] for i in range(6)]
-    ac("kw", "pres", pres, T.kw[:, 0:192], fn=AF.Sign)
-    tt("kw mask", "pm", pm, T.kw[:, 0:192], T.mask[:, 0:192], A.min)
-    scan("pres ones", "cum", cum, pres, T.ones[:], 0.0, A.add, A.mult)
-    for a, b, n, c in ((64, 0, 64, 0), (32, 0, 32, 1), (96, 64, 32, 1), (64, 32, 32, 2), (96, 0, 32, 2)):
-        ac("cum bt3", "bx%d%d" % (a, c), T.bt3[a:a + n, c:c + 1], g1[b:b + n, 383:384])
-    for o in range(O):
-        for b in range(2):
-            ac("ps%d" % (2 * b + o), "res%d%d" % (o, b), T.res[:, 592 * o + 1 + 192 * b:592 * o + 193 + 192 * b], T.ps[:, 512 * (2 * b + o):512 * (2 * b + o) + 192])
-    tt("pm cum", "mmm", mk, pm, cum, A.mult)
-    scan("mmm seg", "mf", mf, T.seg[:, 0:192], mk, 0.0, A.mult, A.add)
-    E("v", "bt3 bx640 bx321 bx961 bx642 bx962", "base", lambda e: e.tensor_reduce(h[:, 48:49], T.bt3[:, 0:3], AxisListType.X, A.add))
-    cI = g1[:, 192 * 4 + 15:192 * 5:16]
-    ts("mf", "k0", h[:, 0:12], cI, 0.0, None, A.is_gt)
-    tt("mf trx1", "k1", h[:, 12:24], cI, trp1, A.subtract)
-    ts("k1 base", "k2", h[:, 24:36], h[:, 12:24], h[:, 48:49], None, A.add)
-    tt("kw keyc", "pk", pk, T.kw[:, 0:192], T.vk[:, 384:576], A.add)
-    tt("k0 k2", "k3", h[:, 36:48], h[:, 0:12], h[:, 24:36], A.mult)
-    tt("k3 trx0 k1 k2", "k4", h[:, 12:24], h[:, 36:48], trp, A.add)
-    cp("k4", "o3", T.o3[:], h[:, 12:24])
-    E("v", "pw o3 pk", "pw", lambda e: e.tensor_copy(T.pw[:].indirect(T.o3[:]), pk))
-    tt("pw mask", "f3a", T.f3[:, 0:288], T.pw[:, 0:288], T.mask[:, 0:288], A.mult)
-    scan("f3a seg", "f3", T.f3[:, 288:576], T.seg[:, 0:288], T.f3[:, 0:288], 0.0, A.mult, A.add)
-    mg = T.mg
-    ac("f3", "ga", mg[lower, 0:18], T.f3[upper, 303:576:16])
-    cp("f3", "gb", mg[upper, 0:18], T.f3[lower, 303:576:16])
-    tt("f3 ga gb", "gc", mg[:, 18:36], T.f3[:, 303:576:16], mg[:, 0:18], A.add)
-    for q in range(N):
-        (ac if q % 2 else cp)("gc", "gd%d" % q, mg[Qd[q], 36:54], mg[Qd[q ^ 1], 18:36])
-    tt("gc gd0 gd1 gd2 gd3", "pki", T.pki[:, 0:18], mg[:, 18:36], mg[:, 36:54], A.add)
-    pki = T.pki[:, 0:18]
-    ts("pki", "yli", T.pki[:, 18:36], pki, 10, None, A.arith_shift_right)
-    cp("yli", "yl", T.yl[:], T.pki[:, 18:36])
-    ac("ps4", "res02", T.res[:, 385:577], T.ps[:, 512 * 4:512 * 4 + 192])
-    ac("ps5", "res12", T.res[:, 592 + 385:592 + 577], T.ps[:, 512 * 5:512 * 5 + 192])
-    E("v", "resz0 res00 res01 res02 yl", "ys0", lambda e: e.tensor_copy(T.ysb[:, 0:M], T.res[:, 0:577].indirect(T.yl[:])))
-    ac("resz1 res10 res11 res12 yl", "ys1", T.ysb[:, M:2 * M], T.res[:, 592:592 + 577].indirect(T.yl[:]))
-    D("y", T.y[:, 0:M], T.ysb[:, 0:M], "dy0", r="ys0")
-    D("s", T.y[:, M:2 * M], T.ysb[:, M:2 * M], "dy1", r="ys1")
-    ii = T.idi
-    ts("pki", "ii0", ii[:, 0:18], pki, 8, 3, A.arith_shift_right, A.bitwise_and)
-    ts("pki", "ii1", ii[:, 18:36], pki, 255, None, A.bitwise_and)
-    ts("pki", "ii2", ii[:, 36:54], pki, 1024.0, -1.0, A.is_ge, A.add)
-    tt("ii0 ii2 idt", "it0", T.idt[:, 0:18], ii[:, 0:18], ii[:, 36:54], A.add)
-    tt("ii1 ii2 idt", "it1", T.idt[:, 32:50], ii[:, 18:36], ii[:, 36:54], A.add)
-    E("v", "it0 it1 idt", "idx", lambda e: e.transpose(T.idx[:], T.idt[:]))
-    D("y", T.id[0:1, :], T.idx[0:18, 0:16], "di0", r="idx")
-    D("s", T.id[1:2, :], T.idx[0:18, 32:48], "di1", r="idx")
+    def e2():
+        tt(R("Zf", 24, 36), R("Zf", 12, 24), landed("mz", 1), A.min)
 
-    wait("g", [(q, cnt[q]) for q in ("v", "s", "t", "g")] + [("loc", loc[0])] + [(s, dsum[s]) for s in DMAS] + [a for h_ in HOPS for a in arrivals[h_]])
+    def s3():
+        tt(R("hg", 12, 24), ends("f2", a=192), R("hg", 0, 12), A.add)
+
+    def e3():
+        tt(R("Zi", 0, 12), R("Zf", 24, 36), landed("mz", 2), A.min)
+
+    def s4():
+        ac(R("hg", 24, 36, upper), R("hg", 12, 24, lower))
+        cp(R("hg", 24, 36, lower), R("hg", 12, 24, upper))
+
+    def e4():
+        ts(R("Zi", 12, 24), R("Zi", 0, 12), 20, None, A.arith_shift_right)
+        ts(R("Zi", 24, 36), R("Zi", 0, 12), 11, 511, A.arith_shift_right, A.bitwise_and)
+        ts(R("Zi", 36, 48), R("Zi", 0, 12), 2047, None, A.bitwise_and)
+
+    def s5():
+        tt(R("fa", 0, 12), R("hg", 12, 24), R("hg", 24, 36), A.add)
+
+    def e5():
+        ts(R("PZ", 0, 12), R("Zi", 12, 24), float(rank), -1.0, A.is_equal, A.add)
+        ts(R("ze", 0, 12), R("Zi", 24, 36), ev, None, A.mult)
+
+    def s6():
+        ts(R("fa", 12, 24), R("fa", 0, 12), 10, None, A.arith_shift_right)
+        ts(R("fa", 24, 36), R("fa", 0, 12), 1023, None, A.bitwise_and)
+
+    def e6():
+        turn(tc[0], R("PZ"))
+        tt(R("ze", 12, 24), R("ze", 0, 12), R("K2"), A.add)
+
+    def s7():
+        cp(R("l34", 0, 12), R("fa", 12, 24))
+        cp(R("l34", 12, 24), R("fa", 24, 36))
+
+    def e7():
+        scan(tc[1], R("seg", 0, 32), tc[0])
+        cp(R("zl", 12, 24), R("ze", 12, 24))
+
+    def s8():
+        pickq(R("Q3"), R("QX"), R("l34", 0, 12))
+        picks(R("S3"), R("SX"), R("l34", 0, 12))
+        send("qb", block("Q3"), True)
+
+    def e8():
+        for a, b, n, c, v in ((32, 0, 32, 1, 0), (64, 32, 32, 2, 0), (64, 0, 64, 0, 1), (96, 64, 32, 1, 1), (96, 0, 32, 2, 1)):
+            (cp if v else ac)(R("g3", c, c + 1, slice(a, a + n)), R("tc", 47, 48, slice(b, b + n)))
+        ts(R("pr"), R("Zi", 12, 24), float(rank), None, A.is_equal)
+
+    def e9():
+        scan(R("g3", 3, 6), R("sg", 132, 135), R("g3", 0, 3))
+        ac(R("uf2"), ind(idn, R("zl", 12, 24)), scale=1024.0, bias=col(15))
+
+    def s9():
+        pickq(R("Q4"), R("W1", 0, X1), R("l34", 12, 24))
+        picks(R("S4"), R("P1", 0, X1), R("l34", 12, 24))
+        send("sb", block("S3"))
+        send("qc", block("Q4"), True)
+        send("sc", block("S4"))
+
+    for fn in (s0, e0, s1, s2, e1, s3, e2, s4, e3, s5, e4, s6, e5, s7, e6, s8, e7, e8, e9, s9):
+        fn()
+    cp(R("zl", 0, 12), R("Zi", 36, 48))
+    ts(tc[2], R("maskc"), R("tc", 47, 48), R("g3", 5, 6), A.mult, A.add)
+    turn(tc[3], tc[2])
+    scan(tc[4], R("sg", 36, 68), tc[3])
+    ts(tc[5], tc[1], R("tc", 159, 160), col(14), A.add, A.add)
+    turn(tc[6], tc[5])
+    tt(R("val3"), ind(idn, R("zl", 0, 12)), R("uf2"), A.add)
+    tt(R("pz", 0, 12), R("tc", 192, 204), R("pr"), A.mult)
+    tt(R("pz", 12, 24), R("pz", 0, 12), R("park"), A.add)
+    slot3 = R("sl", 24, 36)
+    cp(slot3, R("pz", 12, 24))
+    scatter(R("pw"), slot3, R("val3"))
+    turn(R("f3"), R("pw", 0, 288))
+    for q in (1, 3, 0, 2):
+        (ac if q % 2 else cp)(R("hm", P=Qd[q]), R("f3", 0, 288, Qd[q ^ 1], 16))
+    tt(R("F32", 0, 18), R("f3", 0, 288, every, 16), R("hm"), A.add)
+    turn(R("TF"), R("F32"))
+    ac(R("hx", P=upper), R("TF", P=lower))
+    cp(R("hx", P=lower), R("TF", P=upper))
+    for i in range(4):
+        a = 16 * (i // 2)
+        tt(R("DD", 16 * i, 16 * i + 16), R("TF", a, a + 16), R("hx", a, a + 16), A.add)
+    turn(R("LT"), R("DD"))
+    for i in range(4):
+        o, h = i % 2, i // 2
+        cp(R("li", 18 * o + h, 18 * o + 18, every, 2), R("LT", 32 * h + o, 32 * h + 18, every, 2))
+    li, lh, ll = R("li", 0, 36), R("li", 36, 72), R("li", 72, 108)
+    ts(lh, li, 10, None, A.arith_shift_right)
+    ts(ll, li, 1023, None, A.bitwise_and)
+    cp(R("HU"), R("li", 36, 54))
+    cp(R("LU"), ll)
+
+    def products(i, q, s, a, b):
+        for o in range(O):
+            c, d = 128 * ((2 - i) * O + o), 512 * (2 * o + (1 if a else 0))
+            E("t", [R(q, a, b), R(s, a, b), R("WQ", c, c + 128), R("WS", c, c + 128)], [R("ps", d, d + b - a)] if i == 2 else [],
+              lambda e: e.matmul_mx(ap(R("ps", d, d + b - a)), ap(R("WQ", c, c + 128)), ap(R("WS", c, c + 128)), ap(R(q, a, b)), ap(R(s, a, b)), i == 0, i == 2))
+
+    for i, (q, s, w, p, l) in enumerate((("G2", "H2", R("QX"), R("SX"), R("HU")), ("G1", "H1", R("W1"), R("P1"), R("LU", 18, 36)))):
+        pickq(R(q), w, l)
+        picks(R(s), p, l)
+        for a, b in ((0, H), (H, M)):
+            products(i, q, s, a, b)
+    for a, b in ((0, H), (H, M)):
+        l = R("LU", a // 16, b // 16)
+        pickq(R("G0", a, b), R("W2"), l)
+        picks(R("H0", a, b), R("P2"), l)
+        products(2, "G0", "H0", a, b)
+    ii = R("idi", 0, 18), R("idi", 18, 36), R("idi", 36, 54)
+    ts(ii[0], R("li", 18, 36), 18, None, A.arith_shift_right)
+    ts(ii[1], R("li", 54, 72), 255, None, A.bitwise_and)
+    ts(ii[2], R("li", 18, 36), 1.0, -1.0, A.is_ge, A.add)
+    cp(R("ysb", 0, H), R("ps", 0, H))
+    ac(R("ysb", M, M + H), R("ps", 1024, 1024 + H))
+    tt(R("idt", 0, 18), ii[0], ii[2], A.add)
+    tt(R("idt", 32, 50), ii[1], ii[2], A.add)
+    cp(R("ysb", H, M), R("ps", 512, 512 + M - H))
+    ac(R("ysb", M + H, 2 * M), R("ps", 1536, 1536 + M - H))
+    D("y", None, R("ysb", 0, M), "dy0", outap=T.y[:, 0:M])
+    D("s", None, R("ysb", M, 2 * M), "dy1", outap=T.y[:, M:2 * M])
+    turn(R("idx"), R("idt"))
+    D("y", None, R("idx", 0, 16, slice(0, 18)), "di0", outap=T.id[0:1, :])
+    D("y", None, R("idx", 32, 48, slice(0, 18)), "di1", outap=T.id[1:2, :])
+
+    wait("g", [(q, cnt[q]) for q in ("v", "s", "t", "g")] + [("loc", loc[0])] + [(s, dsum[s]) for s in DMAS] + arrivals)

@@ -6,7 +6,7 @@ C = 64
 Z0 = 8
 X0 = Z0 + 512
 X1 = X0 + 192
-H = 160
+L = M // 2
 F, I, U, B = "float32", "int32", "uint16", "bfloat16"
 Q8, S8 = "float8_e4m3fn_x4", "uint8"
 
@@ -16,29 +16,29 @@ def _sb(w, d):
 
 
 SCRATCH = {
-    "tba": _sb(1024, I), "tb": _sb(1032, F), "tbd": ("dram", [1, 1024], F), "sb": _sb(24, I), "nxi": _sb(64, I), "nxf": _sb(64, F), "nxt": _sb(64, F),
+    "tba": _sb(1024, I), "tb": _sb(1032, F), "sb": _sb(24, I), "nxi": _sb(64, I), "nxf": _sb(64, F), "nxt": _sb(64, F),
     "xs": _sb(4 * X0, B), "ws": _sb(3072, B),
     "QX": _sb(X0, Q8), "SX": _sb(X0, S8), "W1": _sb(X1 + 192, Q8), "P1": _sb(X1 + 192, S8), "W2": _sb(X1 + 192, Q8), "P2": _sb(X1 + 192, S8),
     "WQ": _sb(768, Q8), "WS": _sb(768, S8),
     "Q1": _sb(192, Q8), "S1": _sb(192, S8), "Q3": _sb(192, Q8), "S3": _sb(192, S8), "Q4": _sb(192, Q8), "S4": _sb(192, S8),
     "G0": _sb(288, Q8), "H0": _sb(288, S8), "G1": _sb(288, Q8), "H1": _sb(288, S8), "G2": _sb(288, Q8), "H2": _sb(288, S8),
-    "j15": _sb(192, F), "pI": _sb(1, I), "c16": _sb(12, F), "ident": _sb(1104, F), "mask": _sb(192, F), "seg": _sb(192, F), "maskb": _sb(32, F),
-    "maskc": _sb(32, F), "sg": _sb(144, F), "ci": _sb(4, I), "cf": _sb(24, F), "i16": _sb(12, F), "tri": _sb(12, F), "park": _sb(12, F), "K2": _sb(12, F),
-    "l0": _sb(84, I), "lx": _sb(24, U), "b2f": _sb(12, F), "stf": _sb(12, F),
-    "val1": _sb(192, F), "n1m": _sb(192, F), "n1s": _sb(192, F), "t1": _sb(12, I), "E1x": _sb(12, F), "E1": _sb(12, F), "M1": _sb(12, U), "A1": _sb(36, U),
+    "j15": _sb(192, F), "pI": _sb(1, I), "c16": _sb(12, F), "ident": _sb(1104, F), "mask": _sb(192, F), "mask2": _sb(192, F), "seg": _sb(192, F), "maskb": _sb(32, F),
+    "maskc": _sb(32, F), "sg": _sb(192, F), "ci": _sb(4, I), "cf": _sb(24, F), "i16": _sb(12, F), "park": _sb(12, F), "K2": _sb(12, F),
+    "l0": _sb(36, I), "lf": _sb(48, F), "lx": _sb(24, U), "stf": _sb(12, F),
+    "val1": _sb(192, F), "n1m": _sb(192, F), "n1s": _sb(192, F), "t1": _sb(12, I), "E1": _sb(12, F), "M1": _sb(12, U), "A1": _sb(36, U),
     "MP": _sb(12, B), "AP": _sb(36, B),
-    "eqa": _sb(72, F), "sa": _sb(36, F), "ba": _sb(96, F), "bta": _sb(96, F), "ra": _sb(96, F), "pa": _sb(36, F), "xa": _sb(72, F),
-    "eqb": _sb(72, F), "sc": _sb(36, F), "bb": _sb(96, F), "btb": _sb(96, F), "rb": _sb(96, F), "pb": _sb(36, F), "xb": _sb(72, F), "g9": _sb(18, F),
+    "eqa": _sb(72, F), "sa": _sb(36, F), "ba": _sb(96, F), "bta": _sb(96, F), "ra": _sb(96, F), "pa": _sb(36, F), "xa": _sb(96, F),
+    "eqb": _sb(72, F), "sc": _sb(36, F), "bb": _sb(96, F), "btb": _sb(96, F), "rb": _sb(96, F), "pb": _sb(36, F), "xb": _sb(96, F), "g9": _sb(18, F),
     "sl": _sb(36, U), "w1": _sb(384, F), "w2": _sb(384, F), "pw": _sb(480, F), "f1": _sb(384, F), "f2": _sb(384, F), "f3": _sb(288, F),
     "stl": _sb(12, U), "off": _sb(12, U), "n2m": _sb(192, F), "n2s": _sb(192, F), "t2": _sb(12, I), "c1i": _sb(12, I), "c1u": _sb(12, U), "c1o": _sb(12, F),
     "L0f": _sb(12, F), "L0e": _sb(12, F), "L0u": _sb(12, U), "SBm": _sb(12, F), "n2k": _sb(12, F), "M2": _sb(12, F), "A2": _sb(36, F), "uf1": _sb(192, F), "val2": _sb(192, F),
     "hg": _sb(36, F), "fa": _sb(48, I), "l34": _sb(24, U),
     "Zf": _sb(36, F), "Zi": _sb(48, I), "zl": _sb(24, U), "ze": _sb(24, F), "uf2": _sb(192, F), "val3": _sb(192, F), "pr": _sb(12, F), "PZ": _sb(32, F),
-    "tc": _sb(224, F), "g3": _sb(6, F), "pz": _sb(24, F), "hm": _sb(18, F), "F32": _sb(32, F), "TF": _sb(32, F), "hx": _sb(32, F), "DD": _sb(64, F), "LT": _sb(64, F),
-    "li": _sb(108, I), "LU": _sb(36, U), "HU": _sb(18, U), "idi": _sb(72, I), "idt": _sb(64, F), "idx": _sb(64, F), "ysb": _sb(576, F),
+    "tc": _sb(224, F), "g3": _sb(6, F), "pz": _sb(24, F), "hm": _sb(18, F), "F32": _sb(32, F), "TF": _sb(32, F), "hx": _sb(32, F), "DD": _sb(64, I), "LT": _sb(64, I),
+    "SS": _sb(32, I), "li": _sb(64, I), "LU": _sb(64, U), "HU": _sb(64, U), "idi": _sb(96, I), "idt": _sb(64, F), "ysb": _sb(576, F),
     "ps": ("psum", [128, 2048], F),
 }
-DMAS = ["dnx", "dst", "dx", "dw0", "dw1", "dni", "dz", "dtd", "dtr", "dtq", "dq1", "dq2", "dy0", "dy1", "di0", "di1"]
+DMAS = ["dnx", "dst", "dsu", "dx", "dx1", "dw0", "dw1", "dni", "dtr", "dtq", "dq1", "dq2", "dy0", "dy1", "di0", "di1"]
 HOPS = ("ma", "mp", "qa", "sa", "mz", "qb", "sb", "qc", "sc")
 SEMAPHORES = ["v", "s", "t", "g", "loc"] + DMAS + [n + str(k) for n in HOPS for k in range(N - 1)]
 
@@ -72,7 +72,7 @@ def rank_program(g, core, T, topo):
     seen, writers, readers, dsum, pend, loc = {}, {}, {}, {}, {}, [0]
     Qd = [slice(32 * q, 32 * q + 32) for q in range(4)]
     lower, upper, every = slice(0, 64), slice(64, 128), slice(0, 128)
-    QM = Qd[rank]
+    QM, q0 = Qd[rank], Qd[0]
 
     def R(name, a=0, b=None, P=every, st=1):
         return (name, P.start, P.stop, a, SCRATCH[name][1][1] if b is None else b, st)
@@ -244,85 +244,86 @@ def rank_program(g, core, T, topo):
     for i in range(2):
         D("y", R("sb", 0, 12, slice(16 * i, 16 * i + 16)), None, "dst", False, inap=T.st[:])
         D("s", R("sb", 12, 24, slice(16 * i, 16 * i + 16)), None, "dst", i == 1, inap=T.bt[:])
+    for i in range(2):
+        D("ys"[i], R("nxi", P=slice(16 * i, 16 * i + 16)), None, "dni", i == 1, inap=T.nx[:])
     for i in range(16):
         D("y", R("tba", P=slice(i, i + 1)), None, "dnx", False, inap=T.nx[:])
         D("s", R("tba", P=slice(16 + i, 17 + i)), None, "dnx", i == 15, inap=T.nx[:])
+    for i in range(2, 8):
+        D("y", R("sb", 0, 12, slice(16 * i, 16 * i + 16)), None, "dsu", False, inap=T.st[:])
+        D("s", R("sb", 12, 24, slice(16 * i, 16 * i + 16)), None, "dsu", i == 7, inap=T.bt[:])
+    D("y", R("xs", 4 * Z0, 2 * X0), None, "dx", inap=T.x[:, 0:2 * X0 - 4 * Z0])
     iota(R("pI"), [[1, 1]], 1, False)
-    fill(R("tba", P=Qd[1]), 0)
-    D("y", R("tba", P=Qd[2]), R("tba", P=Qd[1]), "dz", False)
-    D("y", R("tba", P=Qd[3]), R("tba", P=Qd[1]), "dz")
-    for i in range(2):
-        D("y", R("nxi", P=slice(16 * i, 16 * i + 16)), None, "dni", i == 1, inap=T.nx[:])
-    D("y", R("xs", 4 * Z0), None, "dx", inap=T.x[:])
-    iota(R("c16"), [[16, 12]])
     iota(R("j15"), [[0, 12], [1, 16]])
+    iota(R("c16"), [[16, 12]])
     iota(R("sg", 0, 36), [[0, 3], [1, 12]])
     iota(R("sg", 36, 132), [[0, 3], [1, 32]])
     iota(R("sg", 132, 141), [[0, 3], [1, 3]])
+    iota(R("sg", 141, 189), [[0, 12], [1, 4]])
     iota(R("ident", 0, 256), [[1, 256]])
     idn = R("ident")
 
     r15, p31, qf, ev, od = [col(i) for i in range(5)]
+    off0, stu = R("lx", 0, 12), R("lx", 12, 24)
+    for P in (Qd[1], upper):
+        fill(R("tba", 0, 8, P), 0)
+    fill(off0, 0)
+    fill(R("M1"), 0)
+    fill(R("xs", 0, 4 * Z0), 0.0)
     ts(R("ci", 0, 1), R("pI"), 15, None, A.bitwise_and)
     ts(R("ci", 1, 2), R("pI"), 31, None, A.bitwise_and)
     ts(R("ci", 2, 3), R("pI"), 5, None, A.arith_shift_right)
     cp(R("cf", 0, 3), R("ci", 0, 3))
-    sti, bti = R("sb", 0, 12), R("sb", 12, 24)
-    cp(R("sb", P=Qd[1]), R("sb", P=Qd[0]))
-    cp(R("sb", P=upper), R("sb", P=lower))
-
-    def l0(i):
-        return R("l0", 12 * i, 12 * i + 12)
-    off0, stu = R("lx", 0, 12), R("lx", 12, 24)
-    ts(l0(0), bti, 1, None, A.bitwise_and)
-    ts(l0(1), sti, 2.0, None, A.mult)
-    ts(l0(6), bti, 1, None, A.arith_shift_right)
-    tt(l0(2), l0(1), l0(0), A.add)
     ts(R("mask"), R("j15"), r15, None, A.is_equal)
-    ts(l0(3), l0(2), 4, None, A.arith_shift_right)
-    ts(l0(4), l0(2), 64.0, None, A.mult)
-    cp(stu, sti)
-    ts(l0(5), l0(3), -1023.0, None, A.mult)
-    cp(R("b2f"), l0(6))
-    tt(l0(2), l0(4), l0(5), A.add)
-    cp(R("stf"), sti)
-    cp(off0, l0(2))
+    ts(R("mask2"), R("j15"), r15, 2.0, A.is_equal, A.mult)
+    ts(R("maskb"), R("j15", 0, 32), p31, None, A.is_gt)
+    ts(ev, p31, 16.0, None, A.is_lt)
+
+    sti = R("sb", 0, 12)
+    st0, bt0 = R("sb", 0, 12, q0), R("sb", 12, 24, q0)
+    la, lb, b2 = [R("l0", 12 * i, 12 * i + 12, q0) for i in range(3)]
+    fb, fc, fd, fe = [R("lf", 12 * i, 12 * i + 12, q0) for i in range(4)]
+    ts(la, st0, 3, None, A.arith_shift_right)
+    ts(lb, bt0, 1, None, A.bitwise_and)
+    ts(fb, st0, 2.0, None, A.mult)
+    ts(fc, la, -1023.0 / 64, None, A.mult)
+    tt(fd, fb, lb, A.add)
+    cp(R("nxf", P=q0), R("nxi", P=q0))
+    tt(fe, fd, fc, A.add)
+    turn(R("nxt", P=q0), R("nxf", P=q0))
+    ts(R("lx", 0, 12, q0), fe, 64.0, None, A.mult)
 
     ac(R("seg"), R("j15"), fn=AF.Sign)
-    ac(R("sg", 0, 141), R("sg", 0, 141), fn=AF.Sign)
+    ac(R("sg", 0, 189), R("sg", 0, 189), fn=AF.Sign)
     ac(R("i16"), R("c16", 0, 12), bias=r15)
-    ac(R("tri"), R("i16"), bias=192.0)
+    for n in ("xa", "xb"):
+        ac(R(n, 3, 48, every, 4), R("i16"), bias=192.0)
     for d in range(3):
         ac(col(8 + d), r15, scale=191.0, bias=15.0 - 192 + C * d)
     ac(R("ident", 256, 512), R("ident", 0, 256), bias=256.0)
     ac(R("ident", 512, 1024), R("ident", 0, 512), bias=512.0)
     ac(R("ident", 1024, 1104), R("ident", 0, 80), bias=1024.0)
 
-    tt(R("n1m"), ind(R("tba"), off0), R("mask"), A.mult)
-    cp(R("nxf", P=Qd[0]), R("nxi", P=Qd[0]))
-    fill(R("M1"), 0)
+    tt(R("n1m"), ind(R("tba"), off0), R("mask2"), A.mult)
+    ts(b2, bt0, 1, None, A.arith_shift_right)
+    cp(stu, sti)
     scan(R("n1s"), R("seg"), R("n1m"))
-    turn(R("nxt", P=Qd[0]), R("nxf", P=Qd[0]))
-    n1v = ends("n1s", Qd[0])
-    ts(R("E1x", P=QM), n1v, 2.0, None, A.mult)
-    for q in range(2):
-        ts(R("t1", P=Qd[q]), n1v, 1.0 / 512, -255.5 / 512, A.mult, A.add)
-    tt(R("E1", P=QM), R("E1x", P=QM), R("b2f", P=QM), A.add)
-    ts(R("maskb"), R("j15", 0, 32), p31, None, A.is_gt)
-    for q in range(2, 4):
-        ts(R("t1", P=Qd[q]), n1v, 1.0 / 512, -255.5 / 512, A.mult, A.add)
-    cp(R("M1", P=QM), R("E1", P=QM))
+    n1v = ends("n1s", q0)
+    cp(R("stf"), sti)
+    tt(R("E1", P=q0), n1v, b2, A.add)
+    for q in range(4):
+        ts(R("t1", P=Qd[q]), n1v, 1.0 / 1024, -255.5 / 512, A.mult, A.add)
+    cp(R("M1", P=QM), R("E1", P=q0))
     send("ma", lambda k: R("M1"))
     co(R("tb", 0, 4), 4096.0)
     co(R("tb", 1028, 1032), 4096.0)
-    for i in range(2):
-        D("y", ("tbd", 0, 1, 512 * i, 512 * i + 512, 1), R("nxt", 32 * i, 32 * i + 16, Qd[0]), "dtd", i == 1)
-    for i in range(16):
-        D("y", R("tb", 4, 1028, slice(i, i + 1)), ("tbd", 0, 1, 0, 1024, 1), "dtr", i == 15)
-    for i in range(1, 8):
-        D("y", R("tb", 4, 1028, slice(16 * i, 16 * i + 16)), R("tb", 4, 1028, slice(0, 16)), "dtq", i == 7)
-    D("y", R("ws", 0, 2048), None, "dw0", inap=T.w[:, 0:2048])
-    D("y", R("ws", 2048, 3072), None, "dw1", inap=T.w[:, 2048:3072])
+    for i in range(8):
+        for h in range(2):
+            D("y", R("tb", 4 + 512 * h, 516 + 512 * h, slice(i, i + 1)), R("nxt", 32 * h, 32 * h + 16, q0), "dtr", i == 7 and h == 1)
+    D("y", R("xs", 2 * X0, 4 * X0), None, "dx1", inap=T.x[:, 2 * X0 - 4 * Z0:2048])
+    for i in range(1, 16):
+        D("y", R("tb", 4, 1028, slice(8 * i, 8 * i + 8)), R("tb", 4, 1028, slice(0, 8)), "dtq", i == 15)
+    D("y", R("ws", 0, 1024), None, "dw0", inap=T.w[:, 0:1024])
 
     ac(R("val1"), ind(idn, stu), bias=float(Z0))
     co(R("w1", 0, 192), 0.0)
@@ -352,8 +353,11 @@ def rank_program(g, core, T, topo):
         gap()
         for j in range(3):
             last = R(s, 12 * j + 11, 12 * j + 12)
-            if cross:
-                ts(part(bb, j, 32), R("maskb"), last, R("g9", 11 + 3 * j, 12 + 3 * j), A.mult, A.add)
+            before = R("g9", 11 + 3 * j, 12 + 3 * j) if cross else None
+            if j == 2 and cross:
+                ac(part(bb, j, 32), R("maskb"), scale=last, bias=before)
+            elif cross:
+                ts(part(bb, j, 32), R("maskb"), last, before, A.mult, A.add)
             else:
                 ts(part(bb, j, 32), R("maskb"), last, None, A.mult)
         gap()
@@ -364,20 +368,14 @@ def rank_program(g, core, T, topo):
         for j in range(3):
             ts(part(pp, j), part(s, j), R(rr, 32 * j + 31, 32 * j + 32), col(kc + j), A.add, A.add)
         gap()
-        tt(R(xx, 0, 36), R(pp), R(eq, 36, 72), A.mult)
+        for j in range(3):
+            tt(R(xx, j, 48, every, 4), part(pp, j), part(eq, 3 + j), A.mult)
         gap()
-        tt(part(xx, 4), part(xx, 2), R("tri"), A.add)
-        tt(part(xx, 3), part(xx, 0), part(xx, 1), A.add)
-        gap()
-        tt(part(xx, 5), part(xx, 3), part(xx, 4), A.add)
-        return part(xx, 5)
-
-    def zeros():
-        fill(R("xs", 0, 4 * Z0), 0.0)
-        ts(ev, p31, 16.0, None, A.is_lt)
+        scan(R(xx, 48, 96), R("sg", 141, 189), R(xx, 0, 48))
+        return R(xx, 51, 96, every, 4)
 
     def own():
-        ts(R("off", P=QM), R("E1", P=QM), 4.0 - 1024 * rank, 1028.0, A.add, A.min)
+        ts(R("off", P=QM), R("E1", P=q0), 4.0 - 1024 * rank, 1028.0, A.add, A.min)
 
     def qx(i):
         return lambda: quant(R("QX", 130 * i, 130 * i + 130), R("SX", 130 * i, 130 * i + 130), R("xs", 520 * i, 520 * i + 520))
@@ -386,18 +384,17 @@ def rank_program(g, core, T, topo):
         return lambda: quant(R("WQ", 128 * i, 128 * i + 128), R("WS", 128 * i, 128 * i + 128), R("ws", 512 * i, 512 * i + 512))
 
     z1 = classes(R("t1"), "eqa", "sa", "ba", "bta", "ra", "pa", "xa", 8, False,
-                 [zeros, own, lambda: ts(R("maskc"), R("ident", 0, 32), p31, None, A.is_gt)] + [qx(i) for i in range(4)])
+                 [own, lambda: ts(R("maskc"), R("ident", 0, 32), p31, None, A.is_gt), lambda: None] + [qx(i) for i in range(4)])
     slot1 = R("sl", 0, 12)
     cp(slot1, z1)
     ac(R("MP"), z1)
     send("mp", lambda k: R("MP"))
     ac(od, ev, scale=-1.0, bias=1.0)
     ac(col(6), ev, scale=float(Z0))
-    ac(col(7), qf, scale=262144.0)
+    ac(col(7), qf, scale=524288.0)
     ac(col(15), col(7), scale=od)
     for d in range(3):
         ac(col(11 + d), qf, scale=3072.0, bias=col(8 + d))
-    ac(col(14), qf, scale=192.0, bias=-288.0)
     ac(R("park"), R("i16"), bias=288.0)
     ac(R("K2"), R("i16"), scale=od, bias=col(6))
     co(R("g9", 0, 9), 0.0)
@@ -406,45 +403,46 @@ def rank_program(g, core, T, topo):
 
     scatter(R("w1"), slot1, R("val1"))
     tt(R("f1", 0, 192), R("w1", 0, 192), R("mask"), A.mult)
+    for k, d in enumerate(oth):
+        ts(R("off", P=Qd[d]), R("A1", 12 * k, 12 * k + 12, Qd[d]), 4.0 - 1024 * rank, 1028.0, A.add, A.min)
     scan(R("f1", 192, 384), R("seg"), R("f1", 0, 192))
+    ts(R("c1i"), R("off"), 0.5, Z0 - 2.25, A.mult, A.add)
     cp(R("stl"), ends("f1", a=192))
+    tt(R("n2m"), ind(R("tb"), R("off")), R("mask"), A.mult)
     pickq(R("Q1"), R("QX"), R("stl"))
     picks(R("S1"), R("SX"), R("stl"))
+    D("s", R("ws", 1024, 3072), None, "dw1", inap=T.w[:, 1024:3072])
     send("qa", block("Q1"), True)
     send("sa", block("S1"))
     D("y", R("W1", 0, X0), R("QX"), "dq1", False, outap=u8(ap(R("W1", 0, X0))), inap=u8(ap(R("QX"))))
     D("y", R("P1", 0, X0), R("SX"), "dq1")
     D("y", R("W2", 0, X1), R("W1", 0, X1), "dq2", False, outap=u8(ap(R("W2", 0, X1))), inap=u8(ap(R("W1", 0, X1))))
     D("y", R("P2", 0, X1), R("P1", 0, X1), "dq2")
-
-    for k, d in enumerate(oth):
-        ts(R("off", P=Qd[d]), R("A1", 12 * k, 12 * k + 12, Qd[d]), 4.0 - 1024 * rank, 1028.0, A.add, A.min)
-    tt(R("n2m"), ind(R("tb"), R("off")), R("mask"), A.mult)
-    ts(R("c1i"), R("off"), 0.5, Z0 - 2.25, A.mult, A.add)
     scan(R("n2s"), R("seg"), R("n2m"))
     cp(R("c1u"), R("c1i"))
     n2v = ends("n2s")
     ts(R("t2"), n2v, 1.0 / 512, -255.5 / 512, A.mult, A.add)
-    ac(R("uf1"), ind(idn, R("c1u")), scale=1024.0)
+    ac(R("uf1"), ind(idn, R("c1u")), scale=2048.0)
     ac(R("n2k"), n2v, scale=2048.0, bias=float(X1))
     z2 = classes(R("t2"), "eqb", "sc", "bb", "btb", "rb", "pb", "xb", 11, True,
-                 [lambda: ts(R("c1o"), R("c1i"), od, float(-X1), A.mult, A.add)] + [wq(i) for i in range(6)])
+                 [lambda: ts(R("c1o"), R("c1i"), od, float(-X1), A.mult, A.add), wq(0), wq(1)])
     for k, d in enumerate(oth):
         ac(R("L0f", P=Qd[d]), R("AP", 12 * k, 12 * k + 12, Qd[d]), bias=float(X0))
     ac(R("L0e"), R("L0f"), scale=ev)
     tt(R("M2"), R("n2k"), z2, A.add)
     send("mz", lambda k: R("M2"))
-    cp(R("L0u"), R("L0f"))
     slot2 = R("sl", 12, 24)
     cp(slot2, z2)
+    cp(R("L0u"), R("L0f"))
     tt(R("val2"), ind(idn, R("L0u")), R("uf1"), A.add)
+    wq(2)()
     scatter(R("w2"), slot2, R("val2"))
     tt(R("SBm"), R("L0e"), R("c1o"), A.add)
     co(R("pw", 0, 288), 0.0)
     co(R("PZ"), 0.0)
     co(R("g3", 0, 3), 0.0)
     co(R("F32"), 0.0)
-    co(R("idt"), 0.0)
+    near, far0, far1 = sorted(range(N - 1), key=lambda k: topo.chip(cores[oth[k]]) != topo.chip(core))
     tc = [R("tc", 32 * i, 32 * i + 32) for i in range(7)]
 
     def s0():
@@ -455,22 +453,23 @@ def rank_program(g, core, T, topo):
 
     def s1():
         scan(R("f2", 192, 384), R("seg"), R("f2", 0, 192))
+        wq(3)()
 
     def e1():
-        tt(R("Zf", 12, 24), R("Zf", 0, 12), landed("mz", 0), A.min)
+        tt(R("Zf", 12, 24), R("Zf", 0, 12), landed("mz", near), A.min)
 
     def s2():
         for q in (1, 3, 0, 2):
             (ac if q % 2 else cp)(R("hg", 0, 12, Qd[q]), ends("f2", Qd[q ^ 1], a=192))
 
     def e2():
-        tt(R("Zf", 24, 36), R("Zf", 12, 24), landed("mz", 1), A.min)
+        tt(R("Zf", 24, 36), landed("mz", far0), landed("mz", far1), A.min)
 
     def s3():
         tt(R("hg", 12, 24), ends("f2", a=192), R("hg", 0, 12), A.add)
 
     def e3():
-        tt(R("Zi", 0, 12), R("Zf", 24, 36), landed("mz", 2), A.min)
+        tt(R("Zi", 0, 12), R("Zf", 24, 36), R("Zf", 12, 24), A.min)
 
     def s4():
         ac(R("hg", 24, 36, upper), R("hg", 12, 24, lower))
@@ -485,19 +484,19 @@ def rank_program(g, core, T, topo):
         tt(R("fa", 0, 12), R("hg", 12, 24), R("hg", 24, 36), A.add)
 
     def e5():
-        ts(R("PZ", 0, 12), R("Zi", 12, 24), float(rank), -1.0, A.is_equal, A.add)
+        ts(R("PZ", 0, 12), R("Zi", 12, 24), float(rank), None, A.is_equal)
+        ac(R("pr"), R("PZ", 0, 12), scale=-1024.0)
         ts(R("ze", 0, 12), R("Zi", 24, 36), ev, None, A.mult)
 
     def s6():
-        ts(R("fa", 12, 24), R("fa", 0, 12), 10, None, A.arith_shift_right)
-        ts(R("fa", 24, 36), R("fa", 0, 12), 1023, None, A.bitwise_and)
+        ts(R("l34", 0, 12), R("fa", 0, 12), 1.0 / 2048, None, A.mult)
+        ts(R("fa", 24, 36), R("fa", 0, 12), 2047, None, A.bitwise_and)
 
     def e6():
         turn(tc[0], R("PZ"))
         tt(R("ze", 12, 24), R("ze", 0, 12), R("K2"), A.add)
 
     def s7():
-        cp(R("l34", 0, 12), R("fa", 12, 24))
         cp(R("l34", 12, 24), R("fa", 24, 36))
 
     def e7():
@@ -512,11 +511,11 @@ def rank_program(g, core, T, topo):
     def e8():
         for a, b, n, c, v in ((32, 0, 32, 1, 0), (64, 32, 32, 2, 0), (64, 0, 64, 0, 1), (96, 64, 32, 1, 1), (96, 0, 32, 2, 1)):
             (cp if v else ac)(R("g3", c, c + 1, slice(a, a + n)), R("tc", 47, 48, slice(b, b + n)))
-        ts(R("pr"), R("Zi", 12, 24), float(rank), None, A.is_equal)
+        tt(R("pz", 0, 12), R("park"), R("pr"), A.add)
 
     def e9():
         scan(R("g3", 3, 6), R("sg", 132, 135), R("g3", 0, 3))
-        ac(R("uf2"), ind(idn, R("zl", 12, 24)), scale=1024.0, bias=col(15))
+        ac(R("uf2"), ind(idn, R("zl", 12, 24)), scale=2048.0, bias=col(15))
 
     def s9():
         pickq(R("Q4"), R("W1", 0, X1), R("l34", 12, 24))
@@ -530,65 +529,58 @@ def rank_program(g, core, T, topo):
     cp(R("zl", 0, 12), R("Zi", 36, 48))
     ts(tc[2], R("maskc"), R("tc", 47, 48), R("g3", 5, 6), A.mult, A.add)
     turn(tc[3], tc[2])
+    wq(4)()
     scan(tc[4], R("sg", 36, 68), tc[3])
-    ts(tc[5], tc[1], R("tc", 159, 160), col(14), A.add, A.add)
+    wq(5)()
+    ts(tc[5], tc[1], R("tc", 159, 160), -1.0, A.add, A.add)
     turn(tc[6], tc[5])
     tt(R("val3"), ind(idn, R("zl", 0, 12)), R("uf2"), A.add)
-    tt(R("pz", 0, 12), R("tc", 192, 204), R("pr"), A.mult)
-    tt(R("pz", 12, 24), R("pz", 0, 12), R("park"), A.add)
+    tt(R("pz", 12, 24), R("tc", 192, 204), R("pz", 0, 12), A.max)
     slot3 = R("sl", 24, 36)
     cp(slot3, R("pz", 12, 24))
     scatter(R("pw"), slot3, R("val3"))
     turn(R("f3"), R("pw", 0, 288))
     for q in (1, 3, 0, 2):
         (ac if q % 2 else cp)(R("hm", P=Qd[q]), R("f3", 0, 288, Qd[q ^ 1], 16))
-    tt(R("F32", 0, 18), R("f3", 0, 288, every, 16), R("hm"), A.add)
+    for k in range(2):
+        tt(R("F32", 16 * k, 16 * k + 9), R("f3", 16 * k, 288, every, 32), R("hm", k, 18, every, 2), A.add)
     turn(R("TF"), R("F32"))
     ac(R("hx", P=upper), R("TF", P=lower))
     cp(R("hx", P=lower), R("TF", P=upper))
     for i in range(4):
-        a = 16 * (i // 2)
-        tt(R("DD", 16 * i, 16 * i + 16), R("TF", a, a + 16), R("hx", a, a + 16), A.add)
+        h = i // 2
+        tt(R("DD", 16 * i, 16 * i + 16), R("TF", h, 32, every, 2), R("hx", h, 32, every, 2), A.add)
     turn(R("LT"), R("DD"))
-    for i in range(4):
-        o, h = i % 2, i // 2
-        cp(R("li", 18 * o + h, 18 * o + 18, every, 2), R("LT", 32 * h + o, 32 * h + 18, every, 2))
-    li, lh, ll = R("li", 0, 36), R("li", 36, 72), R("li", 72, 108)
-    ts(lh, li, 10, None, A.arith_shift_right)
-    ts(ll, li, 1023, None, A.bitwise_and)
-    cp(R("HU"), R("li", 36, 54))
-    cp(R("LU"), ll)
+    tt(R("SS"), R("TF"), R("hx"), A.add)
+    ts(R("HU"), R("LT"), 1.0 / 2048, None, A.mult)
+    ts(R("li"), R("LT"), 2047, None, A.bitwise_and)
+    ts(R("idi", 0, 32), R("SS"), 19, None, A.arith_shift_right)
+    ts(R("idi", 32, 64), R("SS"), 11, 255, A.arith_shift_right, A.bitwise_and)
+    ts(R("idi", 64, 96), R("SS"), 1.0, -1.0, A.is_ge, A.add)
 
-    def products(i, q, s, a, b):
+    def products(i, q, s, h):
         for o in range(O):
-            c, d = 128 * ((2 - i) * O + o), 512 * (2 * o + (1 if a else 0))
-            E("t", [R(q, a, b), R(s, a, b), R("WQ", c, c + 128), R("WS", c, c + 128)], [R("ps", d, d + b - a)] if i == 2 else [],
-              lambda e: e.matmul_mx(ap(R("ps", d, d + b - a)), ap(R("WQ", c, c + 128)), ap(R("WS", c, c + 128)), ap(R(q, a, b)), ap(R(s, a, b)), i == 0, i == 2))
+            c, d = 128 * ((2 - i) * O + o), 512 * (2 * o + h)
+            a, b = L * h, L * h + L
+            E("t", [R(q, a, b), R(s, a, b), R("WQ", c, c + 128), R("WS", c, c + 128)], [R("ps", d, d + L)] if i == 2 else [],
+              lambda e: e.matmul_mx(ap(R("ps", d, d + L)), ap(R("WQ", c, c + 128)), ap(R("WS", c, c + 128)), ap(R(q, a, b)), ap(R(s, a, b)), i == 0, i == 2))
 
-    for i, (q, s, w, p, l) in enumerate((("G2", "H2", R("QX"), R("SX"), R("HU")), ("G1", "H1", R("W1"), R("P1"), R("LU", 18, 36)))):
-        pickq(R(q), w, l)
-        picks(R(s), p, l)
-        for a, b in ((0, H), (H, M)):
-            products(i, q, s, a, b)
-    for a, b in ((0, H), (H, M)):
-        l = R("LU", a // 16, b // 16)
-        pickq(R("G0", a, b), R("W2"), l)
-        picks(R("H0", a, b), R("P2"), l)
-        products(2, "G0", "H0", a, b)
-    ii = R("idi", 0, 18), R("idi", 18, 36), R("idi", 36, 54)
-    ts(ii[0], R("li", 18, 36), 18, None, A.arith_shift_right)
-    ts(ii[1], R("li", 54, 72), 255, None, A.bitwise_and)
-    ts(ii[2], R("li", 18, 36), 1.0, -1.0, A.is_ge, A.add)
-    cp(R("ysb", 0, H), R("ps", 0, H))
-    ac(R("ysb", M, M + H), R("ps", 1024, 1024 + H))
-    tt(R("idt", 0, 18), ii[0], ii[2], A.add)
-    tt(R("idt", 32, 50), ii[1], ii[2], A.add)
-    cp(R("ysb", H, M), R("ps", 512, 512 + M - H))
-    ac(R("ysb", M + H, 2 * M), R("ps", 1536, 1536 + M - H))
+    for i, (q, s, w, p, l, a) in enumerate((("G2", "H2", R("QX"), R("SX"), "HU", 0), ("G1", "H1", R("W1"), R("P1"), "LU", 16), ("G0", "H0", R("W2"), R("P2"), "LU", 0))):
+        for h in range(2):
+            lst = R(l, 32 * h + a, 32 * h + a + 9)
+            pickq(R(q, L * h, L * h + L), w, lst)
+            picks(R(s, L * h, L * h + L), p, lst)
+            products(i, q, s, h)
+            if i == 0 and h == 0:
+                cp(R("LU"), R("li"))
+    tt(R("idt", 0, 32), R("idi", 0, 32), R("idi", 64, 96), A.add)
+    tt(R("idt", 32, 64), R("idi", 32, 64), R("idi", 64, 96), A.add)
+    for h in range(2):
+        cp(R("ysb", h, M, every, 2), R("ps", 512 * h, 512 * h + L))
+        ac(R("ysb", M + h, 2 * M, every, 2), R("ps", 1024 + 512 * h, 1024 + 512 * h + L))
+    for o in range(2):
+        D("y", None, R("idt", 32 * o, 32 * o + 32, slice(16, 25)), "di%d" % o, outap=T.id[o:o + 1, :])
     D("y", None, R("ysb", 0, M), "dy0", outap=T.y[:, 0:M])
     D("s", None, R("ysb", M, 2 * M), "dy1", outap=T.y[:, M:2 * M])
-    turn(R("idx"), R("idt"))
-    D("y", None, R("idx", 0, 16, slice(0, 18)), "di0", outap=T.id[0:1, :])
-    D("y", None, R("idx", 32, 48, slice(0, 18)), "di1", outap=T.id[1:2, :])
 
     wait("g", [(q, cnt[q]) for q in ("v", "s", "t", "g")] + [("loc", loc[0])] + [(s, dsum[s]) for s in DMAS] + arrivals)

from concourse.bass import DstId, RemoteDMATransfer
from concourse.mybir import dt, AluOpType as A, ActivationFunctionType as AF

N, V, M, O = 4, 192, 288, 2
C = 64
Z0 = 8
X0 = Z0 + 512
X1 = X0 + 192
L = M // 2
F, I, U, B = "float32", "int32", "uint16", "bfloat16"
Q8, S8 = "float8_e4m3fn_x4", "uint8"


def _sb(w, d):
    return ("sbuf", [128, w], d)


SCRATCH = {
    "tba": _sb(1024, I), "tb": _sb(1032, F), "sb": _sb(24, I), "nxi": _sb(64, I), "nxf": _sb(64, F), "nxt": _sb(64, F),
    "xs": _sb(4 * X0, B), "ws": _sb(3072, B),
    "QX": _sb(X0, Q8), "SX": _sb(X0, S8), "W1": _sb(X1 + 192, Q8), "P1": _sb(X1 + 192, S8), "W2": _sb(X1 + 192, Q8), "P2": _sb(X1 + 192, S8),
    "WQ": _sb(768, Q8), "WS": _sb(768, S8),
    "Q1": _sb(192, Q8), "S1": _sb(192, S8), "Q3": _sb(192, Q8), "S3": _sb(192, S8), "Q4": _sb(192, Q8), "S4": _sb(192, S8),
    "G0": _sb(288, Q8), "H0": _sb(288, S8), "G1": _sb(288, Q8), "H1": _sb(288, S8), "G2": _sb(288, Q8), "H2": _sb(288, S8),
    "j15": _sb(192, F), "pI": _sb(1, I), "c16": _sb(12, F), "ident": _sb(1104, F), "mask": _sb(192, F), "mask2": _sb(192, F), "seg": _sb(192, F), "maskb": _sb(32, F),
    "maskc": _sb(32, F), "sg": _sb(192, F), "ci": _sb(4, I), "cf": _sb(24, F), "i16": _sb(12, F), "park": _sb(12, F), "K2": _sb(12, F),
    "l0": _sb(36, I), "lf": _sb(48, F), "lx": _sb(24, U), "stf": _sb(12, F),
    "val1": _sb(192, F), "n1m": _sb(192, F), "n1s": _sb(192, F), "t1": _sb(12, I), "E1": _sb(12, F), "M1": _sb(12, U), "A1": _sb(36, U),
    "MP": _sb(12, B), "AP": _sb(36, B),
    "eqa": _sb(72, F), "sa": _sb(36, F), "ba": _sb(96, F), "bta": _sb(96, F), "ra": _sb(96, F), "pa": _sb(36, F), "xa": _sb(96, F),
    "eqb": _sb(72, F), "sc": _sb(36, F), "bb": _sb(96, F), "btb": _sb(96, F), "rb": _sb(96, F), "pb": _sb(36, F), "xb": _sb(96, F), "g9": _sb(18, F),
    "sl": _sb(36, U), "w1": _sb(384, F), "w2": _sb(384, F), "pw": _sb(480, F), "f1": _sb(384, F), "f2": _sb(384, F), "f3": _sb(288, F),
    "stl": _sb(12, U), "off": _sb(12, U), "n2m": _sb(192, F), "n2s": _sb(192, F), "t2": _sb(12, I), "c1i": _sb(12, I), "c1u": _sb(12, U), "c1o": _sb(12, F),
    "L0f": _sb(12, F), "L0e": _sb(12, F), "L0u": _sb(12, U), "SBm": _sb(12, F), "n2k": _sb(12, F), "M2": _sb(12, F), "A2": _sb(36, F), "uf1": _sb(192, F), "val2": _sb(192, F),
    "hg": _sb(36, F), "fa": _sb(48, I), "l34": _sb(24, U),
    "Zf": _sb(36, F), "Zi": _sb(48, I), "zl": _sb(24, U), "ze": _sb(24, F), "uf2": _sb(192, F), "val3": _sb(192, F), "pr": _sb(12, F), "PZ": _sb(32, F),
    "tc": _sb(224, F), "g3": _sb(6, F), "pz": _sb(24, F), "hm": _sb(18, F), "F32": _sb(32, F), "TF": _sb(32, F), "hx": _sb(32, F), "DD": _sb(64, I), "LT": _sb(64, I),
    "SS": _sb(32, I), "li": _sb(64, I), "LU": _sb(64, U), "HU": _sb(64, U), "idi": _sb(96, I), "idt": _sb(64, F), "ysb": _sb(576, F),
    "ps": ("psum", [128, 2048], F),
}
DMAS = ["dnx", "dst", "dsu", "dx", "dx1", "dw0", "dw1", "dni", "dtr", "dtq", "dq1", "dq2", "dy0", "dy1", "di0", "di1"]
HOPS = ("ma", "mp", "qa", "sa", "mz", "qb", "sb", "qc", "sc")
SEMAPHORES = ["v", "s", "t", "g", "loc"] + DMAS + [n + str(k) for n in HOPS for k in range(N - 1)]


def plan(topo, src, cores):
    dsts = [c for c in cores if c != src]
    off = [c for c in dsts if topo.chip(c) != topo.chip(src)]
    on = [c for c in dsts if topo.chip(c) == topo.chip(src)]
    out, used = {}, []
    for grp in (off, on):
        if not grp:
            continue
        free = [e for e in topo.engines(src, grp[0]) if e not in used]
        w = 1
        while 2 * w * len(grp) <= len(free):
            w *= 2
        for i, c in enumerate(grp):
            out[c] = free[w * i:w * i + w]
        used = used + [e for c in grp for e in out[c]]
    return out


def rank_program(g, core, T, topo):
    rank = T.rank_of(core)
    if rank is None:
        return
    cores = list(T.cores)
    oth = [rank ^ (k + 1) for k in range(N - 1)]
    eng = {"v": g.vector, "s": g.scalar, "t": g.tensor, "g": g, "y": g.sync}
    cnt = {q: 0 for q in eng}
    seen, writers, readers, dsum, pend, loc = {}, {}, {}, {}, {}, [0]
    Qd = [slice(32 * q, 32 * q + 32) for q in range(4)]
    lower, upper, every = slice(0, 64), slice(64, 128), slice(0, 128)
    QM, q0 = Qd[rank], Qd[0]

    def R(name, a=0, b=None, P=every, st=1):
        return (name, P.start, P.stop, a, SCRATCH[name][1][1] if b is None else b, st)

    def ind(win, off):
        return ("ind", win, off)

    def ap(x):
        if x[0] == "ind":
            return ap(x[1]).indirect(ap(x[2]))
        if x[5] == 1:
            return T[x[0]][x[1]:x[2], x[3]:x[4]]
        return T[x[0]][x[1]:x[2], x[3]:x[4]:x[5]]

    def flat(xs):
        out = []
        for x in xs:
            if isinstance(x, tuple):
                out += flat(x[1:]) if x[0] == "ind" else [x]
        return out

    def meet(x, y):
        if x[1] >= y[2] or y[1] >= x[2] or x[3] >= y[4] or y[3] >= x[4]:
            return False
        return not (x[5] == y[5] and (x[3] - y[3]) % x[5])

    def inside(x, y):
        return y[1] <= x[1] and x[2] <= y[2] and y[3] <= x[3] and x[4] <= y[4] and (y[5] == 1 or y == x)

    def wait(q, toks):
        need = {}
        for sem, val in toks:
            if val > seen.get((q, sem), 0):
                need[sem] = max(need.get(sem, 0), val)
        for sem in need:
            eng[q].wait_ge(T.sem[sem], need[sem])
            seen[(q, sem)] = need[sem]

    def deps(q, rs, ws):
        toks = []
        for x in rs + ws:
            toks += [t for y, t in writers.get(x[0], []) if meet(x, y)]
        for x in ws:
            toks += [t for y, t in readers.get(x[0], []) if meet(x, y) and t[0] != q]
        wait(q, toks)

    def done(tok, rs, ws):
        for x in rs:
            readers.setdefault(x[0], []).append((x, tok))
        for x in ws:
            writers[x[0]] = [e for e in writers.get(x[0], []) if not inside(e[0], x)] + [(x, tok)]
            readers[x[0]] = [e for e in readers.get(x[0], []) if not inside(e[0], x)]

    def E(q, rs, ws, fn):
        rs, ws = flat(rs), flat(ws)
        deps(q, rs, ws)
        fn(eng[q]).then_inc(T.sem[q], 1)
        cnt[q] += 1
        done((q, cnt[q]), rs, ws)

    def D(q, out, in_, sem, fin=True, outap=None, inap=None):
        rs, ws = flat([in_]), flat([out])
        deps(q, rs, ws)
        eng[q].dma_start(ap(out) if outap is None else outap, ap(in_) if inap is None else inap).then_inc(T.sem[sem], 16)
        dsum[sem] = dsum.get(sem, 0) + 16
        pend.setdefault(sem, []).append((rs, ws))
        if fin:
            for rs, ws in pend.pop(sem):
                done((sem, dsum[sem]), rs, ws)

    mine = plan(topo, core, cores)

    def u8(v):
        return v.bitcast(dt.uint8)

    def u32(v):
        return v.bitcast(dt.uint32)

    land = {"ma": ("A1", 0, 12), "mp": ("AP", 0, 12), "qa": ("W1", X0, C), "sa": ("P1", X0, C), "mz": ("A2", 0, 12),
            "qb": ("W1", X1, C), "sb": ("P1", X1, C), "qc": ("W2", X1, C), "sc": ("P2", X1, C)}

    def landed(h, k):
        n, a, w = land[h]
        return R(n, a + w * k, a + w * k + w)

    def send(h, src, codes=False):
        deps("g", flat([src(k) for k in range(N - 1)]), [])
        tr = []
        for k, d in enumerate(oth):
            rid, pid, _ = topo.addr(cores[d])
            es = mine[cores[d]]
            loc[0] += len(es)
            s, t = ap(src(k)), ap(landed(h, k))
            tr.append(RemoteDMATransfer(dst_ids=[DstId(rid=rid, pnc=pid)], dma_engine_mask=sum(1 << e for e in es),
                                        remote_sem=T.sem[h + str(k)], srcs=[u8(s) if codes else s], dsts=[u8(t) if codes else t]))
        g.remote_dma_fused(tr, local_sem=T.sem.loc)

    def block(n):
        return lambda k: R(n, C * k, C * k + C)

    arrivals = []
    for h in HOPS:
        for k, d in enumerate(oth):
            tok = (h + str(k), len(plan(topo, cores[d], cores)[core]))
            arrivals.append(tok)
            writers.setdefault(land[h][0], []).append((landed(h, k), tok))

    def sc_(x):
        return ap(x) if isinstance(x, tuple) else x

    def ts(out, in0, s1, s2, o1, o2=None):
        if o2 is None:
            E("v", [in0, s1], [out], lambda e: e.tensor_scalar(ap(out), ap(in0), sc_(s1), None, o1))
        else:
            E("v", [in0, s1, s2], [out], lambda e: e.tensor_scalar(ap(out), ap(in0), sc_(s1), sc_(s2), o1, o2))

    def tt(out, a, b, op):
        E("v", [a, b], [out], lambda e: e.tensor_tensor(ap(out), ap(a), ap(b), op))

    def cp(out, in_):
        E("v", [in_], [out], lambda e: e.tensor_copy(ap(out), ap(in_)))

    def scatter(win, off, val):
        E("v", [off, val], [win], lambda e: e.tensor_copy(ap(win).indirect(ap(off)), ap(val)))

    def fill(out, c):
        E("v", [], [out], lambda e: e.memset(ap(out), c))

    def scan(out, d0, d1):
        E("v", [d0, d1], [out], lambda e: e.tensor_tensor_scan(ap(out), ap(d0), ap(d1), 0.0, A.mult, A.add))

    def turn(out, in_):
        E("v", [in_], [out], lambda e: e.transpose(ap(out), ap(in_)))

    def ac(out, in_, scale=None, bias=None, fn=None):
        f = fn or (AF.Copy if bias is None else AF.Identity)
        kw = {}
        if scale is not None:
            kw["scale"] = sc_(scale)
        if bias is not None:
            kw["bias"] = sc_(bias)
        E("s", [in_, scale, bias], [out], lambda e: e.activation(ap(out), ap(in_), f, **kw))

    def co(out, c):
        n = out[4] - out[3]
        ac(out, R("j15" if n <= 192 else "ident", 0, n, slice(out[1], out[2])), scale=0.0, bias=c)

    def iota(out, pattern, cm=0, flag=True):
        if flag:
            E("g", [], [out], lambda e: e.iota(ap(out), pattern, 0, cm, allow_small_or_imprecise_dtypes=True))
        else:
            E("g", [], [out], lambda e: e.iota(ap(out), pattern, 0, cm))

    def pickq(out, win, off):
        E("v", [win, off], [out], lambda e: e.tensor_copy(u32(ap(out)), u32(ap(win)).indirect(ap(off))))

    def picks(out, win, off):
        E("s", [win, off], [out], lambda e: e.activation(ap(out), ap(win).indirect(ap(off)), AF.Copy))

    def quant(q, s, in_):
        E("v", [in_], [q, s], lambda e: e.quantize_mx(ap(q), ap(s), ap(in_)))

    def col(i, P=every):
        return R("cf", i, i + 1, P)

    def ends(name, P=every, n=12, a=0):
        return R(name, a + 15, a + 16 * n, P, 16)

    for i in range(2):
        D("y", R("sb", 0, 12, slice(16 * i, 16 * i + 16)), None, "dst", False, inap=T.st[:])
        D("s", R("sb", 12, 24, slice(16 * i, 16 * i + 16)), None, "dst", i == 1, inap=T.bt[:])
    for i in range(2):
        D("ys"[i], R("nxi", P=slice(16 * i, 16 * i + 16)), None, "dni", i == 1, inap=T.nx[:])
    for i in range(16):
        D("y", R("tba", P=slice(i, i + 1)), None, "dnx", False, inap=T.nx[:])
        D("s", R("tba", P=slice(16 + i, 17 + i)), None, "dnx", i == 15, inap=T.nx[:])
    for i in range(2, 8):
        D("y", R("sb", 0, 12, slice(16 * i, 16 * i + 16)), None, "dsu", False, inap=T.st[:])
        D("s", R("sb", 12, 24, slice(16 * i, 16 * i + 16)), None, "dsu", i == 7, inap=T.bt[:])
    D("y", R("xs", 4 * Z0, 2 * X0), None, "dx", inap=T.x[:, 0:2 * X0 - 4 * Z0])
    iota(R("pI"), [[1, 1]], 1, False)
    iota(R("j15"), [[0, 12], [1, 16]])
    iota(R("c16"), [[16, 12]])
    iota(R("sg", 0, 36), [[0, 3], [1, 12]])
    iota(R("sg", 36, 132), [[0, 3], [1, 32]])
    iota(R("sg", 132, 141), [[0, 3], [1, 3]])
    iota(R("sg", 141, 189), [[0, 12], [1, 4]])
    iota(R("ident", 0, 256), [[1, 256]])
    idn = R("ident")

    r15, p31, qf, ev, od = [col(i) for i in range(5)]
    off0, stu = R("lx", 0, 12), R("lx", 12, 24)
    for P in (Qd[1], upper):
        fill(R("tba", 0, 8, P), 0)
    fill(off0, 0)
    fill(R("M1"), 0)
    fill(R("xs", 0, 4 * Z0), 0.0)
    ts(R("ci", 0, 1), R("pI"), 15, None, A.bitwise_and)
    ts(R("ci", 1, 2), R("pI"), 31, None, A.bitwise_and)
    ts(R("ci", 2, 3), R("pI"), 5, None, A.arith_shift_right)
    cp(R("cf", 0, 3), R("ci", 0, 3))
    ts(R("mask"), R("j15"), r15, None, A.is_equal)
    ts(R("mask2"), R("j15"), r15, 2.0, A.is_equal, A.mult)
    ts(R("maskb"), R("j15", 0, 32), p31, None, A.is_gt)
    ts(ev, p31, 16.0, None, A.is_lt)

    sti = R("sb", 0, 12)
    st0, bt0 = R("sb", 0, 12, q0), R("sb", 12, 24, q0)
    la, lb, b2 = [R("l0", 12 * i, 12 * i + 12, q0) for i in range(3)]
    fb, fc, fd, fe = [R("lf", 12 * i, 12 * i + 12, q0) for i in range(4)]
    ts(la, st0, 3, None, A.arith_shift_right)
    ts(lb, bt0, 1, None, A.bitwise_and)
    ts(fb, st0, 2.0, None, A.mult)
    ts(fc, la, -1023.0 / 64, None, A.mult)
    tt(fd, fb, lb, A.add)
    cp(R("nxf", P=q0), R("nxi", P=q0))
    tt(fe, fd, fc, A.add)
    turn(R("nxt", P=q0), R("nxf", P=q0))
    ts(R("lx", 0, 12, q0), fe, 64.0, None, A.mult)

    ac(R("seg"), R("j15"), fn=AF.Sign)
    ac(R("sg", 0, 189), R("sg", 0, 189), fn=AF.Sign)
    ac(R("i16"), R("c16", 0, 12), bias=r15)
    for n in ("xa", "xb"):
        ac(R(n, 3, 48, every, 4), R("i16"), bias=192.0)
    for d in range(3):
        ac(col(8 + d), r15, scale=191.0, bias=15.0 - 192 + C * d)
    ac(R("ident", 256, 512), R("ident", 0, 256), bias=256.0)
    ac(R("ident", 512, 1024), R("ident", 0, 512), bias=512.0)
    ac(R("ident", 1024, 1104), R("ident", 0, 80), bias=1024.0)

    tt(R("n1m"), ind(R("tba"), off0), R("mask2"), A.mult)
    ts(b2, bt0, 1, None, A.arith_shift_right)
    cp(stu, sti)
    scan(R("n1s"), R("seg"), R("n1m"))
    n1v = ends("n1s", q0)
    cp(R("stf"), sti)
    tt(R("E1", P=q0), n1v, b2, A.add)
    for q in range(4):
        ts(R("t1", P=Qd[q]), n1v, 1.0 / 1024, -255.5 / 512, A.mult, A.add)
    cp(R("M1", P=QM), R("E1", P=q0))
    send("ma", lambda k: R("M1"))
    co(R("tb", 0, 4), 4096.0)
    co(R("tb", 1028, 1032), 4096.0)
    for i in range(8):
        for h in range(2):
            D("y", R("tb", 4 + 512 * h, 516 + 512 * h, slice(i, i + 1)), R("nxt", 32 * h, 32 * h + 16, q0), "dtr", i == 7 and h == 1)
    D("y", R("xs", 2 * X0, 4 * X0), None, "dx1", inap=T.x[:, 2 * X0 - 4 * Z0:2048])
    for i in range(1, 16):
        D("y", R("tb", 4, 1028, slice(8 * i, 8 * i + 8)), R("tb", 4, 1028, slice(0, 8)), "dtq", i == 15)
    D("y", R("ws", 0, 1024), None, "dw0", inap=T.w[:, 0:1024])

    ac(R("val1"), ind(idn, stu), bias=float(Z0))
    co(R("w1", 0, 192), 0.0)

    def classes(t, eq, s, bb, bt, rr, pp, xx, kc, cross, fillers):
        def part(name, j, n=12):
            return R(name, n * j, n * j + n)

        def gap():
            if fillers:
                fillers.pop(0)()
        gap()
        for j, d in enumerate(oth):
            ts(part(eq, j), t, float(d), -16.0, A.is_equal, A.add)
        gap()
        scan(R(s), R("sg", 0, 36), R(eq, 0, 36))
        ac(R(eq, 36, 72), R(eq, 0, 36), bias=16.0)
        if cross:
            for a, b, n, c, v in ((64, 32, 32, 2, 0), (32, 0, 32, 1, 0), (64, 0, 64, 0, 1), (96, 64, 32, 1, 1), (96, 0, 32, 2, 1)):
                o, i_ = R("g9", c, 9, slice(a, a + n), 3), R(s, 11, 36, slice(b, b + n), 12)
                if v:
                    ts(o, i_, 0.5, None, A.mult)
                else:
                    ac(o, i_, scale=0.5)
            gap()
            scan(R("g9", 9, 18), R("sg", 132, 141), R("g9", 0, 9))
        gap()
        for j in range(3):
            last = R(s, 12 * j + 11, 12 * j + 12)
            before = R("g9", 11 + 3 * j, 12 + 3 * j) if cross else None
            if j == 2 and cross:
                ac(part(bb, j, 32), R("maskb"), scale=last, bias=before)
            elif cross:
                ts(part(bb, j, 32), R("maskb"), last, before, A.mult, A.add)
            else:
                ts(part(bb, j, 32), R("maskb"), last, None, A.mult)
        gap()
        turn(R(bt), R(bb))
        gap()
        scan(R(rr), R("sg", 36, 132), R(bt))
        gap()
        for j in range(3):
            ts(part(pp, j), part(s, j), R(rr, 32 * j + 31, 32 * j + 32), col(kc + j), A.add, A.add)
        gap()
        for j in range(3):
            tt(R(xx, j, 48, every, 4), part(pp, j), part(eq, 3 + j), A.mult)
        gap()
        scan(R(xx, 48, 96), R("sg", 141, 189), R(xx, 0, 48))
        return R(xx, 51, 96, every, 4)

    def own():
        ts(R("off", P=QM), R("E1", P=q0), 4.0 - 1024 * rank, 1028.0, A.add, A.min)

    def qx(i):
        return lambda: quant(R("QX", 130 * i, 130 * i + 130), R("SX", 130 * i, 130 * i + 130), R("xs", 520 * i, 520 * i + 520))

    def wq(i):
        return lambda: quant(R("WQ", 128 * i, 128 * i + 128), R("WS", 128 * i, 128 * i + 128), R("ws", 512 * i, 512 * i + 512))

    z1 = classes(R("t1"), "eqa", "sa", "ba", "bta", "ra", "pa", "xa", 8, False,
                 [own, lambda: ts(R("maskc"), R("ident", 0, 32), p31, None, A.is_gt), lambda: None] + [qx(i) for i in range(4)])
    slot1 = R("sl", 0, 12)
    cp(slot1, z1)
    ac(R("MP"), z1)
    send("mp", lambda k: R("MP"))
    ac(od, ev, scale=-1.0, bias=1.0)
    ac(col(6), ev, scale=float(Z0))
    ac(col(7), qf, scale=524288.0)
    ac(col(15), col(7), scale=od)
    for d in range(3):
        ac(col(11 + d), qf, scale=3072.0, bias=col(8 + d))
    ac(R("park"), R("i16"), bias=288.0)
    ac(R("K2"), R("i16"), scale=od, bias=col(6))
    co(R("g9", 0, 9), 0.0)
    ac(R("L0f", P=QM), R("stf", P=QM), bias=float(Z0))
    co(R("w2", 0, 192), 0.0)

    scatter(R("w1"), slot1, R("val1"))
    tt(R("f1", 0, 192), R("w1", 0, 192), R("mask"), A.mult)
    for k, d in enumerate(oth):
        ts(R("off", P=Qd[d]), R("A1", 12 * k, 12 * k + 12, Qd[d]), 4.0 - 1024 * rank, 1028.0, A.add, A.min)
    scan(R("f1", 192, 384), R("seg"), R("f1", 0, 192))
    ts(R("c1i"), R("off"), 0.5, Z0 - 2.25, A.mult, A.add)
    cp(R("stl"), ends("f1", a=192))
    tt(R("n2m"), ind(R("tb"), R("off")), R("mask"), A.mult)
    pickq(R("Q1"), R("QX"), R("stl"))
    picks(R("S1"), R("SX"), R("stl"))
    D("s", R("ws", 1024, 3072), None, "dw1", inap=T.w[:, 1024:3072])
    send("qa", block("Q1"), True)
    send("sa", block("S1"))
    D("y", R("W1", 0, X0), R("QX"), "dq1", False, outap=u8(ap(R("W1", 0, X0))), inap=u8(ap(R("QX"))))
    D("y", R("P1", 0, X0), R("SX"), "dq1")
    D("y", R("W2", 0, X1), R("W1", 0, X1), "dq2", False, outap=u8(ap(R("W2", 0, X1))), inap=u8(ap(R("W1", 0, X1))))
    D("y", R("P2", 0, X1), R("P1", 0, X1), "dq2")
    scan(R("n2s"), R("seg"), R("n2m"))
    cp(R("c1u"), R("c1i"))
    n2v = ends("n2s")
    ts(R("t2"), n2v, 1.0 / 512, -255.5 / 512, A.mult, A.add)
    ac(R("uf1"), ind(idn, R("c1u")), scale=2048.0)
    ac(R("n2k"), n2v, scale=2048.0, bias=float(X1))
    z2 = classes(R("t2"), "eqb", "sc", "bb", "btb", "rb", "pb", "xb", 11, True,
                 [lambda: ts(R("c1o"), R("c1i"), od, float(-X1), A.mult, A.add), wq(0), wq(1)])
    for k, d in enumerate(oth):
        ac(R("L0f", P=Qd[d]), R("AP", 12 * k, 12 * k + 12, Qd[d]), bias=float(X0))
    ac(R("L0e"), R("L0f"), scale=ev)
    tt(R("M2"), R("n2k"), z2, A.add)
    send("mz", lambda k: R("M2"))
    slot2 = R("sl", 12, 24)
    cp(slot2, z2)
    cp(R("L0u"), R("L0f"))
    tt(R("val2"), ind(idn, R("L0u")), R("uf1"), A.add)
    wq(2)()
    scatter(R("w2"), slot2, R("val2"))
    tt(R("SBm"), R("L0e"), R("c1o"), A.add)
    co(R("pw", 0, 288), 0.0)
    co(R("PZ"), 0.0)
    co(R("g3", 0, 3), 0.0)
    co(R("F32"), 0.0)
    near, far0, far1 = sorted(range(N - 1), key=lambda k: topo.chip(cores[oth[k]]) != topo.chip(core))
    tc = [R("tc", 32 * i, 32 * i + 32) for i in range(7)]

    def s0():
        tt(R("f2", 0, 192), R("w2", 0, 192), R("mask"), A.mult)

    def e0():
        tt(R("Zf", 0, 12), R("n2k"), R("SBm"), A.add)

    def s1():
        scan(R("f2", 192, 384), R("seg"), R("f2", 0, 192))
        wq(3)()

    def e1():
        tt(R("Zf", 12, 24), R("Zf", 0, 12), landed("mz", near), A.min)

    def s2():
        for q in (1, 3, 0, 2):
            (ac if q % 2 else cp)(R("hg", 0, 12, Qd[q]), ends("f2", Qd[q ^ 1], a=192))

    def e2():
        tt(R("Zf", 24, 36), landed("mz", far0), landed("mz", far1), A.min)

    def s3():
        tt(R("hg", 12, 24), ends("f2", a=192), R("hg", 0, 12), A.add)

    def e3():
        tt(R("Zi", 0, 12), R("Zf", 24, 36), R("Zf", 12, 24), A.min)

    def s4():
        ac(R("hg", 24, 36, upper), R("hg", 12, 24, lower))
        cp(R("hg", 24, 36, lower), R("hg", 12, 24, upper))

    def e4():
        ts(R("Zi", 12, 24), R("Zi", 0, 12), 20, None, A.arith_shift_right)
        ts(R("Zi", 24, 36), R("Zi", 0, 12), 11, 511, A.arith_shift_right, A.bitwise_and)
        ts(R("Zi", 36, 48), R("Zi", 0, 12), 2047, None, A.bitwise_and)

    def s5():
        tt(R("fa", 0, 12), R("hg", 12, 24), R("hg", 24, 36), A.add)

    def e5():
        ts(R("PZ", 0, 12), R("Zi", 12, 24), float(rank), None, A.is_equal)
        ac(R("pr"), R("PZ", 0, 12), scale=-1024.0)
        ts(R("ze", 0, 12), R("Zi", 24, 36), ev, None, A.mult)

    def s6():
        ts(R("l34", 0, 12), R("fa", 0, 12), 1.0 / 2048, None, A.mult)
        ts(R("fa", 24, 36), R("fa", 0, 12), 2047, None, A.bitwise_and)

    def e6():
        turn(tc[0], R("PZ"))
        tt(R("ze", 12, 24), R("ze", 0, 12), R("K2"), A.add)

    def s7():
        cp(R("l34", 12, 24), R("fa", 24, 36))

    def e7():
        scan(tc[1], R("seg", 0, 32), tc[0])
        cp(R("zl", 12, 24), R("ze", 12, 24))

    def s8():
        pickq(R("Q3"), R("QX"), R("l34", 0, 12))
        picks(R("S3"), R("SX"), R("l34", 0, 12))
        send("qb", block("Q3"), True)

    def e8():
        for a, b, n, c, v in ((32, 0, 32, 1, 0), (64, 32, 32, 2, 0), (64, 0, 64, 0, 1), (96, 64, 32, 1, 1), (96, 0, 32, 2, 1)):
            (cp if v else ac)(R("g3", c, c + 1, slice(a, a + n)), R("tc", 47, 48, slice(b, b + n)))
        tt(R("pz", 0, 12), R("park"), R("pr"), A.add)

    def e9():
        scan(R("g3", 3, 6), R("sg", 132, 135), R("g3", 0, 3))
        ac(R("uf2"), ind(idn, R("zl", 12, 24)), scale=2048.0, bias=col(15))

    def s9():
        pickq(R("Q4"), R("W1", 0, X1), R("l34", 12, 24))
        picks(R("S4"), R("P1", 0, X1), R("l34", 12, 24))
        send("sb", block("S3"))
        send("qc", block("Q4"), True)
        send("sc", block("S4"))

    for fn in (s0, e0, s1, s2, e1, s3, e2, s4, e3, s5, e4, s6, e5, s7, e6, s8, e7, e8, e9, s9):
        fn()
    cp(R("zl", 0, 12), R("Zi", 36, 48))
    ts(tc[2], R("maskc"), R("tc", 47, 48), R("g3", 5, 6), A.mult, A.add)
    turn(tc[3], tc[2])
    wq(4)()
    scan(tc[4], R("sg", 36, 68), tc[3])
    wq(5)()
    ts(tc[5], tc[1], R("tc", 159, 160), -1.0, A.add, A.add)
    turn(tc[6], tc[5])
    tt(R("val3"), ind(idn, R("zl", 0, 12)), R("uf2"), A.add)
    tt(R("pz", 12, 24), R("tc", 192, 204), R("pz", 0, 12), A.max)
    slot3 = R("sl", 24, 36)
    cp(slot3, R("pz", 12, 24))
    scatter(R("pw"), slot3, R("val3"))
    turn(R("f3"), R("pw", 0, 288))
    for q in (1, 3, 0, 2):
        (ac if q % 2 else cp)(R("hm", P=Qd[q]), R("f3", 0, 288, Qd[q ^ 1], 16))
    for k in range(2):
        tt(R("F32", 16 * k, 16 * k + 9), R("f3", 16 * k, 288, every, 32), R("hm", k, 18, every, 2), A.add)
    turn(R("TF"), R("F32"))
    ac(R("hx", P=upper), R("TF", P=lower))
    cp(R("hx", P=lower), R("TF", P=upper))
    for i in range(4):
        h = i // 2
        tt(R("DD", 16 * i, 16 * i + 16), R("TF", h, 32, every, 2), R("hx", h, 32, every, 2), A.add)
    turn(R("LT"), R("DD"))
    tt(R("SS"), R("TF"), R("hx"), A.add)
    ts(R("HU"), R("LT"), 1.0 / 2048, None, A.mult)
    ts(R("li"), R("LT"), 2047, None, A.bitwise_and)
    ts(R("idi", 0, 32), R("SS"), 19, None, A.arith_shift_right)
    ts(R("idi", 32, 64), R("SS"), 11, 255, A.arith_shift_right, A.bitwise_and)
    ts(R("idi", 64, 96), R("SS"), 1.0, -1.0, A.is_ge, A.add)

    def products(i, q, s, h):
        for o in range(O):
            c, d = 128 * ((2 - i) * O + o), 512 * (2 * o + h)
            a, b = L * h, L * h + L
            E("t", [R(q, a, b), R(s, a, b), R("WQ", c, c + 128), R("WS", c, c + 128)], [R("ps", d, d + L)] if i == 2 else [],
              lambda e: e.matmul_mx(ap(R("ps", d, d + L)), ap(R("WQ", c, c + 128)), ap(R("WS", c, c + 128)), ap(R(q, a, b)), ap(R(s, a, b)), i == 0, i == 2))

    for i, (q, s, w, p, l, a) in enumerate((("G2", "H2", R("QX"), R("SX"), "HU", 0), ("G1", "H1", R("W1"), R("P1"), "LU", 16), ("G0", "H0", R("W2"), R("P2"), "LU", 0))):
        for h in range(2):
            lst = R(l, 32 * h + a, 32 * h + a + 9)
            pickq(R(q, L * h, L * h + L), w, lst)
            picks(R(s, L * h, L * h + L), p, lst)
            products(i, q, s, h)
            if i == 0 and h == 0:
                cp(R("LU"), R("li"))
    tt(R("idt", 0, 32), R("idi", 0, 32), R("idi", 64, 96), A.add)
    tt(R("idt", 32, 64), R("idi", 32, 64), R("idi", 64, 96), A.add)
    for h in range(2):
        cp(R("ysb", h, M, every, 2), R("ps", 512 * h, 512 * h + L))
        ac(R("ysb", M + h, 2 * M, every, 2), R("ps", 1024 + 512 * h, 1024 + 512 * h + L))
    for o in range(2):
        D("y", None, R("idt", 32 * o, 32 * o + 32, slice(16, 25)), "di%d" % o, outap=T.id[o:o + 1, :])
    D("y", None, R("ysb", 0, M), "dy0", outap=T.y[:, 0:M])
    D("s", None, R("ysb", M, 2 * M), "dy1", outap=T.y[:, M:2 * M])

    wait("g", [(q, cnt[q]) for q in ("v", "s", "t", "g")] + [("loc", loc[0])] + [(s, dsum[s]) for s in DMAS] + arrivals)
